import numpy as np
import ml_dtypes


def mxq(x, axis, fmt="e4m3"):
    dtype, down = {"e4m3": (ml_dtypes.float8_e4m3fn, 7), "e5m2": (ml_dtypes.float8_e5m2, 14)}[fmt]
    v = np.moveaxis(np.asarray(x, np.float32).astype(ml_dtypes.bfloat16).astype(np.float64), axis, -1)
    blocks = v.reshape(v.shape[:-1] + (-1, 32))
    amax = np.abs(blocks).max(-1, keepdims=True)
    byte = np.maximum(np.where(amax > 0, np.frexp(amax)[1] - 1 + 127, 0) - down, 1)
    scale = np.exp2(byte - 127.0)
    codes = (blocks / scale).astype(np.float32).astype(dtype).astype(np.float64)
    return np.moveaxis((codes * scale).reshape(v.shape), -1, axis)


WIDE = False


def mx_kscale(k):
    if not WIDE:
        return np.ones(k)
    levels = np.array([10, -10, 5, -5, 0])
    if k % 512:
        return np.exp2(np.random.permutation(np.resize(levels, k // 32))).repeat(32)
    a = np.empty((k // 512, 16))
    for p in range(k // 512):
        a[p, :8] = np.random.permutation(np.resize(levels, 8))
        for g in range(8):
            far = levels[np.abs(levels - a[p, g]) >= 10]
            a[p, g + 8] = far[np.random.randint(len(far))]
    return np.exp2(a.ravel()).repeat(32)


BF16 = ml_dtypes.bfloat16


def bf(x):
    return np.asarray(x, np.float32).astype(BF16)


def f64(x):
    return np.asarray(x).astype(np.float64)


E2M1 = np.array([0.0, 0.5, 1.0, 1.5, 2.0, 3.0, 4.0, 6.0, -0.0, -0.5, -1.0, -1.5, -2.0, -3.0, -4.0, -6.0])


def pack_weight(w, fmt):
    k, n = w.shape
    w = f64(bf(w)).reshape(k // 32, 32, n)
    amax = np.abs(w).max(1)
    if fmt == "e4m3":
        byte = np.frexp(amax)[1] - 1 + 127 - 7
    else:
        mant, ex = np.frexp(amax / 6.0)
        byte = np.where(mant > 0.5, ex, ex - 1) + 127
    byte = np.clip(np.where(amax > 0, byte, 1), 1, 254)
    scaled = (w * np.exp2(127.0 - byte)[:, None, :]).reshape(k, n).astype(np.float32)
    by_word = np.ascontiguousarray(scaled.reshape(k // 512, 128, 4, n).transpose(0, 1, 3, 2))
    if fmt == "e4m3":
        words = by_word.astype(ml_dtypes.float8_e4m3fn).view(np.uint8)
    else:
        c = by_word.astype(ml_dtypes.float4_e2m1fn).view(np.uint8) & 0xF
        words = c[..., 0::2] | (c[..., 1::2] << 4)
    return np.ascontiguousarray(words), np.ascontiguousarray(byte.astype(np.uint8).reshape(k // 512, 16, n))


def unpack_weight(words, scales, fmt):
    g, p, n, _ = words.shape
    if fmt == "e4m3":
        vals = np.ascontiguousarray(words).view(ml_dtypes.float8_e4m3fn).astype(np.float64)
    else:
        nib = np.empty((g, p, n, 4), np.uint8)
        nib[..., 0::2] = words & 0xF
        nib[..., 1::2] = words >> 4
        vals = E2M1[nib]
    vals = vals * np.repeat(np.exp2(scales.astype(np.float64) - 127.0), 8, axis=1)[..., None]
    return vals.transpose(0, 1, 3, 2).reshape(g * 512, n)
def pack4(w):
    words, scales = pack_weight(w, "e2m1")
    return words.reshape(words.shape[0], 128, -1), scales


def unpack4(words, scales):
    return unpack_weight(words.reshape(words.shape[0], 128, -1, 2), scales, "e2m1")


M, K, F, N, R = 1024, 1024, 2048, 1024, 128


def draw0():
    s, t, u = mx_kscale(K), mx_kscale(F), mx_kscale(M)
    x = np.random.standard_normal((M, K)) * s * u[:, None]
    w_up = np.random.standard_normal((K, F)) / np.sqrt(K) / s[:, None] * t
    gate = 1.4 * np.random.standard_normal((M, F))
    w_down = np.random.standard_normal((F, N)) / np.sqrt(F) / t[:, None]
    lora_a = np.random.standard_normal((F, R)) / np.sqrt(F) / t[:, None]
    dz = np.random.standard_normal((M, R)) / np.sqrt(M) / u[:, None]
    down_words, down_scales = pack4(w_down)
    return {"x": bf(x), "w_up": bf(w_up), "gate": bf(gate),
            "down_words": down_words, "down_scales": down_scales,
            "lora_a": bf(lora_a), "dz": bf(dz)}


def core(x, w_up, gate, down_words, down_scales, lora_a, dz):
    up = mxq(f64(x), 1, "e4m3") @ mxq(f64(w_up), 0, "e4m3")
    h = np.maximum(f64(gate), 0.0) * up
    h_f = mxq(h, 1, "e4m3")
    h_m = mxq(h, 0, "e4m3")
    y = h_f @ unpack4(down_words, down_scales)
    z = h_f @ mxq(f64(lora_a), 0, "e4m3")
    da = h_m.T @ mxq(f64(dz), 0, "e4m3")
    return y, z, da


def e4m3fn_bytes(y):
    return np.clip(np.asarray(y, np.float64), -448.0, 448.0).astype(np.float32).astype(ml_dtypes.float8_e4m3fn).view(np.uint8)


def e4m3fn_values(b):
    return np.asarray(b, np.uint8).view(ml_dtypes.float8_e4m3fn).astype(np.float64)


def setup_inputs():
    d = draw0()
    x0 = np.asarray(d['lora_a']).astype(np.float64)
    s = (np.max(np.abs(x0), axis=(1,), keepdims=True) / 448.0).astype(np.float32)
    out = {}
    for k, v in d.items():
        if k == 'lora_a':
            out['lora_a_bytes'] = e4m3fn_bytes(x0 / s.astype(np.float64))
            out['lora_a_scale'] = s
        else:
            out[k] = v
    return out


def reference(x, w_up, gate, down_words, down_scales, lora_a_bytes, lora_a_scale, dz):
    return core(x, w_up, gate, down_words, down_scales, e4m3fn_values(lora_a_bytes) * lora_a_scale.astype(np.float64), dz)

@@ -1,0 +1,589 @@
+from contextlib import ExitStack
+
+import concourse.mybir as mybir
+from concourse.masks import make_identity
+
+M, K, F, N, R = 1024, 1024, 2048, 1024, 128
+FLOPS = 2 * M * K * F + 2 * M * F * N + 4 * M * F * R
+
+F32 = mybir.dt.float32
+BF16 = mybir.dt.bfloat16
+I32 = mybir.dt.int32
+U32 = mybir.dt.uint32
+U8 = mybir.dt.uint8
+FP8 = mybir.dt.float8_e4m3fn
+FP8X4 = mybir.dt.float8_e4m3fn_x4
+FP4X4 = mybir.dt.float4_e2m1fn_x4
+ALU = mybir.AluOpType
+COPY = mybir.ActivationFunctionType.Copy
+
+P = 128
+GM = 512
+GF = 512
+BLOCKS = [(0, 0), (0, 1), (1, 0), (1, 1), (2, 0), (3, 0), (2, 1), (3, 1)]
+
+
+def tile_qlora_down_projection_s8_kernel(
+    tc, x, w_up, gate, down_words, down_scales, lora_a_bytes, lora_a_scale, dz, y, z, da
+):
+    nc = tc.nc
+    with ExitStack() as ctx:
+        keep = ctx.enter_context(tc.tile_pool(name="keep", bufs=1))
+        work = ctx.enter_context(tc.tile_pool(name="work", bufs=2))
+        psum = ctx.enter_context(tc.psum_pool(name="psum", bufs=2))
+
+        def kept(name, shape, dtype):
+            return keep.tile(shape, dtype, name=name, align_bytes=64)
+
+        ident = kept("ident", [P, P], F32)
+        make_identity(nc, ident[:])
+        dsc = kept("dsc", [P, 4, N], U8)
+        nc.gpsimd.memset(dsc[:].rearrange("p g n -> p (g n)").bitcast(I32), 0)
+
+        x_raw = [kept("x_raw%d" % g, [P, 4, K], BF16) for g in range(2)]
+        w_raw = {(G, c): kept("w_raw%d%d" % (G, c), [P, 4, GF], BF16) for G in range(4) for c in range(2)}
+        gate_sb = {b: kept("gate%d%d" % b, [P, 4, GF], BF16) for b in BLOCKS}
+        words = kept("words", [P, 4, 2 * N], U8)
+        lbytes = kept("lbytes", [P, 4, 4 * R], U8)
+        lscale = kept("lscale", [P, 16], F32)
+        dz_raw = kept("dz_raw", [P, 2, 4 * R], BF16)
+
+        xv = x.rearrange("(g p s) k -> g p s k", p=P, s=4)
+        wv = w_up.rearrange("(c p j) f -> c p j f", p=P, j=4)
+        gv = gate.rearrange("(g p s) f -> g p s f", p=P, s=4)
+
+        def load_x(g, s):
+            nc.sync.dma_start(out=x_raw[g][:, s, :], in_=xv[g, :, s, :])
+
+        def load_w(G, c):
+            nc.sync.dma_start(out=w_raw[G, c][:], in_=wv[c, :, :, G * GF : (G + 1) * GF])
+
+        def load_gate(b):
+            G, g = b
+            nc.sync.dma_start(out=gate_sb[b][:], in_=gv[g, :, :, G * GF : (G + 1) * GF])
+
+        def load_dz():
+            nc.sync.dma_start(out=dz_raw[:], in_=dz.rearrange("(g p t) r -> p g (t r)", p=P, t=4))
+
+        def load_down():
+            for Q in range(4):
+                nc.sync.dma_start(
+                    out=dsc[32 * Q : 32 * Q + 4, :, :].bitcast(I32),
+                    in_=down_scales[:, 4 * Q : 4 * Q + 4, :].bitcast(I32).rearrange("g q w -> q g w"),
+                )
+            nc.sync.dma_start(out=words[:], in_=down_words.rearrange("g p w -> p g w"))
+
+        def load_lora():
+            nc.sync.dma_start(out=lbytes[:], in_=lora_a_bytes.rearrange("(g p t) r -> p g (t r)", p=P, t=4))
+            nc.sync.dma_start(
+                out=lscale[:].rearrange("p (g t) -> p g t", t=4),
+                in_=lora_a_scale.rearrange("(g p t) o -> p g (t o)", p=P, t=4),
+            )
+
+        x_codes = {(g, s): kept("xc%d%d" % (g, s), [P, 2 * P], U32) for g in range(2) for s in range(4)}
+        x_scales = {(g, s): kept("xs%d%d" % (g, s), [P, 2 * P], U8) for g in range(2) for s in range(4)}
+        w_codes = {(G, c): kept("wc%d%d" % (G, c), [P, GF], U32) for G in range(4) for c in range(2)}
+        w_scales = {(G, c): kept("ws%d%d" % (G, c), [P, GF], U8) for G in range(4) for c in range(2)}
+        hm_codes = {b: kept("hmc%d%d" % b, [P, GF], U32) for b in BLOCKS}
+        hm_scales = {b: kept("hms%d%d" % b, [P, GF], U8) for b in BLOCKS}
+        hf_codes = {b: kept("hfc%d%d" % b, [P, GM], U32) for b in BLOCKS}
+        hf_scales = {b: kept("hfs%d%d" % b, [P, GM], U8) for b in BLOCKS}
+        dz_codes = kept("dzc", [P, 2 * R], U32)
+        dz_scales = kept("dzs", [P, 2 * R], U8)
+        la_codes = kept("lac", [P, 4 * R], U32)
+        la_scales = kept("las", [P, 4 * R], U8)
+
+        def copy_on(engine, out, in_):
+            if engine == "V":
+                nc.vector.tensor_copy(out=out, in_=in_)
+            else:
+                nc.scalar.copy(out=out, in_=in_)
+
+        xg = {}
+
+        x_bank = {}
+        h_bank = {}
+        out_bank = {}
+
+        def x_turn(g, s):
+            bank = psum.tile([P, 4, P], F32, name="tr", bufs=2)
+            xw = x_raw[g][:, s, :].bitcast(F32)
+            for c in range(2):
+                for u in range(2):
+                    nc.tensor.transpose(bank[:, 2 * c + u, :], xw[:, 256 * c + u : 256 * (c + 1) : 2], ident[:])
+            x_bank[g, s] = bank
+
+        def x_copy(g, s, engine):
+            bank = x_bank[g, s]
+            t = work.tile([P, 2 * P * 4], BF16, name="xg", bufs=2, align_bytes=64)
+            copy_on(
+                engine,
+                t[:].bitcast(F32).rearrange("p (c q u) -> p c q u", c=2, u=2),
+                bank[:].rearrange("p (c u) q -> p c q u", c=2),
+            )
+            xg[g, s] = t
+
+        def x_quant(g, s):
+            nc.vector.quantize_mx(out=x_codes[g, s][:].bitcast(FP8X4), scales=x_scales[g, s][:], in_=xg[g, s][:])
+
+        wg = {}
+
+        def w_mix(G, c, half, engine):
+            if half == 0:
+                wt = work.tile([P, GF * 4], BF16, name="wg", bufs=4, align_bytes=64)
+                wg[G, c] = wt
+            t = wg[G, c][:, 1024 * half : 1024 * (half + 1)]
+            src = w_raw[G, c][:, :, 256 * half : 256 * (half + 1)]
+            copy_on(
+                engine,
+                t.rearrange("p (f i j) -> p f j i", i=4, j=4),
+                src.rearrange("p j (f i) -> p f j i", i=4),
+            )
+
+        def w_quant(G, c, f0, f1):
+            nc.vector.quantize_mx(
+                out=w_codes[G, c][:, f0:f1].bitcast(FP8X4),
+                scales=w_scales[G, c][:, f0:f1],
+                in_=wg[G, c][:, 4 * f0 : 4 * f1],
+            )
+
+        up_bank = {}
+
+        def up(b, s):
+            G, g = b
+            bank = psum.tile([P, GF], F32, name="up", bufs=3)
+            for c in range(2):
+                ks = slice(P * c, P * (c + 1))
+                nc.tensor.matmul_mx(
+                    out=bank[:],
+                    lhsT=x_codes[g, s][:, ks].bitcast(FP8X4),
+                    lhsT_scale=x_scales[g, s][:, ks],
+                    rhs=w_codes[G, c][:].bitcast(FP8X4),
+                    rhs_scale=w_scales[G, c][:],
+                    start=(c == 0),
+                    stop=(c == 1),
+                )
+            up_bank[b, s] = bank
+
+        def h_mul(b, s):
+            nc.vector.scalar_tensor_tensor(
+                out=gate_sb[b][:, s, :],
+                in0=gate_sb[b][:, s, :],
+                scalar=0.0,
+                in1=up_bank[b, s][:],
+                op0=ALU.max,
+                op1=ALU.mult,
+            )
+
+        hm_tile = {}
+
+        def hm_mix(b, half, engine):
+            if half == 0:
+                hmt = work.tile([P, GF * 4], BF16, name="wg", bufs=4, align_bytes=64)
+                hm_tile[b] = hmt
+            copy_on(
+                engine,
+                hm_tile[b][:, 1024 * half : 1024 * (half + 1)].rearrange("p (f i s) -> p f s i", i=4, s=4),
+                gate_sb[b][:, :, 256 * half : 256 * (half + 1)].rearrange("p s (f i) -> p f s i", i=4),
+            )
+
+        def hm_quant(b):
+            nc.vector.quantize_mx(out=hm_codes[b][:].bitcast(FP8X4), scales=hm_scales[b][:], in_=hm_tile[b][:])
+
+        hf_tile = {}
+
+        def h_turn(b, half):
+            bank = psum.tile([P, 4, P], F32, name="tr", bufs=2)
+            for k in range(2):
+                hw = gate_sb[b][:, 2 * half + k, :].bitcast(F32)
+                for u in range(2):
+                    nc.tensor.transpose(bank[:, 2 * k + u, :], hw[:, u : GF // 2 : 2], ident[:])
+            h_bank[b, half] = bank
+
+        def h_copy(b, half, engine):
+            hft = work.tile([P, GM * 2], BF16, name="hf", bufs=4, align_bytes=64)
+            hf_tile[b, half] = hft
+            copy_on(
+                engine,
+                hft[:].bitcast(F32).rearrange("p (s q u) -> p s q u", s=2, u=2),
+                h_bank[b, half][:].rearrange("p (s u) q -> p s q u", u=2),
+            )
+
+        def hf_quant(b, half):
+            cols = slice(256 * half, 256 * (half + 1))
+            nc.vector.quantize_mx(
+                out=hf_codes[b][:, cols].bitcast(FP8X4), scales=hf_scales[b][:, cols], in_=hf_tile[b, half][:]
+            )
+
+        dzg = {}
+
+        def dz_mix(g, engine):
+            if g == 0:
+                dzt = work.tile([P, 2 * R * 4], BF16, name="xg", bufs=2, align_bytes=64)
+                dzg[0] = dzt
+            copy_on(
+                engine,
+                dzg[0][:, 512 * g : 512 * (g + 1)].rearrange("p (r t) -> p r t", t=4),
+                dz_raw[:, g, :].rearrange("p (t r) -> p r t", t=4),
+            )
+
+        def dz_quant():
+            nc.vector.quantize_mx(out=dz_codes[:].bitcast(FP8X4), scales=dz_scales[:], in_=dzg[0][:])
+
+        lora = {}
+
+        def la_widen(G):
+            if G == 0:
+                lt = work.tile([P, 4, 4, R], BF16, name="wg", bufs=4, align_bytes=64)
+                lora[0] = lt
+            for j in range(4):
+                nc.scalar.activation(
+                    out=lora[0][:, G, j, :],
+                    in_=lbytes[:, G, R * j : R * (j + 1)].bitcast(FP8),
+                    func=COPY,
+                    scale=lscale[:, 4 * G + j : 4 * G + j + 1],
+                )
+
+        def la_mix(half, engine):
+            if half == 0:
+                lm = work.tile([P, 4 * R * 4], BF16, name="wg", bufs=4, align_bytes=64)
+                lora[1] = lm
+            copy_on(
+                engine,
+                lora[1][:, 1024 * half : 1024 * (half + 1)].rearrange("p (g r j) -> p g r j", g=2, j=4),
+                lora[0][:, 2 * half : 2 * half + 2].rearrange("p g j r -> p g r j"),
+            )
+
+        def la_quant():
+            nc.vector.quantize_mx(out=la_codes[:].bitcast(FP8X4), scales=la_scales[:], in_=lora[1][:])
+
+        yv = y.rearrange("(g q s) n -> g s q n", q=P, s=4)
+        zv = z.rearrange("(g q s) r -> g q s r", q=P, s=4)
+        dav = da.rearrange("(g t q) r -> g q t r", q=P, t=4)
+
+        def y_mul(g, s, half):
+            bank = psum.tile([P, 512], F32, name="acc", bufs=3)
+            ns = slice(512 * half, 512 * (half + 1))
+            for G in range(4):
+                nc.tensor.matmul_mx(
+                    out=bank[:],
+                    lhsT=hf_codes[G, g][:, P * s : P * (s + 1)].bitcast(FP8X4),
+                    lhsT_scale=hf_scales[G, g][:, P * s : P * (s + 1)],
+                    rhs=words[:, G, 1024 * half : 1024 * (half + 1)].bitcast(FP4X4),
+                    rhs_scale=dsc[:, G, ns],
+                    start=(G == 0),
+                    stop=(G == 3),
+                )
+            out_bank["y", g, s, half] = bank
+
+        def y_copy(g, s, half, engine):
+            t = work.tile([P, 512], F32, name="yo", bufs=5)
+            copy_on(engine, t[:], out_bank["y", g, s, half][:])
+            nc.sync.dma_start(out=yv[g, s, :, 512 * half : 512 * (half + 1)], in_=t[:])
+
+        def z_mul(g):
+            bank = psum.tile([P, 4, R], F32, name="acc", bufs=3)
+            for s in range(4):
+                for G in range(4):
+                    nc.tensor.matmul_mx(
+                        out=bank[:, s, :],
+                        lhsT=hf_codes[G, g][:, P * s : P * (s + 1)].bitcast(FP8X4),
+                        lhsT_scale=hf_scales[G, g][:, P * s : P * (s + 1)],
+                        rhs=la_codes[:, R * G : R * (G + 1)].bitcast(FP8X4),
+                        rhs_scale=la_scales[:, R * G : R * (G + 1)],
+                        start=(G == 0),
+                        stop=(G == 3),
+                    )
+            out_bank["z", g] = bank
+
+        def z_copy(g, engine):
+            t = work.tile([P, 4, R], F32, name="yo", bufs=5)
+            copy_on(engine, t[:], out_bank["z", g][:])
+            nc.sync.dma_start(out=zv[g], in_=t[:])
+
+        def da_mul(G):
+            bank = psum.tile([P, 4, R], F32, name="acc", bufs=3)
+            for t in range(4):
+                for g in range(2):
+                    nc.tensor.matmul_mx(
+                        out=bank[:, t, :],
+                        lhsT=hm_codes[G, g][:, P * t : P * (t + 1)].bitcast(FP8X4),
+                        lhsT_scale=hm_scales[G, g][:, P * t : P * (t + 1)],
+                        rhs=dz_codes[:, R * g : R * (g + 1)].bitcast(FP8X4),
+                        rhs_scale=dz_scales[:, R * g : R * (g + 1)],
+                        start=(g == 0),
+                        stop=(g == 1),
+                    )
+            out_bank["da", G] = bank
+
+        def da_copy(G, engine):
+            t = work.tile([P, 4, R], F32, name="yo", bufs=5)
+            copy_on(engine, t[:], out_bank["da", G][:])
+            nc.sync.dma_start(out=dav[G], in_=t[:])
+
+        ctx.enter_context(tc.manual_schedule())
+        load_x(1,3)
+        x_turn(1,3)
+        load_w(0,0)
+        x_copy(1,3,"S")
+        w_mix(0,0,0,"V")
+        load_w(0,1)
+        load_x(0,0)
+        w_mix(0,1,0,"V")
+        x_turn(0,0)
+        load_x(0,1)
+        w_mix(0,0,1,"S")
+        load_x(1,1)
+        w_mix(0,1,1,"V")
+        x_quant(1,3)
+        x_turn(0,1)
+        load_x(1,2)
+        load_x(1,0)
+        x_copy(0,0,"S")
+        load_w(1,1)
+        load_gate(BLOCKS[0])
+        x_turn(1,1)
+        x_quant(0,0)
+        w_quant(0,0,0,512)
+        x_copy(0,1,"S")
+        load_w(1,0)
+        x_copy(1,1,"S")
+        x_quant(0,1)
+        w_quant(0,1,0,512)
+        x_turn(1,2)
+        x_quant(1,1)
+        load_gate(BLOCKS[1])
+        w_mix(1,1,0,"V")
+        x_turn(1,0)
+        up(BLOCKS[0],1)
+        x_copy(1,2,"S")
+        up(BLOCKS[0],0)
+        x_quant(1,2)
+        up(BLOCKS[1],1)
+        h_mul(BLOCKS[0],1)
+        x_copy(1,0,"S")
+        w_mix(1,1,1,"S")
+        h_mul(BLOCKS[0],0)
+        x_quant(1,0)
+        up(BLOCKS[1],3)
+        w_quant(1,1,0,512)
+        w_mix(1,0,0,"S")
+        load_x(0,2)
+        h_mul(BLOCKS[1],1)
+        h_turn(BLOCKS[0],0)
+        h_mul(BLOCKS[1],3)
+        w_mix(1,0,1,"S")
+        up(BLOCKS[1],2)
+        h_copy(BLOCKS[0],0,"S")
+        h_mul(BLOCKS[1],2)
+        up(BLOCKS[1],0)
+        x_turn(0,2)
+        load_x(0,3)
+        x_turn(0,3)
+        x_copy(0,2,"S")
+        w_quant(1,0,0,512)
+        load_w(2,1)
+        h_mul(BLOCKS[1],0)
+        x_quant(0,2)
+        up(BLOCKS[3],2)
+        hf_quant(BLOCKS[0],0)
+        up(BLOCKS[3],1)
+        load_gate(BLOCKS[3])
+        load_gate(BLOCKS[2])
+        w_mix(2,1,0,"S")
+        h_mul(BLOCKS[3],2)
+        up(BLOCKS[3],0)
+        h_mul(BLOCKS[3],1)
+        h_mul(BLOCKS[3],0)
+        up(BLOCKS[2],1)
+        h_mul(BLOCKS[2],1)
+        up(BLOCKS[2],0)
+        w_mix(2,1,1,"S")
+        up(BLOCKS[2],2)
+        load_w(3,0)
+        x_copy(0,3,"S")
+        h_turn(BLOCKS[1],0)
+        w_mix(3,0,0,"S")
+        load_w(2,0)
+        h_mul(BLOCKS[2],0)
+        up(BLOCKS[3],3)
+        h_copy(BLOCKS[1],0,"S")
+        w_mix(2,0,0,"S")
+        load_gate(BLOCKS[4])
+        up(BLOCKS[0],2)
+        x_quant(0,3)
+        h_turn(BLOCKS[1],1)
+        w_quant(2,1,0,512)
+        h_copy(BLOCKS[1],1,"S")
+        w_mix(2,0,1,"V")
+        h_turn(BLOCKS[3],0)
+        h_mul(BLOCKS[2],2)
+        up(BLOCKS[0],3)
+        h_mul(BLOCKS[3],3)
+        w_quant(2,0,0,512)
+        h_mul(BLOCKS[0],2)
+        up(BLOCKS[4],3)
+        h_copy(BLOCKS[3],0,"S")
+        load_w(3,1)
+        w_mix(3,1,0,"S")
+        h_mul(BLOCKS[0],3)
+        up(BLOCKS[4],0)
+        hf_quant(BLOCKS[1],0)
+        h_mul(BLOCKS[4],0)
+        up(BLOCKS[2],3)
+        load_gate(BLOCKS[7])
+        w_mix(3,0,1,"S")
+        h_mul(BLOCKS[4],3)
+        hf_quant(BLOCKS[3],0)
+        h_turn(BLOCKS[0],1)
+        h_mul(BLOCKS[2],3)
+        h_turn(BLOCKS[2],0)
+        up(BLOCKS[4],1)
+        h_copy(BLOCKS[0],1,"S")
+        up(BLOCKS[6],1)
+        w_mix(3,1,1,"S")
+        load_gate(BLOCKS[5])
+        load_gate(BLOCKS[6])
+        w_quant(3,0,0,512)
+        up(BLOCKS[4],2)
+        h_copy(BLOCKS[2],0,"S")
+        h_mul(BLOCKS[4],1)
+        hf_quant(BLOCKS[1],1)
+        w_quant(3,1,0,512)
+        h_turn(BLOCKS[2],1)
+        h_mul(BLOCKS[6],1)
+        load_down()
+        h_turn(BLOCKS[4],0)
+        up(BLOCKS[5],1)
+        hm_mix(BLOCKS[1],0,"S")
+        h_mul(BLOCKS[4],2)
+        up(BLOCKS[7],1)
+        up(BLOCKS[5],0)
+        h_mul(BLOCKS[5],1)
+        up(BLOCKS[5],3)
+        h_mul(BLOCKS[7],1)
+        hm_mix(BLOCKS[3],0,"S")
+        h_copy(BLOCKS[2],1,"S")
+        h_mul(BLOCKS[5],0)
+        up(BLOCKS[5],2)
+        hf_quant(BLOCKS[0],1)
+        h_mul(BLOCKS[5],3)
+        hf_quant(BLOCKS[2],0)
+        up(BLOCKS[7],0)
+        h_mul(BLOCKS[5],2)
+        h_turn(BLOCKS[4],1)
+        h_copy(BLOCKS[4],0,"S")
+        h_mul(BLOCKS[7],0)
+        hm_mix(BLOCKS[3],1,"S")
+        load_lora()
+        h_copy(BLOCKS[4],1,"S")
+        h_turn(BLOCKS[5],0)
+        hf_quant(BLOCKS[4],0)
+        h_copy(BLOCKS[5],0,"V")
+        up(BLOCKS[7],3)
+        h_mul(BLOCKS[7],3)
+        hf_quant(BLOCKS[5],0)
+        la_widen(0)
+        up(BLOCKS[7],2)
+        up(BLOCKS[6],3)
+        h_mul(BLOCKS[7],2)
+        h_turn(BLOCKS[7],0)
+        hf_quant(BLOCKS[2],1)
+        h_mul(BLOCKS[6],3)
+        h_turn(BLOCKS[5],1)
+        hm_mix(BLOCKS[1],1,"S")
+        up(BLOCKS[6],0)
+        h_copy(BLOCKS[7],0,"V")
+        up(BLOCKS[6],2)
+        y_mul(0,0,1)
+        h_copy(BLOCKS[5],1,"S")
+        y_mul(0,1,1)
+        la_widen(3)
+        load_dz()
+        h_turn(BLOCKS[7],1)
+        h_mul(BLOCKS[6],2)
+        hf_quant(BLOCKS[4],1)
+        h_mul(BLOCKS[6],0)
+        h_turn(BLOCKS[6],0)
+        y_copy(0,0,1,"S")
+        hm_quant(BLOCKS[1])
+        hf_quant(BLOCKS[5],1)
+        y_copy(0,1,1,"V")
+        la_widen(2)
+        dz_mix(0,"V")
+        hf_quant(BLOCKS[7],0)
+        la_widen(1)
+        y_mul(0,2,0)
+        h_copy(BLOCKS[6],0,"S")
+        la_mix(0,"S")
+        hm_mix(BLOCKS[0],0,"S")
+        y_mul(0,0,0)
+        h_copy(BLOCKS[7],1,"V")
+        h_turn(BLOCKS[6],1)
+        la_mix(1,"V")
+        h_turn(BLOCKS[3],1)
+        y_copy(0,2,0,"V")
+        hm_quant(BLOCKS[3])
+        y_mul(0,3,0)
+        hf_quant(BLOCKS[6],0)
+        y_copy(0,0,0,"V")
+        y_mul(1,0,1)
+        h_copy(BLOCKS[3],1,"S")
+        y_copy(0,3,0,"S")
+        hm_mix(BLOCKS[2],0,"V")
+        hf_quant(BLOCKS[7],1)
+        h_copy(BLOCKS[6],1,"S")
+        hf_quant(BLOCKS[3],1)
+        y_copy(1,0,1,"V")
+        hm_mix(BLOCKS[2],1,"S")
+        y_mul(0,3,1)
+        y_mul(1,1,1)
+        y_copy(1,1,1,"S")
+        y_mul(1,1,0)
+        y_copy(0,3,1,"V")
+        hf_quant(BLOCKS[6],1)
+        hm_quant(BLOCKS[2])
+        y_mul(0,1,0)
+        hm_mix(BLOCKS[0],1,"S")
+        dz_mix(1,"V")
+        y_copy(1,1,0,"V")
+        y_copy(0,1,0,"S")
+        y_mul(1,3,0)
+        hm_mix(BLOCKS[7],0,"V")
+        hm_quant(BLOCKS[0])
+        dz_quant()
+        y_mul(1,2,0)
+        la_quant()
+        hm_mix(BLOCKS[6],0,"V")
+        hm_mix(BLOCKS[4],0,"V")
+        y_copy(1,3,0,"S")
+        hm_mix(BLOCKS[5],0,"V")
+        z_mul(0)
+        y_copy(1,2,0,"S")
+        da_mul(1)
+        y_mul(1,2,1)
+        hm_mix(BLOCKS[7],1,"S")
+        z_copy(0,"V")
+        hm_mix(BLOCKS[5],1,"V")
+        z_mul(1)
+        da_copy(1,"S")
+        hm_mix(BLOCKS[4],1,"S")
+        hm_quant(BLOCKS[7])
+        y_copy(1,2,1,"S")
+        z_copy(1,"S")
+        y_mul(1,3,1)
+        hm_mix(BLOCKS[6],1,"V")
+        hm_quant(BLOCKS[4])
+        y_copy(1,3,1,"V")
+        y_mul(1,0,0)
+        hm_quant(BLOCKS[5])
+        hm_quant(BLOCKS[6])
+        da_mul(0)
+        y_copy(1,0,0,"S")
+        da_mul(3)
+        da_mul(2)
+        da_copy(0,"S")
+        da_copy(3,"V")
+        da_copy(2,"V")
+        y_mul(0,2,1)
+        y_copy(0,2,1,"S")

@@ -18,9 +18,13 @@ ALU = mybir.AluOpType
 COPY = mybir.ActivationFunctionType.Copy
 
 P = 128
-GM = 512
-GF = 512
-BLOCKS = [(0, 0), (0, 1), (1, 0), (1, 1), (2, 0), (3, 0), (2, 1), (3, 1)]
+PASS = 512
+BLOCKS = [(G, g) for G in range(4) for g in range(2)]
+RINGS = {"mm": 6, "tr": 2, "xt": 3, "mix": 5, "hf0": 2, "hf1": 4, "out": 5}
+DA = (5, 10, 12, 14)
+HEAD_V = 84
+STEP_V = 32
+HM_S = (2, 4, 6)
 
 
 def tile_qlora_down_projection_s8_kernel(
@@ -35,40 +39,65 @@ def tile_qlora_down_projection_s8_kernel(
         def kept(name, shape, dtype):
             return keep.tile(shape, dtype, name=name, align_bytes=64)
 
+        def operand(name, columns):
+            return kept(name + "c", [P, columns], U32), kept(name + "s", [P, columns], U8)
+
+        def quantize(op, cols, src):
+            nc.vector.quantize_mx(out=op[0][:, cols].bitcast(FP8X4), scales=op[1][:, cols], in_=src)
+
+        def multiply(out, lhs, lhs_cols, rhs, rhs_cols, first, last):
+            nc.tensor.matmul_mx(
+                out=out,
+                lhsT=lhs[0][:, lhs_cols].bitcast(FP8X4),
+                lhsT_scale=lhs[1][:, lhs_cols],
+                rhs=rhs[0][:, rhs_cols].bitcast(FP8X4),
+                rhs_scale=rhs[1][:, rhs_cols],
+                start=first,
+                stop=last,
+            )
+
+        def copy_on(engine, out, in_):
+            if engine == "V":
+                nc.vector.tensor_copy(out=out, in_=in_)
+            else:
+                nc.scalar.copy(out=out, in_=in_)
+
+        def part(width, index):
+            return slice(width * index, width * (index + 1))
+
         ident = kept("ident", [P, P], F32)
         make_identity(nc, ident[:])
-        dsc = kept("dsc", [P, 4, N], U8)
-        nc.gpsimd.memset(dsc[:].rearrange("p g n -> p (g n)").bitcast(I32), 0)
+        down_sc = kept("down_sc", [P, 4, N], U8)
+        nc.gpsimd.memset(down_sc[:].rearrange("p g n -> p (g n)").bitcast(I32), 0)
 
-        x_raw = [kept("x_raw%d" % g, [P, 4, K], BF16) for g in range(2)]
-        w_raw = {(G, c): kept("w_raw%d%d" % (G, c), [P, 4, GF], BF16) for G in range(4) for c in range(2)}
-        gate_sb = {b: kept("gate%d%d" % b, [P, 4, GF], BF16) for b in BLOCKS}
+        x_raw = {(g, s): kept("x_raw%d%d" % (g, s), [P, K], BF16) for g in range(2) for s in range(4)}
+        w_raw = {(G, c): kept("w_raw%d%d" % (G, c), [P, 4, PASS], BF16) for G in range(4) for c in range(2)}
+        gate_sb = {b: kept("gate%d%d" % b, [P, 4, PASS], BF16) for b in BLOCKS}
         words = kept("words", [P, 4, 2 * N], U8)
         lbytes = kept("lbytes", [P, 4, 4 * R], U8)
         lscale = kept("lscale", [P, 16], F32)
-        dz_raw = kept("dz_raw", [P, 2, 4 * R], BF16)
+        dz_raw = kept("dz_raw", [P, 2, 4, R], BF16)
 
         xv = x.rearrange("(g p s) k -> g p s k", p=P, s=4)
         wv = w_up.rearrange("(c p j) f -> c p j f", p=P, j=4)
         gv = gate.rearrange("(g p s) f -> g p s f", p=P, s=4)
 
         def load_x(g, s):
-            nc.sync.dma_start(out=x_raw[g][:, s, :], in_=xv[g, :, s, :])
+            nc.sync.dma_start(out=x_raw[g, s][:], in_=xv[g, :, s, :])
 
         def load_w(G, c):
-            nc.sync.dma_start(out=w_raw[G, c][:], in_=wv[c, :, :, G * GF : (G + 1) * GF])
+            nc.sync.dma_start(out=w_raw[G, c][:], in_=wv[c, :, :, part(PASS, G)])
 
         def load_gate(b):
-            G, g = b
-            nc.sync.dma_start(out=gate_sb[b][:], in_=gv[g, :, :, G * GF : (G + 1) * GF])
+            nc.sync.dma_start(out=gate_sb[b][:], in_=gv[b[1], :, :, part(PASS, b[0])])
 
         def load_dz():
-            nc.sync.dma_start(out=dz_raw[:], in_=dz.rearrange("(g p t) r -> p g (t r)", p=P, t=4))
+            nc.sync.dma_start(out=dz_raw[:], in_=dz.rearrange("(g p t) r -> p g t r", p=P, t=4))
 
         def load_down():
             for Q in range(4):
                 nc.sync.dma_start(
-                    out=dsc[32 * Q : 32 * Q + 4, :, :].bitcast(I32),
+                    out=down_sc[32 * Q : 32 * Q + 4, :, :].bitcast(I32),
                     in_=down_scales[:, 4 * Q : 4 * Q + 4, :].bitcast(I32).rearrange("g q w -> q g w"),
                 )
             nc.sync.dma_start(out=words[:], in_=down_words.rearrange("g p w -> p g w"))
@@ -80,510 +109,284 @@ def tile_qlora_down_projection_s8_kernel(
                 in_=lora_a_scale.rearrange("(g p t) o -> p g (t o)", p=P, t=4),
             )
 
-        x_codes = {(g, s): kept("xc%d%d" % (g, s), [P, 2 * P], U32) for g in range(2) for s in range(4)}
-        x_scales = {(g, s): kept("xs%d%d" % (g, s), [P, 2 * P], U8) for g in range(2) for s in range(4)}
-        w_codes = {(G, c): kept("wc%d%d" % (G, c), [P, GF], U32) for G in range(4) for c in range(2)}
-        w_scales = {(G, c): kept("ws%d%d" % (G, c), [P, GF], U8) for G in range(4) for c in range(2)}
-        hm_codes = {b: kept("hmc%d%d" % b, [P, GF], U32) for b in BLOCKS}
-        hm_scales = {b: kept("hms%d%d" % b, [P, GF], U8) for b in BLOCKS}
-        hf_codes = {b: kept("hfc%d%d" % b, [P, GM], U32) for b in BLOCKS}
-        hf_scales = {b: kept("hfs%d%d" % b, [P, GM], U8) for b in BLOCKS}
-        dz_codes = kept("dzc", [P, 2 * R], U32)
-        dz_scales = kept("dzs", [P, 2 * R], U8)
-        la_codes = kept("lac", [P, 4 * R], U32)
-        la_scales = kept("las", [P, 4 * R], U8)
+        x_q = {(g, s): operand("x%d%d" % (g, s), 2 * P) for g in range(2) for s in range(4)}
+        w_q = {(G, c): operand("w%d%d" % (G, c), PASS) for G in range(4) for c in range(2)}
+        hf_q = {b: operand("hf%d%d" % b, PASS) for b in BLOCKS}
+        hm_q = {b: operand("hm%d%d" % b, PASS) for b in BLOCKS}
+        dz_q = operand("dz", 2 * R)
+        la_q = operand("la", 4 * R)
+        banks = {}
+        staged = {}
 
-        def copy_on(engine, out, in_):
-            if engine == "V":
-                nc.vector.tensor_copy(out=out, in_=in_)
-            else:
-                nc.scalar.copy(out=out, in_=in_)
+        def bank(key, ring, shape):
+            banks[key] = psum.tile(shape, F32, name=ring, bufs=RINGS[ring])
+            return banks[key]
 
-        xg = {}
+        def stage(key, ring, shape, dtype):
+            staged[key] = work.tile(shape, dtype, name=ring, bufs=RINGS[ring], align_bytes=64)
+            return staged[key]
 
-        x_bank = {}
-        h_bank = {}
-        out_bank = {}
-
-        def x_turn(g, s):
-            bank = psum.tile([P, 4, P], F32, name="tr", bufs=2)
-            xw = x_raw[g][:, s, :].bitcast(F32)
+        def x_turn(g, s, ring):
+            out = bank(("x", g, s), ring, [P, 2, 2, P])
+            xw = x_raw[g, s][:].bitcast(F32)
             for c in range(2):
                 for u in range(2):
-                    nc.tensor.transpose(bank[:, 2 * c + u, :], xw[:, 256 * c + u : 256 * (c + 1) : 2], ident[:])
-            x_bank[g, s] = bank
+                    nc.tensor.transpose(out[:, c, u, :], xw[:, 256 * c + u : 256 * (c + 1) : 2], ident[:])
 
         def x_copy(g, s, engine):
-            bank = x_bank[g, s]
-            t = work.tile([P, 2 * P * 4], BF16, name="xg", bufs=2, align_bytes=64)
+            t = stage(("x", g, s), "xt", [P, K], BF16)
             copy_on(
                 engine,
                 t[:].bitcast(F32).rearrange("p (c q u) -> p c q u", c=2, u=2),
-                bank[:].rearrange("p (c u) q -> p c q u", c=2),
+                banks["x", g, s][:].rearrange("p c u q -> p c q u"),
             )
-            xg[g, s] = t
 
         def x_quant(g, s):
-            nc.vector.quantize_mx(out=x_codes[g, s][:].bitcast(FP8X4), scales=x_scales[g, s][:], in_=xg[g, s][:])
+            quantize(x_q[g, s], slice(0, 2 * P), staged["x", g, s][:])
 
-        wg = {}
-
-        def w_mix(G, c, half, engine):
-            if half == 0:
-                wt = work.tile([P, GF * 4], BF16, name="wg", bufs=4, align_bytes=64)
-                wg[G, c] = wt
-            t = wg[G, c][:, 1024 * half : 1024 * (half + 1)]
-            src = w_raw[G, c][:, :, 256 * half : 256 * (half + 1)]
+        def w_mix(G, c, first, last, engine):
+            if first == 0:
+                stage(("w", G, c), "mix", [P, 4 * PASS], BF16)
+            ns = slice(first, last)
             copy_on(
                 engine,
-                t.rearrange("p (f i j) -> p f j i", i=4, j=4),
-                src.rearrange("p j (f i) -> p f j i", i=4),
+                staged["w", G, c][:].rearrange("p (u n e j) -> p n j u e", u=2, e=2, j=4)[:, ns],
+                w_raw[G, c][:].rearrange("p j (n u e) -> p n j u e", u=2, e=2)[:, ns],
             )
 
-        def w_quant(G, c, f0, f1):
-            nc.vector.quantize_mx(
-                out=w_codes[G, c][:, f0:f1].bitcast(FP8X4),
-                scales=w_scales[G, c][:, f0:f1],
-                in_=wg[G, c][:, 4 * f0 : 4 * f1],
-            )
+        def w_quant(G, c):
+            quantize(w_q[G, c], slice(0, PASS), staged["w", G, c][:])
 
-        up_bank = {}
+        h_sb = {b: w_raw[b][:].rearrange("p (u j) f -> p u (j f)", u=2) for b in BLOCKS}
 
-        def up(b, s):
+        def up(b, pair, u):
             G, g = b
-            bank = psum.tile([P, GF], F32, name="up", bufs=3)
-            for c in range(2):
-                ks = slice(P * c, P * (c + 1))
-                nc.tensor.matmul_mx(
-                    out=bank[:],
-                    lhsT=x_codes[g, s][:, ks].bitcast(FP8X4),
-                    lhsT_scale=x_scales[g, s][:, ks],
-                    rhs=w_codes[G, c][:].bitcast(FP8X4),
-                    rhs_scale=w_scales[G, c][:],
-                    start=(c == 0),
-                    stop=(c == 1),
-                )
-            up_bank[b, s] = bank
+            out = bank(("up", b, pair, u), "mm", [P, 2, 256])
+            for i in range(2):
+                for c in range(2):
+                    multiply(out[:, i, :], x_q[g, 2 * pair + i], part(P, c), w_q[G, c], part(256, u), c == 0, c == 1)
 
-        def h_mul(b, s):
+        def h_mul(b, pair, u):
             nc.vector.scalar_tensor_tensor(
-                out=gate_sb[b][:, s, :],
-                in0=gate_sb[b][:, s, :],
+                out=h_sb[b][:, u, part(PASS, pair)].rearrange("p (m e) -> p m e", e=2),
+                in0=gate_sb[b][:].rearrange("p s (n u e) -> p u (s n) e", u=2, e=2)[:, u, part(256, pair), :],
                 scalar=0.0,
-                in1=up_bank[b, s][:],
+                in1=banks["up", b, pair, u][:].rearrange("p i (n e) -> p (i n) e", e=2),
                 op0=ALU.max,
                 op1=ALU.mult,
             )
 
-        hm_tile = {}
+        def h_turn(b, pair):
+            out = bank(("h", b, pair), "tr", [P, 2, 2, P])
+            hw = h_sb[b].bitcast(F32)
+            for i in range(2):
+                for u in range(2):
+                    nc.tensor.transpose(out[:, i, u, :], hw[:, u, part(P, 2 * pair + i)], ident[:])
 
-        def hm_mix(b, half, engine):
-            if half == 0:
-                hmt = work.tile([P, GF * 4], BF16, name="wg", bufs=4, align_bytes=64)
-                hm_tile[b] = hmt
+        def h_copy(b, pair, engine):
+            if pair == 0:
+                stage(("hf", b), "hf%d" % b[1], [P, 4 * PASS], BF16)
             copy_on(
                 engine,
-                hm_tile[b][:, 1024 * half : 1024 * (half + 1)].rearrange("p (f i s) -> p f s i", i=4, s=4),
-                gate_sb[b][:, :, 256 * half : 256 * (half + 1)].rearrange("p s (f i) -> p f s i", i=4),
+                staged["hf", b][:, part(1024, pair)].bitcast(F32).rearrange("p (i q u) -> p i q u", i=2, u=2),
+                banks["h", b, pair][:].rearrange("p i u q -> p i q u"),
+            )
+
+        def hf_quant(b, first=0, last=2):
+            quantize(hf_q[b], slice(256 * first, 256 * last), staged["hf", b][:, 1024 * first : 1024 * last])
+
+        def hm_mix(b, u, engine):
+            if u == 0:
+                stage(("hm", b), "mix", [P, 4 * PASS], BF16)
+            copy_on(
+                engine,
+                staged["hm", b][:, part(1024, u)].rearrange("p (e n i s) -> p n s i e", e=2, i=2, s=4),
+                h_sb[b][:, u, :].rearrange("p (s n i e) -> p n s i e", s=4, i=2, e=2),
             )
 
         def hm_quant(b):
-            nc.vector.quantize_mx(out=hm_codes[b][:].bitcast(FP8X4), scales=hm_scales[b][:], in_=hm_tile[b][:])
+            quantize(hm_q[b], slice(0, PASS), staged["hm", b][:])
 
-        hf_tile = {}
-
-        def h_turn(b, half):
-            bank = psum.tile([P, 4, P], F32, name="tr", bufs=2)
-            for k in range(2):
-                hw = gate_sb[b][:, 2 * half + k, :].bitcast(F32)
-                for u in range(2):
-                    nc.tensor.transpose(bank[:, 2 * k + u, :], hw[:, u : GF // 2 : 2], ident[:])
-            h_bank[b, half] = bank
-
-        def h_copy(b, half, engine):
-            hft = work.tile([P, GM * 2], BF16, name="hf", bufs=4, align_bytes=64)
-            hf_tile[b, half] = hft
-            copy_on(
-                engine,
-                hft[:].bitcast(F32).rearrange("p (s q u) -> p s q u", s=2, u=2),
-                h_bank[b, half][:].rearrange("p (s u) q -> p s q u", u=2),
-            )
-
-        def hf_quant(b, half):
-            cols = slice(256 * half, 256 * (half + 1))
-            nc.vector.quantize_mx(
-                out=hf_codes[b][:, cols].bitcast(FP8X4), scales=hf_scales[b][:, cols], in_=hf_tile[b, half][:]
-            )
-
-        dzg = {}
-
-        def dz_mix(g, engine):
-            if g == 0:
-                dzt = work.tile([P, 2 * R * 4], BF16, name="xg", bufs=2, align_bytes=64)
-                dzg[0] = dzt
-            copy_on(
-                engine,
-                dzg[0][:, 512 * g : 512 * (g + 1)].rearrange("p (r t) -> p r t", t=4),
-                dz_raw[:, g, :].rearrange("p (t r) -> p r t", t=4),
-            )
+        def dz_mix(engine):
+            t = stage("dz", "xt", [P, 2 * R * 4], BF16)
+            for g in range(2):
+                copy_on(
+                    engine,
+                    t[:, part(PASS, g)].rearrange("p (r i t) -> p r t i", i=4, t=4),
+                    dz_raw[:, g].rearrange("p t (r i) -> p r t i", i=4),
+                )
 
         def dz_quant():
-            nc.vector.quantize_mx(out=dz_codes[:].bitcast(FP8X4), scales=dz_scales[:], in_=dzg[0][:])
-
-        lora = {}
+            quantize(dz_q, slice(0, 2 * R), staged["dz"][:])
 
         def la_widen(G):
             if G == 0:
-                lt = work.tile([P, 4, 4, R], BF16, name="wg", bufs=4, align_bytes=64)
-                lora[0] = lt
-            for j in range(4):
+                stage("la_wide", "mix", [P, 4, 4, R], BF16)
+            for t in range(4):
                 nc.scalar.activation(
-                    out=lora[0][:, G, j, :],
-                    in_=lbytes[:, G, R * j : R * (j + 1)].bitcast(FP8),
+                    out=staged["la_wide"][:, G, t, :],
+                    in_=lbytes[:, G, part(R, t)].bitcast(FP8),
                     func=COPY,
-                    scale=lscale[:, 4 * G + j : 4 * G + j + 1],
+                    scale=lscale[:, 4 * G + t : 4 * G + t + 1],
                 )
 
-        def la_mix(half, engine):
-            if half == 0:
-                lm = work.tile([P, 4 * R * 4], BF16, name="wg", bufs=4, align_bytes=64)
-                lora[1] = lm
+        def la_mix(G, engine):
+            if G == 0:
+                stage("la", "mix", [P, 4 * R * 4], BF16)
             copy_on(
                 engine,
-                lora[1][:, 1024 * half : 1024 * (half + 1)].rearrange("p (g r j) -> p g r j", g=2, j=4),
-                lora[0][:, 2 * half : 2 * half + 2].rearrange("p g j r -> p g r j"),
+                staged["la"][:, part(PASS, G)].rearrange("p (r i t) -> p r t i", i=4, t=4),
+                staged["la_wide"][:, G].rearrange("p t (r i) -> p r t i", i=4),
             )
 
         def la_quant():
-            nc.vector.quantize_mx(out=la_codes[:].bitcast(FP8X4), scales=la_scales[:], in_=lora[1][:])
+            quantize(la_q, slice(0, 4 * R), staged["la"][:])
 
         yv = y.rearrange("(g q s) n -> g s q n", q=P, s=4)
-        zv = z.rearrange("(g q s) r -> g q s r", q=P, s=4)
-        dav = da.rearrange("(g t q) r -> g q t r", q=P, t=4)
+        zv = z.rearrange("(g q s) r -> g q (s r)", q=P, s=4)
+        dav = da.rearrange("(g n a) r -> g n (a r)", n=P, a=4)
 
-        def y_mul(g, s, half):
-            bank = psum.tile([P, 512], F32, name="acc", bufs=3)
-            ns = slice(512 * half, 512 * (half + 1))
-            for G in range(4):
+        def y_mul(g, s, half, groups=range(4)):
+            if 0 in groups:
+                bank(("y", g, s, half), "mm", [P, 512])
+            out = banks["y", g, s, half]
+            for G in groups:
                 nc.tensor.matmul_mx(
-                    out=bank[:],
-                    lhsT=hf_codes[G, g][:, P * s : P * (s + 1)].bitcast(FP8X4),
-                    lhsT_scale=hf_scales[G, g][:, P * s : P * (s + 1)],
-                    rhs=words[:, G, 1024 * half : 1024 * (half + 1)].bitcast(FP4X4),
-                    rhs_scale=dsc[:, G, ns],
+                    out=out[:],
+                    lhsT=hf_q[G, g][0][:, part(P, s)].bitcast(FP8X4),
+                    lhsT_scale=hf_q[G, g][1][:, part(P, s)],
+                    rhs=words[:, G, part(1024, half)].bitcast(FP4X4),
+                    rhs_scale=down_sc[:, G, part(512, half)],
                     start=(G == 0),
                     stop=(G == 3),
                 )
-            out_bank["y", g, s, half] = bank
-
-        def y_copy(g, s, half, engine):
-            t = work.tile([P, 512], F32, name="yo", bufs=5)
-            copy_on(engine, t[:], out_bank["y", g, s, half][:])
-            nc.sync.dma_start(out=yv[g, s, :, 512 * half : 512 * (half + 1)], in_=t[:])
 
         def z_mul(g):
-            bank = psum.tile([P, 4, R], F32, name="acc", bufs=3)
+            out = bank(("z", g), "mm", [P, 4 * R])
             for s in range(4):
                 for G in range(4):
-                    nc.tensor.matmul_mx(
-                        out=bank[:, s, :],
-                        lhsT=hf_codes[G, g][:, P * s : P * (s + 1)].bitcast(FP8X4),
-                        lhsT_scale=hf_scales[G, g][:, P * s : P * (s + 1)],
-                        rhs=la_codes[:, R * G : R * (G + 1)].bitcast(FP8X4),
-                        rhs_scale=la_scales[:, R * G : R * (G + 1)],
-                        start=(G == 0),
-                        stop=(G == 3),
-                    )
-            out_bank["z", g] = bank
-
-        def z_copy(g, engine):
-            t = work.tile([P, 4, R], F32, name="yo", bufs=5)
-            copy_on(engine, t[:], out_bank["z", g][:])
-            nc.sync.dma_start(out=zv[g], in_=t[:])
+                    multiply(out[:, part(R, s)], hf_q[G, g], part(P, s), la_q, part(R, G), G == 0, G == 3)
 
         def da_mul(G):
-            bank = psum.tile([P, 4, R], F32, name="acc", bufs=3)
-            for t in range(4):
+            out = bank(("da", G), "mm", [P, 4 * R])
+            for a in range(4):
                 for g in range(2):
-                    nc.tensor.matmul_mx(
-                        out=bank[:, t, :],
-                        lhsT=hm_codes[G, g][:, P * t : P * (t + 1)].bitcast(FP8X4),
-                        lhsT_scale=hm_scales[G, g][:, P * t : P * (t + 1)],
-                        rhs=dz_codes[:, R * g : R * (g + 1)].bitcast(FP8X4),
-                        rhs_scale=dz_scales[:, R * g : R * (g + 1)],
-                        start=(g == 0),
-                        stop=(g == 1),
-                    )
-            out_bank["da", G] = bank
+                    multiply(out[:, part(R, a)], hm_q[G, g], part(P, a), dz_q, part(R, g), g == 0, g == 1)
 
-        def da_copy(G, engine):
-            t = work.tile([P, 4, R], F32, name="yo", bufs=5)
-            copy_on(engine, t[:], out_bank["da", G][:])
-            nc.sync.dma_start(out=dav[G], in_=t[:])
+        def put(key, engine):
+            t = stage(key, "out", [P, 512], F32)
+            copy_on(engine, t[:], banks[key][:])
+            if key[0] == "y":
+                dst = yv[key[1], key[2], :, part(512, key[3])]
+            else:
+                dst = zv[key[1]] if key[0] == "z" else dav[key[1]]
+            nc.sync.dma_start(out=dst, in_=t[:])
 
         ctx.enter_context(tc.manual_schedule())
-        load_x(1,3)
-        x_turn(1,3)
-        load_w(0,0)
-        x_copy(1,3,"S")
-        w_mix(0,0,0,"V")
-        load_w(0,1)
-        load_x(0,0)
-        w_mix(0,1,0,"V")
-        x_turn(0,0)
-        load_x(0,1)
-        w_mix(0,0,1,"S")
-        load_x(1,1)
-        w_mix(0,1,1,"V")
-        x_quant(1,3)
-        x_turn(0,1)
-        load_x(1,2)
-        load_x(1,0)
-        x_copy(0,0,"S")
-        load_w(1,1)
+
+        for s in range(2):
+            load_x(0, s)
+            load_w(0, s)
+        for s in range(2, 4):
+            load_x(0, s)
         load_gate(BLOCKS[0])
-        x_turn(1,1)
-        x_quant(0,0)
-        w_quant(0,0,0,512)
-        x_copy(0,1,"S")
-        load_w(1,0)
-        x_copy(1,1,"S")
-        x_quant(0,1)
-        w_quant(0,1,0,512)
-        x_turn(1,2)
-        x_quant(1,1)
-        load_gate(BLOCKS[1])
-        w_mix(1,1,0,"V")
-        x_turn(1,0)
-        up(BLOCKS[0],1)
-        x_copy(1,2,"S")
-        up(BLOCKS[0],0)
-        x_quant(1,2)
-        up(BLOCKS[1],1)
-        h_mul(BLOCKS[0],1)
-        x_copy(1,0,"S")
-        w_mix(1,1,1,"S")
-        h_mul(BLOCKS[0],0)
-        x_quant(1,0)
-        up(BLOCKS[1],3)
-        w_quant(1,1,0,512)
-        w_mix(1,0,0,"S")
-        load_x(0,2)
-        h_mul(BLOCKS[1],1)
-        h_turn(BLOCKS[0],0)
-        h_mul(BLOCKS[1],3)
-        w_mix(1,0,1,"S")
-        up(BLOCKS[1],2)
-        h_copy(BLOCKS[0],0,"S")
-        h_mul(BLOCKS[1],2)
-        up(BLOCKS[1],0)
-        x_turn(0,2)
-        load_x(0,3)
-        x_turn(0,3)
-        x_copy(0,2,"S")
-        w_quant(1,0,0,512)
-        load_w(2,1)
-        h_mul(BLOCKS[1],0)
-        x_quant(0,2)
-        up(BLOCKS[3],2)
-        hf_quant(BLOCKS[0],0)
-        up(BLOCKS[3],1)
-        load_gate(BLOCKS[3])
-        load_gate(BLOCKS[2])
-        w_mix(2,1,0,"S")
-        h_mul(BLOCKS[3],2)
-        up(BLOCKS[3],0)
-        h_mul(BLOCKS[3],1)
-        h_mul(BLOCKS[3],0)
-        up(BLOCKS[2],1)
-        h_mul(BLOCKS[2],1)
-        up(BLOCKS[2],0)
-        w_mix(2,1,1,"S")
-        up(BLOCKS[2],2)
-        load_w(3,0)
-        x_copy(0,3,"S")
-        h_turn(BLOCKS[1],0)
-        w_mix(3,0,0,"S")
-        load_w(2,0)
-        h_mul(BLOCKS[2],0)
-        up(BLOCKS[3],3)
-        h_copy(BLOCKS[1],0,"S")
-        w_mix(2,0,0,"S")
-        load_gate(BLOCKS[4])
-        up(BLOCKS[0],2)
-        x_quant(0,3)
-        h_turn(BLOCKS[1],1)
-        w_quant(2,1,0,512)
-        h_copy(BLOCKS[1],1,"S")
-        w_mix(2,0,1,"V")
-        h_turn(BLOCKS[3],0)
-        h_mul(BLOCKS[2],2)
-        up(BLOCKS[0],3)
-        h_mul(BLOCKS[3],3)
-        w_quant(2,0,0,512)
-        h_mul(BLOCKS[0],2)
-        up(BLOCKS[4],3)
-        h_copy(BLOCKS[3],0,"S")
-        load_w(3,1)
-        w_mix(3,1,0,"S")
-        h_mul(BLOCKS[0],3)
-        up(BLOCKS[4],0)
-        hf_quant(BLOCKS[1],0)
-        h_mul(BLOCKS[4],0)
-        up(BLOCKS[2],3)
-        load_gate(BLOCKS[7])
-        w_mix(3,0,1,"S")
-        h_mul(BLOCKS[4],3)
-        hf_quant(BLOCKS[3],0)
-        h_turn(BLOCKS[0],1)
-        h_mul(BLOCKS[2],3)
-        h_turn(BLOCKS[2],0)
-        up(BLOCKS[4],1)
-        h_copy(BLOCKS[0],1,"S")
-        up(BLOCKS[6],1)
-        w_mix(3,1,1,"S")
-        load_gate(BLOCKS[5])
-        load_gate(BLOCKS[6])
-        w_quant(3,0,0,512)
-        up(BLOCKS[4],2)
-        h_copy(BLOCKS[2],0,"S")
-        h_mul(BLOCKS[4],1)
-        hf_quant(BLOCKS[1],1)
-        w_quant(3,1,0,512)
-        h_turn(BLOCKS[2],1)
-        h_mul(BLOCKS[6],1)
-        load_down()
-        h_turn(BLOCKS[4],0)
-        up(BLOCKS[5],1)
-        hm_mix(BLOCKS[1],0,"S")
-        h_mul(BLOCKS[4],2)
-        up(BLOCKS[7],1)
-        up(BLOCKS[5],0)
-        h_mul(BLOCKS[5],1)
-        up(BLOCKS[5],3)
-        h_mul(BLOCKS[7],1)
-        hm_mix(BLOCKS[3],0,"S")
-        h_copy(BLOCKS[2],1,"S")
-        h_mul(BLOCKS[5],0)
-        up(BLOCKS[5],2)
-        hf_quant(BLOCKS[0],1)
-        h_mul(BLOCKS[5],3)
-        hf_quant(BLOCKS[2],0)
-        up(BLOCKS[7],0)
-        h_mul(BLOCKS[5],2)
-        h_turn(BLOCKS[4],1)
-        h_copy(BLOCKS[4],0,"S")
-        h_mul(BLOCKS[7],0)
-        hm_mix(BLOCKS[3],1,"S")
-        load_lora()
-        h_copy(BLOCKS[4],1,"S")
-        h_turn(BLOCKS[5],0)
-        hf_quant(BLOCKS[4],0)
-        h_copy(BLOCKS[5],0,"V")
-        up(BLOCKS[7],3)
-        h_mul(BLOCKS[7],3)
-        hf_quant(BLOCKS[5],0)
-        la_widen(0)
-        up(BLOCKS[7],2)
-        up(BLOCKS[6],3)
-        h_mul(BLOCKS[7],2)
-        h_turn(BLOCKS[7],0)
-        hf_quant(BLOCKS[2],1)
-        h_mul(BLOCKS[6],3)
-        h_turn(BLOCKS[5],1)
-        hm_mix(BLOCKS[1],1,"S")
-        up(BLOCKS[6],0)
-        h_copy(BLOCKS[7],0,"V")
-        up(BLOCKS[6],2)
-        y_mul(0,0,1)
-        h_copy(BLOCKS[5],1,"S")
-        y_mul(0,1,1)
-        la_widen(3)
+        for s in range(4):
+            load_x(1, s)
+        load_w(1, 0)
+        for i in range(1, 8):
+            if i < 6:
+                load_w((i + 2) // 2, i % 2)
+            if i == 6:
+                load_lora()
+            if i == 7:
+                load_down()
+            load_gate(BLOCKS[i])
         load_dz()
-        h_turn(BLOCKS[7],1)
-        h_mul(BLOCKS[6],2)
-        hf_quant(BLOCKS[4],1)
-        h_mul(BLOCKS[6],0)
-        h_turn(BLOCKS[6],0)
-        y_copy(0,0,1,"S")
-        hm_quant(BLOCKS[1])
-        hf_quant(BLOCKS[5],1)
-        y_copy(0,1,1,"V")
-        la_widen(2)
-        dz_mix(0,"V")
-        hf_quant(BLOCKS[7],0)
-        la_widen(1)
-        y_mul(0,2,0)
-        h_copy(BLOCKS[6],0,"S")
-        la_mix(0,"S")
-        hm_mix(BLOCKS[0],0,"S")
-        y_mul(0,0,0)
-        h_copy(BLOCKS[7],1,"V")
-        h_turn(BLOCKS[6],1)
-        la_mix(1,"V")
-        h_turn(BLOCKS[3],1)
-        y_copy(0,2,0,"V")
-        hm_quant(BLOCKS[3])
-        y_mul(0,3,0)
-        hf_quant(BLOCKS[6],0)
-        y_copy(0,0,0,"V")
-        y_mul(1,0,1)
-        h_copy(BLOCKS[3],1,"S")
-        y_copy(0,3,0,"S")
-        hm_mix(BLOCKS[2],0,"V")
-        hf_quant(BLOCKS[7],1)
-        h_copy(BLOCKS[6],1,"S")
-        hf_quant(BLOCKS[3],1)
-        y_copy(1,0,1,"V")
-        hm_mix(BLOCKS[2],1,"S")
-        y_mul(0,3,1)
-        y_mul(1,1,1)
-        y_copy(1,1,1,"S")
-        y_mul(1,1,0)
-        y_copy(0,3,1,"V")
-        hf_quant(BLOCKS[6],1)
-        hm_quant(BLOCKS[2])
-        y_mul(0,1,0)
-        hm_mix(BLOCKS[0],1,"S")
-        dz_mix(1,"V")
-        y_copy(1,1,0,"V")
-        y_copy(0,1,0,"S")
-        y_mul(1,3,0)
-        hm_mix(BLOCKS[7],0,"V")
-        hm_quant(BLOCKS[0])
-        dz_quant()
-        y_mul(1,2,0)
-        la_quant()
-        hm_mix(BLOCKS[6],0,"V")
-        hm_mix(BLOCKS[4],0,"V")
-        y_copy(1,3,0,"S")
-        hm_mix(BLOCKS[5],0,"V")
-        z_mul(0)
-        y_copy(1,2,0,"S")
-        da_mul(1)
-        y_mul(1,2,1)
-        hm_mix(BLOCKS[7],1,"S")
-        z_copy(0,"V")
-        hm_mix(BLOCKS[5],1,"V")
-        z_mul(1)
-        da_copy(1,"S")
-        hm_mix(BLOCKS[4],1,"S")
-        hm_quant(BLOCKS[7])
-        y_copy(1,2,1,"S")
-        z_copy(1,"S")
-        y_mul(1,3,1)
-        hm_mix(BLOCKS[6],1,"V")
-        hm_quant(BLOCKS[4])
-        y_copy(1,3,1,"V")
-        y_mul(1,0,0)
-        hm_quant(BLOCKS[5])
-        hm_quant(BLOCKS[6])
-        da_mul(0)
-        y_copy(1,0,0,"S")
-        da_mul(3)
-        da_mul(2)
-        da_copy(0,"S")
-        da_copy(3,"V")
-        da_copy(2,"V")
-        y_mul(0,2,1)
-        y_copy(0,2,1,"S")
+
+        for s in range(2):
+            x_turn(0, s, "mm")
+            x_copy(0, s, "S")
+            w_mix(0, s, 0, HEAD_V, "V")
+            w_mix(0, s, HEAD_V, P, "S")
+            x_quant(0, s)
+            w_quant(0, s)
+        for s in range(2, 4):
+            x_turn(0, s, "tr")
+            x_copy(0, s, "S")
+            x_quant(0, s)
+        for k in range(4):
+            up((0, 0), k // 2, k % 2)
+            h_mul((0, 0), k // 2, k % 2)
+        for s in range(4):
+            x_turn(1, s, "mm" if s < 2 else "tr")
+            x_copy(1, s, "S")
+            if s % 2 == 0:
+                w_mix(1, 0, 32 * s, 32 * s + 64, "V")
+            x_quant(1, s)
+        w_mix(1, 1, 0, STEP_V, "V")
+        w_mix(1, 1, STEP_V, P, "S")
+        w_quant(1, 0)
+
+        for i in range(1, 8):
+            b = BLOCKS[i]
+            G, g = b
+            if i == 5:
+                for Gl in range(3):
+                    la_widen(Gl)
+            if i == 6:
+                la_widen(3)
+            if i >= 6:
+                hm_mix(BLOCKS[0], i - 6, "S")
+            for k in range(4):
+                up(b, k // 2, k % 2)
+                h_mul(b, k // 2, k % 2)
+                if k == 0 and g == 1 and G < 3:
+                    w_quant(G + 1, 1)
+                if k == 1 and i < 5:
+                    w_mix((i + 3) // 2, (i + 1) % 2, 0, STEP_V, "V")
+                    w_mix((i + 3) // 2, (i + 1) % 2, STEP_V, P, "S")
+                if k == 2 and g == 0:
+                    hf_quant((G - 1, 0))
+                if k == 3 and g == 0 and G < 3:
+                    w_quant(G + 1, 0)
+            for pair in range(2):
+                h_turn(BLOCKS[i - 1], pair)
+                h_copy(BLOCKS[i - 1], pair, "S")
+
+        tiles = [("y", g, s, half) for g in range(2) for s in range(4) for half in range(2)]
+        for G in range(2):
+            la_mix(G, "V")
+        hf_quant((3, 0), 0, 1)
+        hf_quant((3, 0), 1, 2)
+        for i in range(2):
+            y_mul(*tiles[i][1:], range(3))
+        for i in range(16):
+            y_mul(*tiles[i][1:], range(3, 4) if i < 2 else range(4))
+            if i == 1:
+                for pair in range(2):
+                    h_turn(BLOCKS[7], pair)
+                    h_copy(BLOCKS[7], pair, "S")
+            put(tiles[i], "V" if i in (13, 15) else "S")
+            if i == 0:
+                for G in range(2, 4):
+                    la_mix(G, "V")
+                dz_mix("V")
+                la_quant()
+                dz_quant()
+                hm_quant(BLOCKS[0])
+                for G in range(3):
+                    hf_quant((G, 1))
+            if i == 2:
+                hf_quant((3, 1))
+            if 1 <= i < 8:
+                hm_mix(BLOCKS[i], 0, "V")
+                hm_mix(BLOCKS[i], 1, "S" if i in HM_S else "V")
+            if 2 <= i < 9:
+                hm_quant(BLOCKS[i - 1])
+            if i in DA:
+                G = DA.index(i)
+                da_mul(G)
+                put(("da", G), "S")
+            if i in (3, 8):
+                z_mul(i // 8)
+                put(("z", i // 8), "S")

@@ -20,11 +20,13 @@ COPY = mybir.ActivationFunctionType.Copy
 P = 128
 PASS = 512
 BLOCKS = [(G, g) for G in range(4) for g in range(2)]
-RINGS = {"mm": 6, "tr": 2, "xt": 3, "mix": 5, "hf0": 2, "hf1": 4, "out": 5}
-DA = (5, 10, 12, 14)
+RINGS = {"mm": 6, "tr": 2, "xt": 2, "mix": 5, "out": 6}
+DA = (7, 9, 11, 13)
 HEAD_V = 84
-STEP_V = 32
+STEP_V = 24
 HM_S = (2, 4, 6)
+FIRST = 4
+Z0 = 5
 
 
 def tile_qlora_down_projection_s8_kernel(
@@ -109,7 +111,7 @@ def tile_qlora_down_projection_s8_kernel(
                 in_=lora_a_scale.rearrange("(g p t) o -> p g (t o)", p=P, t=4),
             )
 
-        x_q = {(g, s): operand("x%d%d" % (g, s), 2 * P) for g in range(2) for s in range(4)}
+        x_q = {(g, pair): operand("x%d%d" % (g, pair), 4 * P) for g in range(2) for pair in range(2)}
         w_q = {(G, c): operand("w%d%d" % (G, c), PASS) for G in range(4) for c in range(2)}
         hf_q = {b: operand("hf%d%d" % b, PASS) for b in BLOCKS}
         hm_q = {b: operand("hm%d%d" % b, PASS) for b in BLOCKS}
@@ -134,15 +136,16 @@ def tile_qlora_down_projection_s8_kernel(
                     nc.tensor.transpose(out[:, c, u, :], xw[:, 256 * c + u : 256 * (c + 1) : 2], ident[:])
 
         def x_copy(g, s, engine):
-            t = stage(("x", g, s), "xt", [P, K], BF16)
+            if s % 2 == 0:
+                stage(("x", g, s // 2), "xt", [P, 2 * K], BF16)
             copy_on(
                 engine,
-                t[:].bitcast(F32).rearrange("p (c q u) -> p c q u", c=2, u=2),
+                staged["x", g, s // 2][:, part(K, s % 2)].bitcast(F32).rearrange("p (c q u) -> p c q u", c=2, u=2),
                 banks["x", g, s][:].rearrange("p c u q -> p c q u"),
             )
 
-        def x_quant(g, s):
-            quantize(x_q[g, s], slice(0, 2 * P), staged["x", g, s][:])
+        def x_quant(g, pair):
+            quantize(x_q[g, pair], slice(0, 4 * P), staged["x", g, pair][:])
 
         def w_mix(G, c, first, last, engine):
             if first == 0:
@@ -158,13 +161,14 @@ def tile_qlora_down_projection_s8_kernel(
             quantize(w_q[G, c], slice(0, PASS), staged["w", G, c][:])
 
         h_sb = {b: w_raw[b][:].rearrange("p (u j) f -> p u (j f)", u=2) for b in BLOCKS}
+        hf_sb = {b: gate_sb[b][:].rearrange("p s f -> p (s f)") for b in BLOCKS}
 
         def up(b, pair, u):
             G, g = b
             out = bank(("up", b, pair, u), "mm", [P, 2, 256])
             for i in range(2):
                 for c in range(2):
-                    multiply(out[:, i, :], x_q[g, 2 * pair + i], part(P, c), w_q[G, c], part(256, u), c == 0, c == 1)
+                    multiply(out[:, i, :], x_q[g, pair], part(P, 2 * i + c), w_q[G, c], part(256, u), c == 0, c == 1)
 
         def h_mul(b, pair, u):
             nc.vector.scalar_tensor_tensor(
@@ -184,16 +188,19 @@ def tile_qlora_down_projection_s8_kernel(
                     nc.tensor.transpose(out[:, i, u, :], hw[:, u, part(P, 2 * pair + i)], ident[:])
 
         def h_copy(b, pair, engine):
-            if pair == 0:
-                stage(("hf", b), "hf%d" % b[1], [P, 4 * PASS], BF16)
             copy_on(
                 engine,
-                staged["hf", b][:, part(1024, pair)].bitcast(F32).rearrange("p (i q u) -> p i q u", i=2, u=2),
+                hf_sb[b][:, part(1024, pair)].bitcast(F32).rearrange("p (i q u) -> p i q u", i=2, u=2),
                 banks["h", b, pair][:].rearrange("p i u q -> p i q u"),
             )
 
+        def turn(b):
+            for pair in range(2):
+                h_turn(b, pair)
+                h_copy(b, pair, "S")
+
         def hf_quant(b, first=0, last=2):
-            quantize(hf_q[b], slice(256 * first, 256 * last), staged["hf", b][:, 1024 * first : 1024 * last])
+            quantize(hf_q[b], slice(256 * first, 256 * last), hf_sb[b][:, 1024 * first : 1024 * last])
 
         def hm_mix(b, u, engine):
             if u == 0:
@@ -209,12 +216,11 @@ def tile_qlora_down_projection_s8_kernel(
 
         def dz_mix(engine):
             t = stage("dz", "xt", [P, 2 * R * 4], BF16)
-            for g in range(2):
-                copy_on(
-                    engine,
-                    t[:, part(PASS, g)].rearrange("p (r i t) -> p r t i", i=4, t=4),
-                    dz_raw[:, g].rearrange("p t (r i) -> p r t i", i=4),
-                )
+            copy_on(
+                engine,
+                t[:].rearrange("p (g r i t) -> p g r t i", g=2, i=4, t=4),
+                dz_raw[:].rearrange("p g t (r i) -> p g r t i", i=4),
+            )
 
         def dz_quant():
             quantize(dz_q, slice(0, 2 * R), staged["dz"][:])
@@ -230,13 +236,12 @@ def tile_qlora_down_projection_s8_kernel(
                     scale=lscale[:, 4 * G + t : 4 * G + t + 1],
                 )
 
-        def la_mix(G, engine):
-            if G == 0:
-                stage("la", "mix", [P, 4 * R * 4], BF16)
+        def la_mix(engine):
+            t = stage("la", "mix", [P, 4 * R * 4], BF16)
             copy_on(
                 engine,
-                staged["la"][:, part(PASS, G)].rearrange("p (r i t) -> p r t i", i=4, t=4),
-                staged["la_wide"][:, G].rearrange("p t (r i) -> p r t i", i=4),
+                t[:].rearrange("p (g r i t) -> p g r t i", g=4, i=4, t=4),
+                staged["la_wide"][:].rearrange("p g t (r i) -> p g r t i", i=4),
             )
 
         def la_quant():
@@ -261,11 +266,11 @@ def tile_qlora_down_projection_s8_kernel(
                     stop=(G == 3),
                 )
 
-        def z_mul(g):
-            out = bank(("z", g), "mm", [P, 4 * R])
-            for s in range(4):
+        def z_mul(g, first, last):
+            out = bank(("z", g, first, last), "mm", [P, (last - first) * R])
+            for s in range(first, last):
                 for G in range(4):
-                    multiply(out[:, part(R, s)], hf_q[G, g], part(P, s), la_q, part(R, G), G == 0, G == 3)
+                    multiply(out[:, part(R, s - first)], hf_q[G, g], part(P, s), la_q, part(R, G), G == 0, G == 3)
 
         def da_mul(G):
             out = bank(("da", G), "mm", [P, 4 * R])
@@ -274,12 +279,14 @@ def tile_qlora_down_projection_s8_kernel(
                     multiply(out[:, part(R, a)], hm_q[G, g], part(P, a), dz_q, part(R, g), g == 0, g == 1)
 
         def put(key, engine):
-            t = stage(key, "out", [P, 512], F32)
+            t = stage(key, "out", list(banks[key].shape), F32)
             copy_on(engine, t[:], banks[key][:])
             if key[0] == "y":
                 dst = yv[key[1], key[2], :, part(512, key[3])]
+            elif key[0] == "z":
+                dst = zv[key[1], :, R * key[2] : R * key[3]]
             else:
-                dst = zv[key[1]] if key[0] == "z" else dav[key[1]]
+                dst = dav[key[1]]
             nc.sync.dma_start(out=dst, in_=t[:])
 
         ctx.enter_context(tc.manual_schedule())
@@ -290,9 +297,9 @@ def tile_qlora_down_projection_s8_kernel(
         for s in range(2, 4):
             load_x(0, s)
         load_gate(BLOCKS[0])
+        load_w(1, 0)
         for s in range(4):
             load_x(1, s)
-        load_w(1, 0)
         for i in range(1, 8):
             if i < 6:
                 load_w((i + 2) // 2, i % 2)
@@ -308,24 +315,27 @@ def tile_qlora_down_projection_s8_kernel(
             x_copy(0, s, "S")
             w_mix(0, s, 0, HEAD_V, "V")
             w_mix(0, s, HEAD_V, P, "S")
-            x_quant(0, s)
+            if s == 1:
+                x_quant(0, 0)
             w_quant(0, s)
         for s in range(2, 4):
             x_turn(0, s, "tr")
             x_copy(0, s, "S")
-            x_quant(0, s)
+        x_quant(0, 1)
+        w_mix(1, 0, 0, P - STEP_V, "S")
         for k in range(4):
             up((0, 0), k // 2, k % 2)
             h_mul((0, 0), k // 2, k % 2)
-        for s in range(4):
-            x_turn(1, s, "mm" if s < 2 else "tr")
-            x_copy(1, s, "S")
-            if s % 2 == 0:
-                w_mix(1, 0, 32 * s, 32 * s + 64, "V")
-            x_quant(1, s)
-        w_mix(1, 1, 0, STEP_V, "V")
-        w_mix(1, 1, STEP_V, P, "S")
+        w_mix(1, 0, P - STEP_V, P, "V")
         w_quant(1, 0)
+        for pair in range(2):
+            for s in range(2 * pair, 2 * pair + 2):
+                x_turn(1, s, "mm" if s < 2 else "tr")
+                x_copy(1, s, "S")
+            x_quant(1, pair)
+            if pair == 0:
+                w_mix(1, 1, 0, 64, "V")
+        w_mix(1, 1, 64, P, "S")
 
         for i in range(1, 8):
             b = BLOCKS[i]
@@ -345,48 +355,50 @@ def tile_qlora_down_projection_s8_kernel(
                 if k == 1 and i < 5:
                     w_mix((i + 3) // 2, (i + 1) % 2, 0, STEP_V, "V")
                     w_mix((i + 3) // 2, (i + 1) % 2, STEP_V, P, "S")
-                if k == 2 and g == 0:
-                    hf_quant((G - 1, 0))
+                if k == 1 and i == 6:
+                    hf_quant((0, 0))
                 if k == 3 and g == 0 and G < 3:
                     w_quant(G + 1, 0)
-            for pair in range(2):
-                h_turn(BLOCKS[i - 1], pair)
-                h_copy(BLOCKS[i - 1], pair, "S")
+            turn(BLOCKS[i - 1])
 
         tiles = [("y", g, s, half) for g in range(2) for s in range(4) for half in range(2)]
-        for G in range(2):
-            la_mix(G, "V")
+        for u in range(2):
+            hm_mix(BLOCKS[1], u, "S")
+        hf_quant((1, 0))
+        hf_quant((2, 0))
         hf_quant((3, 0), 0, 1)
         hf_quant((3, 0), 1, 2)
-        for i in range(2):
-            y_mul(*tiles[i][1:], range(3))
+        for G in range(3):
+            for i in range(FIRST):
+                y_mul(*tiles[i][1:], range(G, G + 1))
         for i in range(16):
-            y_mul(*tiles[i][1:], range(3, 4) if i < 2 else range(4))
-            if i == 1:
-                for pair in range(2):
-                    h_turn(BLOCKS[7], pair)
-                    h_copy(BLOCKS[7], pair, "S")
-            put(tiles[i], "V" if i in (13, 15) else "S")
+            y_mul(*tiles[i][1:], range(3, 4) if i < FIRST else range(4))
+            if i == FIRST - 1:
+                turn(BLOCKS[7])
+            put(tiles[i], "V" if i == 14 else "S")
             if i == 0:
-                for G in range(2, 4):
-                    la_mix(G, "V")
-                dz_mix("V")
-                la_quant()
-                dz_quant()
-                hm_quant(BLOCKS[0])
+                la_mix("V")
                 for G in range(3):
                     hf_quant((G, 1))
-            if i == 2:
+                la_quant()
+                dz_mix("V")
+                hm_quant(BLOCKS[0])
+                dz_quant()
+            j = i - FIRST + 3
+            if 2 <= j < 8:
+                hm_mix(BLOCKS[j], 0, "V")
+                hm_mix(BLOCKS[j], 1, "S" if j in HM_S else "V")
+            if j == 2:
                 hf_quant((3, 1))
-            if 1 <= i < 8:
-                hm_mix(BLOCKS[i], 0, "V")
-                hm_mix(BLOCKS[i], 1, "S" if i in HM_S else "V")
-            if 2 <= i < 9:
-                hm_quant(BLOCKS[i - 1])
+            if 2 <= j < 9:
+                hm_quant(BLOCKS[j - 1])
             if i in DA:
                 G = DA.index(i)
                 da_mul(G)
                 put(("da", G), "S")
-            if i in (3, 8):
-                z_mul(i // 8)
-                put(("z", i // 8), "S")
+            if i == Z0:
+                z_mul(0, 0, 4)
+                put(("z", 0, 0, 4), "S")
+        for pair in range(2):
+            z_mul(1, 2 * pair, 2 * pair + 2)
+            put(("z", 1, 2 * pair, 2 * pair + 2), "V" if pair == 0 else "S")

@@ -20,11 +20,9 @@ COPY = mybir.ActivationFunctionType.Copy
 P = 128
 PASS = 512
 BLOCKS = [(G, g) for G in range(4) for g in range(2)]
-RINGS = {"mm": 6, "tr": 2, "xt": 2, "mix": 5, "out": 6}
+RINGS = {"mm": 6, "tr": 2, "xt": 2, "mix": 7, "pool": 1, "out": 6}
 DA = (7, 9, 11, 13)
-HEAD_V = 84
-STEP_V = 24
-HM_S = (2, 4, 6)
+HEAD_V = 40
 FIRST = 4
 Z0 = 5
 
@@ -147,18 +145,42 @@ def tile_qlora_down_projection_s8_kernel(
         def x_quant(g, pair):
             quantize(x_q[g, pair], slice(0, 4 * P), staged["x", g, pair][:])
 
-        def w_mix(G, c, first, last, engine):
-            if first == 0:
-                stage(("w", G, c), "mix", [P, 4 * PASS], BF16)
-            ns = slice(first, last)
-            copy_on(
-                engine,
-                staged["w", G, c][:].rearrange("p (u n e j) -> p n j u e", u=2, e=2, j=4)[:, ns],
-                w_raw[G, c][:].rearrange("p j (n u e) -> p n j u e", u=2, e=2)[:, ns],
-            )
+        def halves(key, shared):
+            if shared:
+                first = stage((key, 0), "mix", [P, 2 * PASS], BF16)
+                second = stage((key, 1), "pool", [P, 2 * PASS], BF16)
+                staged[key] = [first[:], second[:]]
+            else:
+                whole = stage((key, 2), "mix", [P, 4 * PASS], BF16)
+                staged[key] = [whole[:, part(1024, 0)], whole[:, part(1024, 1)]]
+
+        def quantize_halves(op, key):
+            if (key, 2) in staged:
+                quantize(op, slice(0, PASS), staged[key, 2][:])
+            else:
+                for u in range(2):
+                    quantize(op, part(256, u), staged[key][u])
+
+        def pool_copy(out, in_):
+            nc.gpsimd.tensor_scalar(out=out, in0=in_, scalar1=1.0, scalar2=0.0, op0=ALU.mult, op1=ALU.add)
+
+        def w_mix(G, c, u, first, last, engine):
+            out = staged["w", G, c][u]
+            if engine == "G":
+                pool_copy(
+                    out.rearrange("p (n e j) -> p n j e", e=2, j=4)[:, first:last],
+                    w_raw[G, c][:].rearrange("p j (n u e) -> p u n j e", u=2, e=2)[:, u, first:last],
+                )
+            else:
+                ms = slice(first // 2, last // 2)
+                copy_on(
+                    engine,
+                    out.rearrange("p (m i e j) -> p m j i e", i=2, e=2, j=4)[:, ms],
+                    w_raw[G, c][:].rearrange("p j (m i u e) -> p u m j i e", i=2, u=2, e=2)[:, u, ms],
+                )
 
         def w_quant(G, c):
-            quantize(w_q[G, c], slice(0, PASS), staged["w", G, c][:])
+            quantize_halves(w_q[G, c], ("w", G, c))
 
         h_sb = {b: w_raw[b][:].rearrange("p (u j) f -> p u (j f)", u=2) for b in BLOCKS}
         hf_sb = {b: gate_sb[b][:].rearrange("p s f -> p (s f)") for b in BLOCKS}
@@ -203,16 +225,24 @@ def tile_qlora_down_projection_s8_kernel(
             quantize(hf_q[b], slice(256 * first, 256 * last), hf_sb[b][:, 1024 * first : 1024 * last])
 
         def hm_mix(b, u, engine):
-            if u == 0:
-                stage(("hm", b), "mix", [P, 4 * PASS], BF16)
-            copy_on(
-                engine,
-                staged["hm", b][:, part(1024, u)].rearrange("p (e n i s) -> p n s i e", e=2, i=2, s=4),
-                h_sb[b][:, u, :].rearrange("p (s n i e) -> p n s i e", s=4, i=2, e=2),
-            )
+            out = staged["hm", b][u]
+            if engine == "G":
+                pool_copy(
+                    out.rearrange("p (e n s) -> p e n s", e=2, s=4),
+                    h_sb[b][:, u, :].rearrange("p (s n e) -> p e n s", s=4, e=2),
+                )
+            else:
+                copy_on(
+                    engine,
+                    out.rearrange("p (e n i s) -> p n s i e", e=2, i=2, s=4),
+                    h_sb[b][:, u, :].rearrange("p (s n i e) -> p n s i e", s=4, i=2, e=2),
+                )
 
-        def hm_quant(b):
-            quantize(hm_q[b], slice(0, PASS), staged["hm", b][:])
+        def hm_quant(b, u=None):
+            if u is None:
+                quantize_halves(hm_q[b], ("hm", b))
+            else:
+                quantize(hm_q[b], part(256, u), staged["hm", b][u])
 
         def dz_mix(engine):
             t = stage("dz", "xt", [P, 2 * R * 4], BF16)
@@ -313,8 +343,10 @@ def tile_qlora_down_projection_s8_kernel(
         for s in range(2):
             x_turn(0, s, "mm")
             x_copy(0, s, "S")
-            w_mix(0, s, 0, HEAD_V, "V")
-            w_mix(0, s, HEAD_V, P, "S")
+            halves(("w", 0, s), s == 1)
+            w_mix(0, s, 0, 0, P, "V")
+            w_mix(0, s, 1, 0, HEAD_V, "V")
+            w_mix(0, s, 1, HEAD_V, P, "S")
             if s == 1:
                 x_quant(0, 0)
             w_quant(0, s)
@@ -322,50 +354,54 @@ def tile_qlora_down_projection_s8_kernel(
             x_turn(0, s, "tr")
             x_copy(0, s, "S")
         x_quant(0, 1)
-        w_mix(1, 0, 0, P - STEP_V, "S")
+        halves(("w", 1, 0), True)
+        w_mix(1, 0, 0, 0, P, "S")
+        w_mix(1, 0, 1, 0, P, "G")
         for k in range(4):
             up((0, 0), k // 2, k % 2)
             h_mul((0, 0), k // 2, k % 2)
-        w_mix(1, 0, P - STEP_V, P, "V")
         w_quant(1, 0)
+        halves(("w", 1, 1), True)
         for pair in range(2):
             for s in range(2 * pair, 2 * pair + 2):
-                x_turn(1, s, "mm" if s < 2 else "tr")
+                x_turn(1, s, "mm")
                 x_copy(1, s, "S")
             x_quant(1, pair)
             if pair == 0:
-                w_mix(1, 1, 0, 64, "V")
-        w_mix(1, 1, 64, P, "S")
+                w_mix(1, 1, 1, 0, P, "V")
+        w_mix(1, 1, 0, 0, P, "S")
+        turn(BLOCKS[0])
+        w_quant(1, 1)
 
         for i in range(1, 8):
             b = BLOCKS[i]
-            G, g = b
+            if i < 5:
+                nxt = ((i + 3) // 2, (i + 1) % 2)
+                halves(("w",) + nxt, True)
+                w_mix(*nxt, 0, 0, P, "S")
+                w_mix(*nxt, 1, 0, P, "G")
+            else:
+                halves(("hm", BLOCKS[i - 5]), True)
+                hm_mix(BLOCKS[i - 5], 1, "G")
+            if i >= 5:
+                la_widen(i - 5)
             if i == 5:
-                for Gl in range(3):
-                    la_widen(Gl)
-            if i == 6:
                 la_widen(3)
             if i >= 6:
-                hm_mix(BLOCKS[0], i - 6, "S")
+                hm_mix(BLOCKS[i - 6], 0, "S")
             for k in range(4):
                 up(b, k // 2, k % 2)
                 h_mul(b, k // 2, k % 2)
-                if k == 0 and g == 1 and G < 3:
-                    w_quant(G + 1, 1)
-                if k == 1 and i < 5:
-                    w_mix((i + 3) // 2, (i + 1) % 2, 0, STEP_V, "V")
-                    w_mix((i + 3) // 2, (i + 1) % 2, STEP_V, P, "S")
-                if k == 1 and i == 6:
-                    hf_quant((0, 0))
-                if k == 3 and g == 0 and G < 3:
-                    w_quant(G + 1, 0)
-            turn(BLOCKS[i - 1])
+            if i < 5:
+                w_quant(*nxt)
+            else:
+                hf_quant((i - 5, 0))
+                hm_quant(BLOCKS[i - 5], 1)
+            if i > 1:
+                turn(BLOCKS[i - 1])
 
         tiles = [("y", g, s, half) for g in range(2) for s in range(4) for half in range(2)]
-        for u in range(2):
-            hm_mix(BLOCKS[1], u, "S")
-        hf_quant((1, 0))
-        hf_quant((2, 0))
+        hm_mix(BLOCKS[2], 0, "S")
         hf_quant((3, 0), 0, 1)
         hf_quant((3, 0), 1, 2)
         for G in range(3):
@@ -382,15 +418,17 @@ def tile_qlora_down_projection_s8_kernel(
                     hf_quant((G, 1))
                 la_quant()
                 dz_mix("V")
-                hm_quant(BLOCKS[0])
+                for j in range(3):
+                    hm_quant(BLOCKS[j], 0)
                 dz_quant()
-            j = i - FIRST + 3
-            if 2 <= j < 8:
+            j = i - FIRST + 4
+            if 3 <= j < 8:
+                halves(("hm", BLOCKS[j]), False)
                 hm_mix(BLOCKS[j], 0, "V")
-                hm_mix(BLOCKS[j], 1, "S" if j in HM_S else "V")
-            if j == 2:
+                hm_mix(BLOCKS[j], 1, "S" if j % 2 else "V")
+            if j == 3:
                 hf_quant((3, 1))
-            if 2 <= j < 9:
+            if 4 <= j < 9:
                 hm_quant(BLOCKS[j - 1])
             if i in DA:
                 G = DA.index(i)

@@ -25,6 +25,7 @@ DA = (7, 9, 11, 13)
 HEAD_V = 40
 FIRST = 4
 Z0 = 5
+TR = "tr"
 
 
 def tile_qlora_down_projection_s8_kernel(
@@ -133,9 +134,9 @@ def tile_qlora_down_projection_s8_kernel(
                 for u in range(2):
                     nc.tensor.transpose(out[:, c, u, :], xw[:, 256 * c + u : 256 * (c + 1) : 2], ident[:])
 
-        def x_copy(g, s, engine):
+        def x_copy(g, s, engine, ring="xt"):
             if s % 2 == 0:
-                stage(("x", g, s // 2), "xt", [P, 2 * K], BF16)
+                stage(("x", g, s // 2), ring, [P, 2 * K], BF16)
             copy_on(
                 engine,
                 staged["x", g, s // 2][:, part(K, s % 2)].bitcast(F32).rearrange("p (c q u) -> p c q u", c=2, u=2),
@@ -161,6 +162,10 @@ def tile_qlora_down_projection_s8_kernel(
                 for u in range(2):
                     quantize(op, part(256, u), staged[key][u])
 
+        def halves_over(key, used):
+            first = stage((key, 0), "mix", [P, 2 * PASS], BF16)
+            staged[key] = [first[:], used[:, part(1024, 0)]]
+
         def pool_copy(out, in_):
             nc.gpsimd.tensor_scalar(out=out, in0=in_, scalar1=1.0, scalar2=0.0, op0=ALU.mult, op1=ALU.add)
 
@@ -179,8 +184,11 @@ def tile_qlora_down_projection_s8_kernel(
                     w_raw[G, c][:].rearrange("p j (m i u e) -> p u m j i e", i=2, u=2, e=2)[:, u, ms],
                 )
 
-        def w_quant(G, c):
-            quantize_halves(w_q[G, c], ("w", G, c))
+        def w_quant(G, c, u=None):
+            if u is None:
+                quantize_halves(w_q[G, c], ("w", G, c))
+            else:
+                quantize(w_q[G, c], part(256, u), staged["w", G, c][u])
 
         h_sb = {b: w_raw[b][:].rearrange("p (u j) f -> p u (j f)", u=2) for b in BLOCKS}
         hf_sb = {b: gate_sb[b][:].rearrange("p s f -> p (s f)") for b in BLOCKS}
@@ -203,7 +211,7 @@ def tile_qlora_down_projection_s8_kernel(
             )
 
         def h_turn(b, pair):
-            out = bank(("h", b, pair), "tr", [P, 2, 2, P])
+            out = bank(("h", b, pair), TR, [P, 2, 2, P])
             hw = h_sb[b].bitcast(F32)
             for i in range(2):
                 for u in range(2):
@@ -321,15 +329,14 @@ def tile_qlora_down_projection_s8_kernel(
 
         ctx.enter_context(tc.manual_schedule())
 
-        for s in range(2):
+        for s in range(4):
             load_x(0, s)
-            load_w(0, s)
-        for s in range(2, 4):
-            load_x(0, s)
-        load_gate(BLOCKS[0])
-        load_w(1, 0)
+        for c in range(2):
+            load_w(0, c)
         for s in range(4):
             load_x(1, s)
+        load_gate(BLOCKS[0])
+        load_w(1, 0)
         for i in range(1, 8):
             if i < 6:
                 load_w((i + 2) // 2, i % 2)
@@ -340,68 +347,66 @@ def tile_qlora_down_projection_s8_kernel(
             load_gate(BLOCKS[i])
         load_dz()
 
-        for s in range(2):
-            x_turn(0, s, "mm")
-            x_copy(0, s, "S")
-            halves(("w", 0, s), s == 1)
-            w_mix(0, s, 0, 0, P, "V")
-            w_mix(0, s, 1, 0, HEAD_V, "V")
-            w_mix(0, s, 1, HEAD_V, P, "S")
-            if s == 1:
-                x_quant(0, 0)
-            w_quant(0, s)
-        for s in range(2, 4):
-            x_turn(0, s, "tr")
-            x_copy(0, s, "S")
-        x_quant(0, 1)
+        for pair in range(2):
+            for s in range(2 * pair, 2 * pair + 2):
+                x_turn(0, s, "mm")
+                x_copy(0, s, "V" if s % 2 else "S")
+            x_quant(0, pair)
+        for c in range(2):
+            halves(("w", 0, c), False)
+            w_mix(0, c, 0, 0, P, "V")
+            w_mix(0, c, 1, 0, HEAD_V, "V")
+            w_mix(0, c, 1, HEAD_V, P, "S")
+        for c in range(2):
+            w_quant(0, c)
+
+        for pair in range(2):
+            for s in range(2 * pair, 2 * pair + 2):
+                x_turn(1, s, "mm" if pair == 0 else TR)
+                x_copy(1, s, "S", "xt" if pair == 0 else "pool")
+            x_quant(1, pair)
         halves(("w", 1, 0), True)
         w_mix(1, 0, 0, 0, P, "S")
         w_mix(1, 0, 1, 0, P, "G")
         for k in range(4):
             up((0, 0), k // 2, k % 2)
             h_mul((0, 0), k // 2, k % 2)
-        w_quant(1, 0)
-        halves(("w", 1, 1), True)
-        for pair in range(2):
-            for s in range(2 * pair, 2 * pair + 2):
-                x_turn(1, s, "mm")
-                x_copy(1, s, "S")
-            x_quant(1, pair)
-            if pair == 0:
-                w_mix(1, 1, 1, 0, P, "V")
+        halves(("w", 1, 1), False)
         w_mix(1, 1, 0, 0, P, "S")
-        turn(BLOCKS[0])
+        w_mix(1, 1, 1, 0, P, "V")
+        w_quant(1, 0, 0)
         w_quant(1, 1)
+        w_quant(1, 0, 1)
 
         for i in range(1, 8):
             b = BLOCKS[i]
             if i < 5:
                 nxt = ((i + 3) // 2, (i + 1) % 2)
                 halves(("w",) + nxt, True)
-                w_mix(*nxt, 0, 0, P, "S")
                 w_mix(*nxt, 1, 0, P, "G")
+                if i > 1:
+                    w_mix(*nxt, 0, 0, P, "S")
+            elif i == 5:
+                halves(("hm", BLOCKS[0]), True)
+                hm_mix(BLOCKS[0], 1, "G")
             else:
-                halves(("hm", BLOCKS[i - 5]), True)
+                halves_over(("hm", BLOCKS[i - 5]), hf_sb[i - 6, 0])
                 hm_mix(BLOCKS[i - 5], 1, "G")
-            if i >= 5:
-                la_widen(i - 5)
-            if i == 5:
-                la_widen(3)
-            if i >= 6:
-                hm_mix(BLOCKS[i - 6], 0, "S")
             for k in range(4):
                 up(b, k // 2, k % 2)
                 h_mul(b, k // 2, k % 2)
+            turn(BLOCKS[i - 1])
             if i < 5:
+                if i == 1:
+                    w_mix(*nxt, 0, 0, P, "S")
                 w_quant(*nxt)
             else:
                 hf_quant((i - 5, 0))
-                hm_quant(BLOCKS[i - 5], 1)
-            if i > 1:
-                turn(BLOCKS[i - 1])
-
+            if i >= 4:
+                la_widen(i - 4)
+            if i >= 5:
+                hm_mix(BLOCKS[i - 5], 0, "S")
         tiles = [("y", g, s, half) for g in range(2) for s in range(4) for half in range(2)]
-        hm_mix(BLOCKS[2], 0, "S")
         hf_quant((3, 0), 0, 1)
         hf_quant((3, 0), 1, 2)
         for G in range(3):
@@ -419,7 +424,7 @@ def tile_qlora_down_projection_s8_kernel(
                 la_quant()
                 dz_mix("V")
                 for j in range(3):
-                    hm_quant(BLOCKS[j], 0)
+                    hm_quant(BLOCKS[j])
                 dz_quant()
             j = i - FIRST + 4
             if 3 <= j < 8:

@@ -74,7 +74,7 @@ def tile_qlora_down_projection_s8_kernel(
         x_raw = {(g, s): kept("x_raw%d%d" % (g, s), [P, K], BF16) for g in range(2) for s in range(4)}
         w_raw = {(G, c): kept("w_raw%d%d" % (G, c), [P, 4, PASS], BF16) for G in range(4) for c in range(2)}
         gate_sb = {b: kept("gate%d%d" % b, [P, 4, PASS], BF16) for b in BLOCKS}
-        words = kept("words", [P, 4, 2 * N], U8)
+        words = [kept("words%d" % G, [P, 2 * N], U8) for G in range(4)]
         lbytes = kept("lbytes", [P, 4, 4 * R], U8)
         lscale = kept("lscale", [P, 16], F32)
         dz_raw = kept("dz_raw", [P, 2, 4, R], BF16)
@@ -96,12 +96,13 @@ def tile_qlora_down_projection_s8_kernel(
             nc.sync.dma_start(out=dz_raw[:], in_=dz.rearrange("(g p t) r -> p g t r", p=P, t=4))
 
         def load_down():
-            for Q in range(4):
+            for r in range(4):
                 nc.sync.dma_start(
-                    out=down_sc[32 * Q : 32 * Q + 4, :, :].bitcast(I32),
-                    in_=down_scales[:, 4 * Q : 4 * Q + 4, :].bitcast(I32).rearrange("g q w -> q g w"),
+                    out=down_sc[r:P:32].bitcast(I32),
+                    in_=down_scales[:, r:16:4, :].bitcast(I32).rearrange("g q w -> q g w"),
                 )
-            nc.sync.dma_start(out=words[:], in_=down_words.rearrange("g p w -> p g w"))
+            for G in range(4):
+                nc.sync.dma_start(out=words[G][:], in_=down_words[G])
 
         def load_lora():
             nc.sync.dma_start(out=lbytes[:], in_=lora_a_bytes.rearrange("(g p t) r -> p g (t r)", p=P, t=4))
@@ -298,7 +299,7 @@ def tile_qlora_down_projection_s8_kernel(
                     out=out[:],
                     lhsT=hf_q[G, g][0][:, part(P, s)].bitcast(FP8X4),
                     lhsT_scale=hf_q[G, g][1][:, part(P, s)],
-                    rhs=words[:, G, part(1024, half)].bitcast(FP4X4),
+                    rhs=words[G][:, part(1024, half)].bitcast(FP4X4),
                     rhs_scale=down_sc[:, G, part(512, half)],
                     start=(G == 0),
                     stop=(G == 3),
@@ -342,9 +343,8 @@ def tile_qlora_down_projection_s8_kernel(
                 load_w((i + 2) // 2, i % 2)
             if i == 6:
                 load_lora()
-            if i == 7:
-                load_down()
             load_gate(BLOCKS[i])
+        load_down()
         load_dz()
 
         for pair in range(2):

@@ -21,10 +21,11 @@ P = 128
 PASS = 512
 BLOCKS = [(G, g) for G in range(4) for g in range(2)]
 RINGS = {"mm": 6, "tr": 2, "xt": 2, "mix": 7, "pool": 1, "out": 6}
-DA = (7, 9, 11, 13)
+DA = (9, 11, 13, 14)
+Z0 = 7
 HEAD_V = 40
-FIRST = 4
-Z0 = 5
+S0 = ()
+S1 = (3, 5, 7)
 TR = "tr"
 
 
@@ -165,7 +166,7 @@ def tile_qlora_down_projection_s8_kernel(
 
         def halves_over(key, used):
             first = stage((key, 0), "mix", [P, 2 * PASS], BF16)
-            staged[key] = [first[:], used[:, part(1024, 0)]]
+            staged[key] = [first[:], used[:, part(1024, 1)]]
 
         def pool_copy(out, in_):
             nc.gpsimd.tensor_scalar(out=out, in0=in_, scalar1=1.0, scalar2=0.0, op0=ALU.mult, op1=ALU.add)
@@ -311,21 +312,19 @@ def tile_qlora_down_projection_s8_kernel(
                 for G in range(4):
                     multiply(out[:, part(R, s - first)], hf_q[G, g], part(P, s), la_q, part(R, G), G == 0, G == 3)
 
-        def da_mul(G):
-            out = bank(("da", G), "mm", [P, 4 * R])
-            for a in range(4):
+        def da_mul(G, first, last):
+            out = bank(("da", G, first, last), "mm", [P, (last - first) * R])
+            for a in range(first, last):
                 for g in range(2):
-                    multiply(out[:, part(R, a)], hm_q[G, g], part(P, a), dz_q, part(R, g), g == 0, g == 1)
+                    multiply(out[:, part(R, a - first)], hm_q[G, g], part(P, a), dz_q, part(R, g), g == 0, g == 1)
 
         def put(key, engine):
             t = stage(key, "out", list(banks[key].shape), F32)
             copy_on(engine, t[:], banks[key][:])
             if key[0] == "y":
                 dst = yv[key[1], key[2], :, part(512, key[3])]
-            elif key[0] == "z":
-                dst = zv[key[1], :, R * key[2] : R * key[3]]
             else:
-                dst = dav[key[1]]
+                dst = (zv if key[0] == "z" else dav)[key[1], :, R * key[2] : R * key[3]]
             nc.sync.dma_start(out=dst, in_=t[:])
 
         ctx.enter_context(tc.manual_schedule())
@@ -378,7 +377,7 @@ def tile_qlora_down_projection_s8_kernel(
         w_quant(1, 1)
         w_quant(1, 0, 1)
 
-        for i in range(1, 8):
+        for i in range(1, 7):
             b = BLOCKS[i]
             if i < 5:
                 nxt = ((i + 3) // 2, (i + 1) % 2)
@@ -390,8 +389,8 @@ def tile_qlora_down_projection_s8_kernel(
                 halves(("hm", BLOCKS[0]), True)
                 hm_mix(BLOCKS[0], 1, "G")
             else:
-                halves_over(("hm", BLOCKS[i - 5]), hf_sb[i - 6, 0])
-                hm_mix(BLOCKS[i - 5], 1, "G")
+                halves_over(("hm", BLOCKS[1]), hf_sb[0, 0])
+                hm_mix(BLOCKS[1], 1, "G")
             for k in range(4):
                 up(b, k // 2, k % 2)
                 h_mul(b, k // 2, k % 2)
@@ -406,39 +405,50 @@ def tile_qlora_down_projection_s8_kernel(
                 la_widen(i - 4)
             if i >= 5:
                 hm_mix(BLOCKS[i - 5], 0, "S")
+
+        last = BLOCKS[7]
         tiles = [("y", g, s, half) for g in range(2) for s in range(4) for half in range(2)]
+        for k in range(4):
+            up(last, k // 2, k % 2)
+        hf_quant((2, 0))
+        h_mul(last, 0, 0)
+        turn(BLOCKS[6])
+        la_widen(3)
         hf_quant((3, 0), 0, 1)
         hf_quant((3, 0), 1, 2)
-        for G in range(3):
-            for i in range(FIRST):
-                y_mul(*tiles[i][1:], range(G, G + 1))
+        halves_over(("hm", BLOCKS[2]), hf_sb[3, 0])
+        hm_mix(BLOCKS[2], 1, "G")
+        hm_mix(BLOCKS[2], 0, "S")
+        for k in range(1, 4):
+            h_mul(last, k // 2, k % 2)
+        for i in range(2):
+            y_mul(*tiles[i][1:], range(3))
         for i in range(16):
-            y_mul(*tiles[i][1:], range(3, 4) if i < FIRST else range(4))
-            if i == FIRST - 1:
-                turn(BLOCKS[7])
+            y_mul(*tiles[i][1:], range(3, 4) if i < 2 else range(4))
+            if i == 3:
+                turn(last)
             put(tiles[i], "V" if i == 14 else "S")
             if i == 0:
-                la_mix("V")
                 for G in range(3):
                     hf_quant((G, 1))
-                la_quant()
+                la_mix("V")
                 dz_mix("V")
+                la_quant()
+            if i == 3:
+                hf_quant(last)
                 for j in range(3):
                     hm_quant(BLOCKS[j])
                 dz_quant()
-            j = i - FIRST + 4
+            j = i
             if 3 <= j < 8:
                 halves(("hm", BLOCKS[j]), False)
-                hm_mix(BLOCKS[j], 0, "V")
-                hm_mix(BLOCKS[j], 1, "S" if j % 2 else "V")
-            if j == 3:
-                hf_quant((3, 1))
+                hm_mix(BLOCKS[j], 0, "S" if j in S0 else "V")
+                hm_mix(BLOCKS[j], 1, "S" if j in S1 else "V")
             if 4 <= j < 9:
                 hm_quant(BLOCKS[j - 1])
             if i in DA:
-                G = DA.index(i)
-                da_mul(G)
-                put(("da", G), "S")
+                da_mul(DA.index(i), 0, 4)
+                put(("da", DA.index(i), 0, 4), "S")
             if i == Z0:
                 z_mul(0, 0, 4)
                 put(("z", 0, 0, 4), "S")

@@ -129,6 +129,11 @@ def tile_qlora_down_projection_s8_kernel(
             staged[key] = work.tile(shape, dtype, name=ring, bufs=RINGS[ring], align_bytes=64)
             return staged[key]
 
+        def warm_up(count):
+            out = bank("warm", "tr", [P, PASS])
+            for i in range(count):
+                nc.tensor.matmul(out[:], lhsT=w_raw[0, 0][:, 0, :P], rhs=w_raw[0, 0][:, 0, :], start=True, stop=True)
+
         def x_turn(g, s, ring):
             out = bank(("x", g, s), ring, [P, 2, 2, P])
             xw = x_raw[g, s][:].bitcast(F32)
@@ -358,6 +363,7 @@ def tile_qlora_down_projection_s8_kernel(
             w_mix(0, c, 1, HEAD_V, P, "S")
         for c in range(2):
             w_quant(0, c)
+        warm_up(4)
 
         for pair in range(2):
             for s in range(2 * pair, 2 * pair + 2):

@@ -20,13 +20,13 @@ COPY = mybir.ActivationFunctionType.Copy
 P = 128
 PASS = 512
 BLOCKS = [(G, g) for G in range(4) for g in range(2)]
-RINGS = {"mm": 6, "tr": 2, "xt": 2, "mix": 7, "pool": 1, "out": 6}
-DA = (9, 11, 13, 14)
+RINGS = {"xt": 2, "mix": 7, "pool": 1, "early": 1, "out": 10}
+DA = (11, 13, 15)
 Z0 = 7
 HEAD_V = 40
+UFIRST = ()
 S0 = ()
 S1 = (3, 5, 7)
-TR = "tr"
 
 
 def tile_qlora_down_projection_s8_kernel(
@@ -72,7 +72,9 @@ def tile_qlora_down_projection_s8_kernel(
         down_sc = kept("down_sc", [P, 4, N], U8)
         nc.gpsimd.memset(down_sc[:].rearrange("p g n -> p (g n)").bitcast(I32), 0)
 
-        x_raw = {(g, s): kept("x_raw%d%d" % (g, s), [P, K], BF16) for g in range(2) for s in range(4)}
+        x_parts = [(g, s, s + 1) for g in range(2) for s in range(4)]
+        x_raw = {(g, a): kept("x_raw%d%d" % (g, a), [P, b - a, K], BF16) for g, a, b in x_parts}
+        x_tile = {(g, s): x_raw[g, a][:, s - a, :] for g, a, b in x_parts for s in range(a, b)}
         w_raw = {(G, c): kept("w_raw%d%d" % (G, c), [P, 4, PASS], BF16) for G in range(4) for c in range(2)}
         gate_sb = {b: kept("gate%d%d" % b, [P, 4, PASS], BF16) for b in BLOCKS}
         words = [kept("words%d" % G, [P, 2 * N], U8) for G in range(4)]
@@ -84,8 +86,8 @@ def tile_qlora_down_projection_s8_kernel(
         wv = w_up.rearrange("(c p j) f -> c p j f", p=P, j=4)
         gv = gate.rearrange("(g p s) f -> g p s f", p=P, s=4)
 
-        def load_x(g, s):
-            nc.sync.dma_start(out=x_raw[g, s][:], in_=xv[g, :, s, :])
+        def load_x(g, a, b):
+            nc.sync.dma_start(out=x_raw[g, a][:], in_=xv[g, :, a:b, :])
 
         def load_w(G, c):
             nc.sync.dma_start(out=w_raw[G, c][:], in_=wv[c, :, :, part(PASS, G)])
@@ -121,22 +123,22 @@ def tile_qlora_down_projection_s8_kernel(
         banks = {}
         staged = {}
 
-        def bank(key, ring, shape):
-            banks[key] = psum.tile(shape, F32, name=ring, bufs=RINGS[ring])
+        def bank(key, n, shape):
+            banks[key] = psum.tile(shape, F32, name="bank%d" % n, bufs=1)
             return banks[key]
 
         def stage(key, ring, shape, dtype):
             staged[key] = work.tile(shape, dtype, name=ring, bufs=RINGS[ring], align_bytes=64)
             return staged[key]
 
-        def warm_up(count):
-            out = bank("warm", "tr", [P, PASS])
+        def warm_up(count, n):
+            out = bank("warm", n, [P, PASS])
             for i in range(count):
                 nc.tensor.matmul(out[:], lhsT=w_raw[0, 0][:, 0, :P], rhs=w_raw[0, 0][:, 0, :], start=True, stop=True)
 
-        def x_turn(g, s, ring):
-            out = bank(("x", g, s), ring, [P, 2, 2, P])
-            xw = x_raw[g, s][:].bitcast(F32)
+        def x_turn(g, s, n):
+            out = bank(("x", g, s), n, [P, 2, 2, P])
+            xw = x_tile[g, s].bitcast(F32)
             for c in range(2):
                 for u in range(2):
                     nc.tensor.transpose(out[:, c, u, :], xw[:, 256 * c + u : 256 * (c + 1) : 2], ident[:])
@@ -153,10 +155,10 @@ def tile_qlora_down_projection_s8_kernel(
         def x_quant(g, pair):
             quantize(x_q[g, pair], slice(0, 4 * P), staged["x", g, pair][:])
 
-        def halves(key, shared):
+        def halves(key, shared, ring="pool"):
             if shared:
                 first = stage((key, 0), "mix", [P, 2 * PASS], BF16)
-                second = stage((key, 1), "pool", [P, 2 * PASS], BF16)
+                second = stage((key, 1), ring, [P, 2 * PASS], BF16)
                 staged[key] = [first[:], second[:]]
             else:
                 whole = stage((key, 2), "mix", [P, 4 * PASS], BF16)
@@ -171,7 +173,7 @@ def tile_qlora_down_projection_s8_kernel(
 
         def halves_over(key, used):
             first = stage((key, 0), "mix", [P, 2 * PASS], BF16)
-            staged[key] = [first[:], used[:, part(1024, 1)]]
+            staged[key] = [first[:], used[:, part(1024, 0)]]
 
         def pool_copy(out, in_):
             nc.gpsimd.tensor_scalar(out=out, in0=in_, scalar1=1.0, scalar2=0.0, op0=ALU.mult, op1=ALU.add)
@@ -200,12 +202,22 @@ def tile_qlora_down_projection_s8_kernel(
         h_sb = {b: w_raw[b][:].rearrange("p (u j) f -> p u (j f)", u=2) for b in BLOCKS}
         hf_sb = {b: gate_sb[b][:].rearrange("p s f -> p (s f)") for b in BLOCKS}
 
-        def up(b, pair, u):
+        def up(b, pair, u, n):
             G, g = b
-            out = bank(("up", b, pair, u), "mm", [P, 2, 256])
+            out = bank(("up", b, pair, u), n, [P, 2, 256])
             for i in range(2):
                 for c in range(2):
                     multiply(out[:, i, :], x_q[g, pair], part(P, 2 * i + c), w_q[G, c], part(256, u), c == 0, c == 1)
+
+        def up_pass(b, pair, u, c, n=None):
+            G, g = b
+            if c == 0:
+                bank(("up", b, pair, u), n, [P, 2, 256])
+            out = banks["up", b, pair, u]
+            for i in range(2):
+                multiply(
+                    out[:, i, :], x_q[g, pair], part(P, 2 * i + c), w_q[G, c], part(256, u), c == 0 and i == 0, c == 1 and i == 1
+                )
 
         def h_mul(b, pair, u):
             nc.vector.scalar_tensor_tensor(
@@ -217,8 +229,8 @@ def tile_qlora_down_projection_s8_kernel(
                 op1=ALU.mult,
             )
 
-        def h_turn(b, pair):
-            out = bank(("h", b, pair), TR, [P, 2, 2, P])
+        def h_turn(b, pair, n):
+            out = bank(("h", b, pair), n, [P, 2, 2, P])
             hw = h_sb[b].bitcast(F32)
             for i in range(2):
                 for u in range(2):
@@ -231,9 +243,9 @@ def tile_qlora_down_projection_s8_kernel(
                 banks["h", b, pair][:].rearrange("p i u q -> p i q u"),
             )
 
-        def turn(b):
+        def turn(b, n0, n1):
             for pair in range(2):
-                h_turn(b, pair)
+                h_turn(b, pair, (n0, n1)[pair])
                 h_copy(b, pair, "S")
 
         def hf_quant(b, first=0, last=2):
@@ -296,9 +308,9 @@ def tile_qlora_down_projection_s8_kernel(
         zv = z.rearrange("(g q s) r -> g q (s r)", q=P, s=4)
         dav = da.rearrange("(g n a) r -> g n (a r)", n=P, a=4)
 
-        def y_mul(g, s, half, groups=range(4)):
+        def y_mul(g, s, half, n, groups=range(4)):
             if 0 in groups:
-                bank(("y", g, s, half), "mm", [P, 512])
+                bank(("y", g, s, half), n, [P, 512])
             out = banks["y", g, s, half]
             for G in groups:
                 nc.tensor.matmul_mx(
@@ -311,35 +323,35 @@ def tile_qlora_down_projection_s8_kernel(
                     stop=(G == 3),
                 )
 
-        def z_mul(g, first, last):
-            out = bank(("z", g, first, last), "mm", [P, (last - first) * R])
+        def z_mul(g, first, last, n):
+            out = bank(("z", g, first, last), n, [P, (last - first) * R])
             for s in range(first, last):
                 for G in range(4):
                     multiply(out[:, part(R, s - first)], hf_q[G, g], part(P, s), la_q, part(R, G), G == 0, G == 3)
 
-        def da_mul(G, first, last):
-            out = bank(("da", G, first, last), "mm", [P, (last - first) * R])
+        def da_mul(G, first, last, n):
+            out = bank(("da", G, first, last), n, [P, (last - first) * R])
             for a in range(first, last):
                 for g in range(2):
                     multiply(out[:, part(R, a - first)], hm_q[G, g], part(P, a), dz_q, part(R, g), g == 0, g == 1)
 
-        def put(key, engine):
+        def put(key, engine, queue=nc.sync):
             t = stage(key, "out", list(banks[key].shape), F32)
             copy_on(engine, t[:], banks[key][:])
             if key[0] == "y":
                 dst = yv[key[1], key[2], :, part(512, key[3])]
             else:
                 dst = (zv if key[0] == "z" else dav)[key[1], :, R * key[2] : R * key[3]]
-            nc.sync.dma_start(out=dst, in_=t[:])
+            queue.dma_start(out=dst, in_=t[:])
 
         ctx.enter_context(tc.manual_schedule())
 
-        for s in range(4):
-            load_x(0, s)
+        for piece in x_parts[:4]:
+            load_x(*piece)
         for c in range(2):
             load_w(0, c)
-        for s in range(4):
-            load_x(1, s)
+        for piece in x_parts[4:]:
+            load_x(*piece)
         load_gate(BLOCKS[0])
         load_w(1, 0)
         for i in range(1, 8):
@@ -351,9 +363,16 @@ def tile_qlora_down_projection_s8_kernel(
         load_down()
         load_dz()
 
+        taken = [5]
+
+        def mm():
+            taken[0] = (taken[0] + 1) % 6
+            return taken[0]
+
+        first = BLOCKS[0]
         for pair in range(2):
             for s in range(2 * pair, 2 * pair + 2):
-                x_turn(0, s, "mm")
+                x_turn(0, s, mm())
                 x_copy(0, s, "V" if s % 2 else "S")
             x_quant(0, pair)
         for c in range(2):
@@ -363,19 +382,18 @@ def tile_qlora_down_projection_s8_kernel(
             w_mix(0, c, 1, HEAD_V, P, "S")
         for c in range(2):
             w_quant(0, c)
-        warm_up(4)
-
+        warm_up(4, 6)
         for pair in range(2):
             for s in range(2 * pair, 2 * pair + 2):
-                x_turn(1, s, "mm" if pair == 0 else TR)
+                x_turn(1, s, mm() if pair == 0 else 9 - s)
                 x_copy(1, s, "S", "xt" if pair == 0 else "pool")
             x_quant(1, pair)
         halves(("w", 1, 0), True)
         w_mix(1, 0, 0, 0, P, "S")
         w_mix(1, 0, 1, 0, P, "G")
         for k in range(4):
-            up((0, 0), k // 2, k % 2)
-            h_mul((0, 0), k // 2, k % 2)
+            up(first, k // 2, k % 2, mm())
+            h_mul(first, k // 2, k % 2)
         halves(("w", 1, 1), False)
         w_mix(1, 1, 0, 0, P, "S")
         w_mix(1, 1, 1, 0, P, "V")
@@ -395,18 +413,20 @@ def tile_qlora_down_projection_s8_kernel(
                 halves(("hm", BLOCKS[0]), True)
                 hm_mix(BLOCKS[0], 1, "G")
             else:
-                halves_over(("hm", BLOCKS[1]), hf_sb[0, 0])
+                halves_over(("hm", BLOCKS[1]), hf_sb[1, 0])
                 hm_mix(BLOCKS[1], 1, "G")
             for k in range(4):
-                up(b, k // 2, k % 2)
-                h_mul(b, k // 2, k % 2)
-            turn(BLOCKS[i - 1])
+                pair, u = (k % 2, k // 2) if i in UFIRST else (k // 2, k % 2)
+                up(b, pair, u, mm())
+                h_mul(b, pair, u)
+            turn(BLOCKS[i - 1], 7, 6)
             if i < 5:
                 if i == 1:
                     w_mix(*nxt, 0, 0, P, "S")
                 w_quant(*nxt)
-            else:
-                hf_quant((i - 5, 0))
+            elif i == 5:
+                for G in range(2):
+                    hf_quant((G, 0), 0, 1)
             if i >= 4:
                 la_widen(i - 4)
             if i >= 5:
@@ -415,33 +435,43 @@ def tile_qlora_down_projection_s8_kernel(
         last = BLOCKS[7]
         tiles = [("y", g, s, half) for g in range(2) for s in range(4) for half in range(2)]
         for k in range(4):
-            up(last, k // 2, k % 2)
-        hf_quant((2, 0))
-        h_mul(last, 0, 0)
-        turn(BLOCKS[6])
-        la_widen(3)
-        hf_quant((3, 0), 0, 1)
-        hf_quant((3, 0), 1, 2)
-        halves_over(("hm", BLOCKS[2]), hf_sb[3, 0])
+            up(last, k // 2, k % 2, mm())
+        hf_quant((2, 0), 0, 1)
+        halves_over(("hm", BLOCKS[2]), hf_sb[2, 0])
         hm_mix(BLOCKS[2], 1, "G")
         hm_mix(BLOCKS[2], 0, "S")
-        for k in range(1, 4):
+        for k in range(4):
             h_mul(last, k // 2, k % 2)
-        for i in range(2):
-            y_mul(*tiles[i][1:], range(3))
+        for i, n in enumerate([mm(), mm(), 7, 6]):
+            y_mul(*tiles[i][1:], n, range(2))
+        for i in range(1):
+            y_mul(*tiles[i][1:], None, range(2, 3))
+        for G in range(3):
+            hf_quant((G, 0), 1, 2)
+        ring8 = [mm(), mm(), mm(), mm()]
+        turn(BLOCKS[6], ring8[0], ring8[1])
+        turn(last, ring8[2], ring8[3])
+        la_widen(3)
+        ring8.extend([mm(), mm(), 7, 6])
+        hf_quant((3, 0), 0, 1)
+        hf_quant((0, 1))
+        hf_quant((3, 0), 1, 2)
+        for i in range(1, 4):
+            y_mul(*tiles[i][1:], None, range(2, 3))
+        taken8 = [-1]
+
+        def nx():
+            taken8[0] = (taken8[0] + 1) % 8
+            return ring8[taken8[0]]
+
         for i in range(16):
-            y_mul(*tiles[i][1:], range(3, 4) if i < 2 else range(4))
-            if i == 3:
-                turn(last)
-            put(tiles[i], "V" if i == 14 else "S")
+            y_mul(*tiles[i][1:], None if i < 4 else nx(), range(3, 4) if i < 4 else range(4))
+            put(tiles[i], "V" if i in () else "S")
             if i == 0:
-                for G in range(3):
+                for G in range(1, 4):
                     hf_quant((G, 1))
-                la_mix("V")
                 dz_mix("V")
-                la_quant()
             if i == 3:
-                hf_quant(last)
                 for j in range(3):
                     hm_quant(BLOCKS[j])
                 dz_quant()
@@ -452,12 +482,14 @@ def tile_qlora_down_projection_s8_kernel(
                 hm_mix(BLOCKS[j], 1, "S" if j in S1 else "V")
             if 4 <= j < 9:
                 hm_quant(BLOCKS[j - 1])
+            if i == 5:
+                la_mix("V")
+            if i == 6:
+                la_quant()
             if i in DA:
-                da_mul(DA.index(i), 0, 4)
+                da_mul(DA.index(i), 0, 4, nx())
                 put(("da", DA.index(i), 0, 4), "S")
-            if i == Z0:
-                z_mul(0, 0, 4)
-                put(("z", 0, 0, 4), "S")
-        for pair in range(2):
-            z_mul(1, 2 * pair, 2 * pair + 2)
-            put(("z", 1, 2 * pair, 2 * pair + 2), "V" if pair == 0 else "S")
+        ends = [("z", 0, 0, 2), ("z", 0, 2, 4), ("da", 3, 0, 2), ("da", 3, 2, 4), ("z", 1, 0, 2), ("z", 1, 2, 3), ("z", 1, 3, 4)]
+        for j, key in enumerate(ends):
+            (z_mul if key[0] == "z" else da_mul)(*key[1:], nx())
+            put(key, "VS"[j % 2])

@@ -453,19 +453,20 @@ def tile_qlora_down_projection_s8_kernel(
         turn(last, ring8[2], ring8[3])
         la_widen(3)
         ring8.extend([mm(), mm(), 7, 6])
-        hf_quant((3, 0), 0, 1)
         hf_quant((0, 1))
+        hf_quant((3, 0), 0, 1)
         hf_quant((3, 0), 1, 2)
         for i in range(1, 4):
             y_mul(*tiles[i][1:], None, range(2, 3))
-        taken8 = [-1]
+        y_mul(*tiles[4][1:], ring8[0], range(3))
+        taken8 = [0]
 
         def nx():
             taken8[0] = (taken8[0] + 1) % 8
             return ring8[taken8[0]]
 
         for i in range(16):
-            y_mul(*tiles[i][1:], None if i < 4 else nx(), range(3, 4) if i < 4 else range(4))
+            y_mul(*tiles[i][1:], None if i < 5 else nx(), range(3, 4) if i < 5 else range(4))
             put(tiles[i], "V" if i in () else "S")
             if i == 0:
                 for G in range(1, 4):
@@ -489,7 +490,7 @@ def tile_qlora_down_projection_s8_kernel(
             if i in DA:
                 da_mul(DA.index(i), 0, 4, nx())
                 put(("da", DA.index(i), 0, 4), "S")
-        ends = [("z", 0, 0, 2), ("z", 0, 2, 4), ("da", 3, 0, 2), ("da", 3, 2, 4), ("z", 1, 0, 2), ("z", 1, 2, 3), ("z", 1, 3, 4)]
+        ends = [("z", 0, 0, 2), ("z", 0, 2, 4), ("z", 1, 0, 2), ("da", 3, 0, 2), ("da", 3, 2, 4), ("z", 1, 2, 3), ("z", 1, 3, 4)]
         for j, key in enumerate(ends):
             (z_mul if key[0] == "z" else da_mul)(*key[1:], nx())
-            put(key, "VS"[j % 2])
+            put(key, "SSSVSVS"[j])

@@ -20,7 +20,7 @@ COPY = mybir.ActivationFunctionType.Copy
 P = 128
 PASS = 512
 BLOCKS = [(G, g) for G in range(4) for g in range(2)]
-RINGS = {"xt": 2, "mix": 7, "pool": 1, "early": 1, "out": 10}
+RINGS = {"xt": 2, "mix": 7, "pool": 1, "half": 3, "out": 10}
 DA = (11, 13, 15)
 Z0 = 7
 HEAD_V = 40
@@ -73,10 +73,10 @@ def tile_qlora_down_projection_s8_kernel(
         nc.gpsimd.memset(down_sc[:].rearrange("p g n -> p (g n)").bitcast(I32), 0)
 
         x_parts = [(g, s, s + 1) for g in range(2) for s in range(4)]
-        x_raw = {(g, a): kept("x_raw%d%d" % (g, a), [P, b - a, K], BF16) for g, a, b in x_parts}
-        x_tile = {(g, s): x_raw[g, a][:, s - a, :] for g, a, b in x_parts for s in range(a, b)}
+        x_raw = [kept("x_raw%d" % g, [P, 4 * K], BF16) for g in range(2)]
+        x_tile = {(g, s): x_raw[g][:, part(K, s)] for g in range(2) for s in range(4)}
         w_raw = {(G, c): kept("w_raw%d%d" % (G, c), [P, 4, PASS], BF16) for G in range(4) for c in range(2)}
-        gate_sb = {b: kept("gate%d%d" % b, [P, 4, PASS], BF16) for b in BLOCKS}
+        gate_sb = {b: kept("gate%d%d" % b, [P, 4 * PASS], BF16)[:].rearrange("p (s f) -> p s f", s=4) for b in BLOCKS}
         words = [kept("words%d" % G, [P, 2 * N], U8) for G in range(4)]
         lbytes = kept("lbytes", [P, 4, 4 * R], U8)
         lscale = kept("lscale", [P, 16], F32)
@@ -87,13 +87,14 @@ def tile_qlora_down_projection_s8_kernel(
         gv = gate.rearrange("(g p s) f -> g p s f", p=P, s=4)
 
         def load_x(g, a, b):
-            nc.sync.dma_start(out=x_raw[g, a][:], in_=xv[g, :, a:b, :])
+            nc.sync.dma_start(out=x_tile[g, a], in_=xv[g, :, a, :])
 
         def load_w(G, c):
             nc.sync.dma_start(out=w_raw[G, c][:], in_=wv[c, :, :, part(PASS, G)])
 
         def load_gate(b):
-            nc.sync.dma_start(out=gate_sb[b][:], in_=gv[b[1], :, :, part(PASS, b[0])])
+            for rows in (slice(0, 2), slice(2, 4)) if b == (1, 1) else (slice(0, 4),):
+                nc.sync.dma_start(out=gate_sb[b][:, rows, :], in_=gv[b[1], :, rows, part(PASS, b[0])])
 
         def load_dz():
             nc.sync.dma_start(out=dz_raw[:], in_=dz.rearrange("(g p t) r -> p g t r", p=P, t=4))
@@ -164,6 +165,9 @@ def tile_qlora_down_projection_s8_kernel(
                 whole = stage((key, 2), "mix", [P, 4 * PASS], BF16)
                 staged[key] = [whole[:, part(1024, 0)], whole[:, part(1024, 1)]]
 
+        def half(key, u, ring):
+            staged.setdefault(key, [None, None])[u] = stage((key, u), ring, [P, 2 * PASS], BF16)[:]
+
         def quantize_halves(op, key):
             if (key, 2) in staged:
                 quantize(op, slice(0, PASS), staged[key, 2][:])
@@ -199,8 +203,10 @@ def tile_qlora_down_projection_s8_kernel(
             else:
                 quantize(w_q[G, c], part(256, u), staged["w", G, c][u])
 
-        h_sb = {b: w_raw[b][:].rearrange("p (u j) f -> p u (j f)", u=2) for b in BLOCKS}
-        hf_sb = {b: gate_sb[b][:].rearrange("p s f -> p (s f)") for b in BLOCKS}
+        h_sb = {(G, g): w_raw[G - 1, g][:].rearrange("p (u j) f -> p u (j f)", u=2) for G, g in BLOCKS[2:]}
+        for g in range(2):
+            h_sb[0, g] = x_raw[g][:, : 2 * K].rearrange("p (u m) -> p u m", u=2)
+        hf_sb = {b: gate_sb[b].rearrange("p s f -> p (s f)") for b in BLOCKS}
 
         def up(b, pair, u, n):
             G, g = b
@@ -222,7 +228,7 @@ def tile_qlora_down_projection_s8_kernel(
         def h_mul(b, pair, u):
             nc.vector.scalar_tensor_tensor(
                 out=h_sb[b][:, u, part(PASS, pair)].rearrange("p (m e) -> p m e", e=2),
-                in0=gate_sb[b][:].rearrange("p s (n u e) -> p u (s n) e", u=2, e=2)[:, u, part(256, pair), :],
+                in0=gate_sb[b].rearrange("p s (n u e) -> p u (s n) e", u=2, e=2)[:, u, part(256, pair), :],
                 scalar=0.0,
                 in1=banks["up", b, pair, u][:].rearrange("p i (n e) -> p (i n) e", e=2),
                 op0=ALU.max,
@@ -363,16 +369,10 @@ def tile_qlora_down_projection_s8_kernel(
         load_down()
         load_dz()
 
-        taken = [5]
-
-        def mm():
-            taken[0] = (taken[0] + 1) % 6
-            return taken[0]
-
         first = BLOCKS[0]
         for pair in range(2):
             for s in range(2 * pair, 2 * pair + 2):
-                x_turn(0, s, mm())
+                x_turn(0, s, s)
                 x_copy(0, s, "V" if s % 2 else "S")
             x_quant(0, pair)
         for c in range(2):
@@ -385,74 +385,89 @@ def tile_qlora_down_projection_s8_kernel(
         warm_up(4, 6)
         for pair in range(2):
             for s in range(2 * pair, 2 * pair + 2):
-                x_turn(1, s, mm() if pair == 0 else 9 - s)
+                x_turn(1, s, (4, 5, 7, 6)[s])
                 x_copy(1, s, "S", "xt" if pair == 0 else "pool")
             x_quant(1, pair)
-        halves(("w", 1, 0), True)
-        w_mix(1, 0, 0, 0, P, "S")
-        w_mix(1, 0, 1, 0, P, "G")
-        for k in range(4):
-            up(first, k // 2, k % 2, mm())
-            h_mul(first, k // 2, k % 2)
-        halves(("w", 1, 1), False)
-        w_mix(1, 1, 0, 0, P, "S")
-        w_mix(1, 1, 1, 0, P, "V")
-        w_quant(1, 0, 0)
-        w_quant(1, 1)
-        w_quant(1, 0, 1)
+        def step(i):
+            if i < 2:
+                return [((0, i), k // 2, k % 2) for k in range(4)]
+            return [((i // 2, k // 2), k % 2, i % 2) for k in range(4)]
 
-        for i in range(1, 7):
-            b = BLOCKS[i]
-            if i < 5:
-                nxt = ((i + 3) // 2, (i + 1) % 2)
-                halves(("w",) + nxt, True)
-                w_mix(*nxt, 1, 0, P, "G")
-                if i > 1:
-                    w_mix(*nxt, 0, 0, P, "S")
-            elif i == 5:
-                halves(("hm", BLOCKS[0]), True)
+        def ups(i, where, ahead):
+            for c in range(2):
+                for k in range(ahead):
+                    up_pass(*step(i)[k], c, where[k])
+            for k in range(ahead, 4):
+                up(*step(i)[k], where[k])
+
+        def hs(i):
+            for item in step(i):
+                h_mul(*item)
+
+        def w_half(G, c, u, engine):
+            half(("w", G, c), u, "pool" if engine == "G" else "half")
+            w_mix(G, c, u, 0, P, engine)
+
+        w_half(1, 0, 1, "G")
+        w_half(1, 0, 0, "S")
+        w_half(1, 1, 0, "S")
+        ups(0, (0, 1, 2, 3), 0)
+        hs(0)
+        w_quant(1, 0, 0)
+        w_quant(1, 1, 0)
+        w_quant(1, 0, 1)
+        where = {0: (0, 1, 2, 3), 1: (4, 5, 0, 1), 2: (2, 3, 7, 6)}
+        for i in range(1, 8):
+            if i < 6:
+                w_half((i + 2) // 2, 1, i % 2, "G")
+            elif i == 6:
+                half(("hm", BLOCKS[0]), 1, "pool")
                 hm_mix(BLOCKS[0], 1, "G")
             else:
                 halves_over(("hm", BLOCKS[1]), hf_sb[1, 0])
                 hm_mix(BLOCKS[1], 1, "G")
-            for k in range(4):
-                pair, u = (k % 2, k // 2) if i in UFIRST else (k // 2, k % 2)
-                up(b, pair, u, mm())
-                h_mul(b, pair, u)
-            turn(BLOCKS[i - 1], 7, 6)
+            if i > 2:
+                where[i] = where[i - 2][2:] + where[i - 2][:2]
+            ups(i, where[i], (0, 0, 4, 2, 2, 2, 2, 2)[i])
+            if i >= 2:
+                turn(BLOCKS[i - 2], *where[i - 1][:2])
             if i < 5:
-                if i == 1:
-                    w_mix(*nxt, 0, 0, P, "S")
-                w_quant(*nxt)
-            elif i == 5:
-                for G in range(2):
-                    hf_quant((G, 0), 0, 1)
+                w_half((i + 3) // 2, 0, (i + 1) % 2, "S")
             if i >= 4:
                 la_widen(i - 4)
-            if i >= 5:
-                hm_mix(BLOCKS[i - 5], 0, "S")
-
+            if i == 5:
+                half(("hm", BLOCKS[0]), 0, "mix")
+                hm_mix(BLOCKS[0], 0, "S")
+            if i == 6:
+                halves(("hm", BLOCKS[2]), False)
+                hm_mix(BLOCKS[2], 0, "S")
+            if i == 7:
+                hm_mix(BLOCKS[1], 0, "S")
+            hs(i)
+            if i < 6:
+                w_quant((i + 2) // 2, 1, i % 2)
+            if i < 5:
+                w_quant((i + 3) // 2, 0, (i + 1) % 2)
+            if i == 5:
+                hf_quant((0, 0), 0, 1)
+            if i == 6:
+                hf_quant((1, 0), 0, 1)
+                hf_quant((2, 0), 0, 1)
         last = BLOCKS[7]
         tiles = [("y", g, s, half) for g in range(2) for s in range(4) for half in range(2)]
-        for k in range(4):
-            up(last, k // 2, k % 2, mm())
-        hf_quant((2, 0), 0, 1)
-        halves_over(("hm", BLOCKS[2]), hf_sb[2, 0])
-        hm_mix(BLOCKS[2], 1, "G")
-        hm_mix(BLOCKS[2], 0, "S")
-        for k in range(4):
-            h_mul(last, k // 2, k % 2)
-        for i, n in enumerate([mm(), mm(), 7, 6]):
-            y_mul(*tiles[i][1:], n, range(2))
+        y_banks = where[6][2:] + where[6][:2]
+        for G in range(2):
+            for i in range(2):
+                y_mul(*tiles[i][1:], y_banks[i], range(G, G + 1))
+        for i in range(2, 4):
+            y_mul(*tiles[i][1:], y_banks[i], range(2))
         for i in range(1):
             y_mul(*tiles[i][1:], None, range(2, 3))
         for G in range(3):
             hf_quant((G, 0), 1, 2)
-        ring8 = [mm(), mm(), mm(), mm()]
+        ring8 = list(where[7] + y_banks)
         turn(BLOCKS[6], ring8[0], ring8[1])
         turn(last, ring8[2], ring8[3])
-        la_widen(3)
-        ring8.extend([mm(), mm(), 7, 6])
         hf_quant((0, 1))
         hf_quant((3, 0), 0, 1)
         hf_quant((3, 0), 1, 2)
@@ -473,6 +488,7 @@ def tile_qlora_down_projection_s8_kernel(
                     hf_quant((G, 1))
                 dz_mix("V")
             if i == 3:
+                hm_mix(BLOCKS[2], 1, "V")
                 for j in range(3):
                     hm_quant(BLOCKS[j])
                 dz_quant()

@@ -186,8 +186,8 @@ def tile_qlora_down_projection_s8_kernel(
             out = staged["w", G, c][u]
             if engine == "G":
                 pool_copy(
-                    out.rearrange("p (n e j) -> p n j e", e=2, j=4)[:, first:last],
-                    w_raw[G, c][:].rearrange("p j (n u e) -> p u n j e", u=2, e=2)[:, u, first:last],
+                    out.rearrange("p (n e j) -> p n e j", e=2, j=4)[:, first:last],
+                    w_raw[G, c][:].rearrange("p j (n u e) -> p u n e j", u=2, e=2)[:, u, first:last],
                 )
             else:
                 ms = slice(first // 2, last // 2)
@@ -370,24 +370,31 @@ def tile_qlora_down_projection_s8_kernel(
         load_dz()
 
         first = BLOCKS[0]
-        for pair in range(2):
-            for s in range(2 * pair, 2 * pair + 2):
-                x_turn(0, s, s)
-                x_copy(0, s, "V" if s % 2 else "S")
-            x_quant(0, pair)
+        for s in range(4):
+            x_turn(0, s, s)
+            x_copy(0, s, "V" if s in (1,) else "S")
+            if s == 1:
+                x_quant(0, 0)
         for c in range(2):
             halves(("w", 0, c), False)
-            w_mix(0, c, 0, 0, P, "V")
-            w_mix(0, c, 1, 0, HEAD_V, "V")
-            w_mix(0, c, 1, HEAD_V, P, "S")
-        for c in range(2):
-            w_quant(0, c)
-        warm_up(4, 6)
-        for pair in range(2):
-            for s in range(2 * pair, 2 * pair + 2):
-                x_turn(1, s, (4, 5, 7, 6)[s])
-                x_copy(1, s, "S", "xt" if pair == 0 else "pool")
-            x_quant(1, pair)
+        w_mix(0, 0, 0, 0, P, "V")
+        w_mix(0, 0, 1, 0, P, "S")
+        x_quant(0, 1)
+        w_quant(0, 0, 0)
+        w_mix(0, 1, 0, 0, P, "V")
+        w_mix(0, 1, 1, 0, P, "S")
+        w_quant(0, 0, 1)
+        for u in range(2):
+            w_quant(0, 1, u)
+        warm_up(3, 6)
+        for s in range(4):
+            x_turn(1, s, (4, 5, 7, 6)[s])
+            x_copy(1, s, "V" if s in (1,) else "S", "xt" if s < 2 else "pool")
+            if s == 1:
+                x_quant(1, 0)
+        for i in range(2):
+            quantize(x_q[1, 1], part(2 * P, i), staged["x", 1, 1][:, part(K, i)])
+
         def step(i):
             if i < 2:
                 return [((0, i), k // 2, k % 2) for k in range(4)]
@@ -431,16 +438,17 @@ def tile_qlora_down_projection_s8_kernel(
             ups(i, where[i], (0, 0, 4, 2, 2, 2, 2, 2)[i])
             if i >= 2:
                 turn(BLOCKS[i - 2], *where[i - 1][:2])
+            if i == 1:
+                half(("hm", BLOCKS[0]), 0, "mix")
+                hm_mix(BLOCKS[0], 0, "S")
             if i < 5:
                 w_half((i + 3) // 2, 0, (i + 1) % 2, "S")
             if i >= 4:
                 la_widen(i - 4)
             if i == 5:
-                half(("hm", BLOCKS[0]), 0, "mix")
-                hm_mix(BLOCKS[0], 0, "S")
-            if i == 6:
                 halves(("hm", BLOCKS[2]), False)
-                hm_mix(BLOCKS[2], 0, "S")
+            if i in (5, 6):
+                hm_mix(BLOCKS[2], i - 5, "S")
             if i == 7:
                 hm_mix(BLOCKS[1], 0, "S")
             hs(i)
@@ -488,7 +496,6 @@ def tile_qlora_down_projection_s8_kernel(
                     hf_quant((G, 1))
                 dz_mix("V")
             if i == 3:
-                hm_mix(BLOCKS[2], 1, "V")
                 for j in range(3):
                     hm_quant(BLOCKS[j])
                 dz_quant()

@@ -20,13 +20,9 @@ COPY = mybir.ActivationFunctionType.Copy
 P = 128
 PASS = 512
 BLOCKS = [(G, g) for G in range(4) for g in range(2)]
-RINGS = {"xt": 2, "mix": 7, "pool": 1, "half": 3, "out": 10}
-DA = (11, 13, 15)
-Z0 = 7
-HEAD_V = 40
-UFIRST = ()
-S0 = ()
-S1 = (3, 5, 7)
+RINGS = {"xt": 2, "mix": 7, "early": 1, "pool": 1, "half": 2, "out": 10}
+DA_AFTER = (11, 13, 15)
+WARM_UPS = 3
 
 
 def tile_qlora_down_projection_s8_kernel(
@@ -72,7 +68,6 @@ def tile_qlora_down_projection_s8_kernel(
         down_sc = kept("down_sc", [P, 4, N], U8)
         nc.gpsimd.memset(down_sc[:].rearrange("p g n -> p (g n)").bitcast(I32), 0)
 
-        x_parts = [(g, s, s + 1) for g in range(2) for s in range(4)]
         x_raw = [kept("x_raw%d" % g, [P, 4 * K], BF16) for g in range(2)]
         x_tile = {(g, s): x_raw[g][:, part(K, s)] for g in range(2) for s in range(4)}
         w_raw = {(G, c): kept("w_raw%d%d" % (G, c), [P, 4, PASS], BF16) for G in range(4) for c in range(2)}
@@ -86,8 +81,9 @@ def tile_qlora_down_projection_s8_kernel(
         wv = w_up.rearrange("(c p j) f -> c p j f", p=P, j=4)
         gv = gate.rearrange("(g p s) f -> g p s f", p=P, s=4)
 
-        def load_x(g, a, b):
-            nc.sync.dma_start(out=x_tile[g, a], in_=xv[g, :, a, :])
+        def load_x(g):
+            for s in range(4):
+                nc.sync.dma_start(out=x_tile[g, s], in_=xv[g, :, s, :])
 
         def load_w(G, c):
             nc.sync.dma_start(out=w_raw[G, c][:], in_=wv[c, :, :, part(PASS, G)])
@@ -132,9 +128,9 @@ def tile_qlora_down_projection_s8_kernel(
             staged[key] = work.tile(shape, dtype, name=ring, bufs=RINGS[ring], align_bytes=64)
             return staged[key]
 
-        def warm_up(count, n):
+        def warm_up(n):
             out = bank("warm", n, [P, PASS])
-            for i in range(count):
+            for i in range(WARM_UPS):
                 nc.tensor.matmul(out[:], lhsT=w_raw[0, 0][:, 0, :P], rhs=w_raw[0, 0][:, 0, :], start=True, stop=True)
 
         def x_turn(g, s, n):
@@ -153,55 +149,39 @@ def tile_qlora_down_projection_s8_kernel(
                 banks["x", g, s][:].rearrange("p c u q -> p c q u"),
             )
 
-        def x_quant(g, pair):
-            quantize(x_q[g, pair], slice(0, 4 * P), staged["x", g, pair][:])
+        def x_quant(g, pair, first=0, last=2):
+            quantize(x_q[g, pair], slice(2 * P * first, 2 * P * last), staged["x", g, pair][:, K * first : K * last])
 
-        def halves(key, shared, ring="pool"):
-            if shared:
-                first = stage((key, 0), "mix", [P, 2 * PASS], BF16)
-                second = stage((key, 1), ring, [P, 2 * PASS], BF16)
-                staged[key] = [first[:], second[:]]
-            else:
-                whole = stage((key, 2), "mix", [P, 4 * PASS], BF16)
-                staged[key] = [whole[:, part(1024, 0)], whole[:, part(1024, 1)]]
+        def halves(key):
+            whole = stage((key, 2), "mix", [P, 4 * PASS], BF16)
+            staged[key] = [whole[:, part(1024, 0)], whole[:, part(1024, 1)]]
 
         def half(key, u, ring):
             staged.setdefault(key, [None, None])[u] = stage((key, u), ring, [P, 2 * PASS], BF16)[:]
 
-        def quantize_halves(op, key):
-            if (key, 2) in staged:
-                quantize(op, slice(0, PASS), staged[key, 2][:])
-            else:
-                for u in range(2):
-                    quantize(op, part(256, u), staged[key][u])
-
-        def halves_over(key, used):
-            first = stage((key, 0), "mix", [P, 2 * PASS], BF16)
-            staged[key] = [first[:], used[:, part(1024, 0)]]
-
         def pool_copy(out, in_):
             nc.gpsimd.tensor_scalar(out=out, in0=in_, scalar1=1.0, scalar2=0.0, op0=ALU.mult, op1=ALU.add)
 
-        def w_mix(G, c, u, first, last, engine):
+        def w_mix(G, c, u, engine):
             out = staged["w", G, c][u]
             if engine == "G":
                 pool_copy(
-                    out.rearrange("p (n e j) -> p n e j", e=2, j=4)[:, first:last],
-                    w_raw[G, c][:].rearrange("p j (n u e) -> p u n e j", u=2, e=2)[:, u, first:last],
+                    out.rearrange("p (n e j) -> p n e j", e=2, j=4),
+                    w_raw[G, c][:].rearrange("p j (n u e) -> p u n e j", u=2, e=2)[:, u],
                 )
             else:
-                ms = slice(first // 2, last // 2)
                 copy_on(
                     engine,
-                    out.rearrange("p (m i e j) -> p m j i e", i=2, e=2, j=4)[:, ms],
-                    w_raw[G, c][:].rearrange("p j (m i u e) -> p u m j i e", i=2, u=2, e=2)[:, u, ms],
+                    out.rearrange("p (m i e j) -> p m j i e", i=2, e=2, j=4),
+                    w_raw[G, c][:].rearrange("p j (m i u e) -> p u m j i e", i=2, u=2, e=2)[:, u],
                 )
 
-        def w_quant(G, c, u=None):
-            if u is None:
-                quantize_halves(w_q[G, c], ("w", G, c))
-            else:
-                quantize(w_q[G, c], part(256, u), staged["w", G, c][u])
+        def w_half(G, c, u, engine, ring):
+            half(("w", G, c), u, ring)
+            w_mix(G, c, u, engine)
+
+        def w_quant(G, c, u):
+            quantize(w_q[G, c], part(256, u), staged["w", G, c][u])
 
         h_sb = {(G, g): w_raw[G - 1, g][:].rearrange("p (u j) f -> p u (j f)", u=2) for G, g in BLOCKS[2:]}
         for g in range(2):
@@ -215,7 +195,7 @@ def tile_qlora_down_projection_s8_kernel(
                 for c in range(2):
                     multiply(out[:, i, :], x_q[g, pair], part(P, 2 * i + c), w_q[G, c], part(256, u), c == 0, c == 1)
 
-        def up_pass(b, pair, u, c, n=None):
+        def up_pass(b, pair, u, c, n):
             G, g = b
             if c == 0:
                 bank(("up", b, pair, u), n, [P, 2, 256])
@@ -242,9 +222,9 @@ def tile_qlora_down_projection_s8_kernel(
                 for u in range(2):
                     nc.tensor.transpose(out[:, i, u, :], hw[:, u, part(P, 2 * pair + i)], ident[:])
 
-        def h_copy(b, pair, engine):
+        def h_copy(b, pair):
             copy_on(
-                engine,
+                "S",
                 hf_sb[b][:, part(1024, pair)].bitcast(F32).rearrange("p (i q u) -> p i q u", i=2, u=2),
                 banks["h", b, pair][:].rearrange("p i u q -> p i q u"),
             )
@@ -252,7 +232,7 @@ def tile_qlora_down_projection_s8_kernel(
         def turn(b, n0, n1):
             for pair in range(2):
                 h_turn(b, pair, (n0, n1)[pair])
-                h_copy(b, pair, "S")
+                h_copy(b, pair)
 
         def hf_quant(b, first=0, last=2):
             quantize(hf_q[b], slice(256 * first, 256 * last), hf_sb[b][:, 1024 * first : 1024 * last])
@@ -271,16 +251,17 @@ def tile_qlora_down_projection_s8_kernel(
                     h_sb[b][:, u, :].rearrange("p (s n i e) -> p n s i e", s=4, i=2, e=2),
                 )
 
-        def hm_quant(b, u=None):
-            if u is None:
-                quantize_halves(hm_q[b], ("hm", b))
+        def hm_quant(b):
+            if (("hm", b), 2) in staged:
+                quantize(hm_q[b], slice(0, PASS), staged[("hm", b), 2][:])
             else:
-                quantize(hm_q[b], part(256, u), staged["hm", b][u])
+                for u in range(2):
+                    quantize(hm_q[b], part(256, u), staged["hm", b][u])
 
-        def dz_mix(engine):
+        def dz_mix():
             t = stage("dz", "xt", [P, 2 * R * 4], BF16)
             copy_on(
-                engine,
+                "V",
                 t[:].rearrange("p (g r i t) -> p g r t i", g=2, i=4, t=4),
                 dz_raw[:].rearrange("p g t (r i) -> p g r t i", i=4),
             )
@@ -299,10 +280,10 @@ def tile_qlora_down_projection_s8_kernel(
                     scale=lscale[:, 4 * G + t : 4 * G + t + 1],
                 )
 
-        def la_mix(engine):
+        def la_mix():
             t = stage("la", "mix", [P, 4 * R * 4], BF16)
             copy_on(
-                engine,
+                "V",
                 t[:].rearrange("p (g r i t) -> p g r t i", g=4, i=4, t=4),
                 staged["la_wide"][:].rearrange("p g t (r i) -> p g r t i", i=4),
             )
@@ -314,7 +295,7 @@ def tile_qlora_down_projection_s8_kernel(
         zv = z.rearrange("(g q s) r -> g q (s r)", q=P, s=4)
         dav = da.rearrange("(g n a) r -> g n (a r)", n=P, a=4)
 
-        def y_mul(g, s, half, n, groups=range(4)):
+        def y_mul(g, s, half, groups, n=None):
             if 0 in groups:
                 bank(("y", g, s, half), n, [P, 512])
             out = banks["y", g, s, half]
@@ -341,23 +322,21 @@ def tile_qlora_down_projection_s8_kernel(
                 for g in range(2):
                     multiply(out[:, part(R, a - first)], hm_q[G, g], part(P, a), dz_q, part(R, g), g == 0, g == 1)
 
-        def put(key, engine, queue=nc.sync):
+        def put(key, engine):
             t = stage(key, "out", list(banks[key].shape), F32)
             copy_on(engine, t[:], banks[key][:])
             if key[0] == "y":
                 dst = yv[key[1], key[2], :, part(512, key[3])]
             else:
                 dst = (zv if key[0] == "z" else dav)[key[1], :, R * key[2] : R * key[3]]
-            queue.dma_start(out=dst, in_=t[:])
+            nc.sync.dma_start(out=dst, in_=t[:])
 
         ctx.enter_context(tc.manual_schedule())
 
-        for piece in x_parts[:4]:
-            load_x(*piece)
+        load_x(0)
         for c in range(2):
             load_w(0, c)
-        for piece in x_parts[4:]:
-            load_x(*piece)
+        load_x(1)
         load_gate(BLOCKS[0])
         load_w(1, 0)
         for i in range(1, 8):
@@ -369,151 +348,154 @@ def tile_qlora_down_projection_s8_kernel(
         load_down()
         load_dz()
 
-        first = BLOCKS[0]
         for s in range(4):
             x_turn(0, s, s)
-            x_copy(0, s, "V" if s in (1,) else "S")
+            x_copy(0, s, "V" if s == 1 else "S")
             if s == 1:
                 x_quant(0, 0)
         for c in range(2):
-            halves(("w", 0, c), False)
-        w_mix(0, 0, 0, 0, P, "V")
-        w_mix(0, 0, 1, 0, P, "S")
+            halves(("w", 0, c))
+        w_mix(0, 0, 0, "V")
+        w_mix(0, 0, 1, "S")
         x_quant(0, 1)
         w_quant(0, 0, 0)
-        w_mix(0, 1, 0, 0, P, "V")
-        w_mix(0, 1, 1, 0, P, "S")
+        w_mix(0, 1, 0, "V")
+        w_mix(0, 1, 1, "S")
         w_quant(0, 0, 1)
         for u in range(2):
             w_quant(0, 1, u)
-        warm_up(3, 6)
+        warm_up(6)
         for s in range(4):
             x_turn(1, s, (4, 5, 7, 6)[s])
-            x_copy(1, s, "V" if s in (1,) else "S", "xt" if s < 2 else "pool")
+            x_copy(1, s, "V" if s == 1 else "S", "xt" if s < 2 else "early")
             if s == 1:
                 x_quant(1, 0)
         for i in range(2):
-            quantize(x_q[1, 1], part(2 * P, i), staged["x", 1, 1][:, part(K, i)])
+            x_quant(1, 1, i, i + 1)
 
         def step(i):
             if i < 2:
                 return [((0, i), k // 2, k % 2) for k in range(4)]
             return [((i // 2, k // 2), k % 2, i % 2) for k in range(4)]
 
-        def ups(i, where, ahead):
+        def step_up(i, where, ahead):
             for c in range(2):
                 for k in range(ahead):
                     up_pass(*step(i)[k], c, where[k])
             for k in range(ahead, 4):
                 up(*step(i)[k], where[k])
 
-        def hs(i):
+        def step_h(i):
             for item in step(i):
                 h_mul(*item)
 
-        def w_half(G, c, u, engine):
-            half(("w", G, c), u, "pool" if engine == "G" else "half")
-            w_mix(G, c, u, 0, P, engine)
-
-        w_half(1, 0, 1, "G")
-        w_half(1, 0, 0, "S")
-        w_half(1, 1, 0, "S")
-        ups(0, (0, 1, 2, 3), 0)
-        hs(0)
-        w_quant(1, 0, 0)
-        w_quant(1, 1, 0)
-        w_quant(1, 0, 1)
         where = {0: (0, 1, 2, 3), 1: (4, 5, 0, 1), 2: (2, 3, 7, 6)}
+        for i in range(3, 8):
+            where[i] = where[i - 2][2:] + where[i - 2][:2]
+
+        w_half(1, 0, 1, "G", "early")
+        w_half(1, 0, 0, "S", "half")
+        w_half(1, 1, 0, "S", "pool")
+        step_up(0, where[0], 0)
+        step_h(0)
+        w_quant(1, 0, 0)
+        w_quant(1, 0, 1)
+        w_quant(1, 1, 0)
         for i in range(1, 8):
+            second = ((i + 2) // 2, 1, i % 2)
+            first = ((i + 3) // 2, 0, (i + 1) % 2)
             if i < 6:
-                w_half((i + 2) // 2, 1, i % 2, "G")
+                w_half(*second, "G", "pool")
             elif i == 6:
                 half(("hm", BLOCKS[0]), 1, "pool")
                 hm_mix(BLOCKS[0], 1, "G")
             else:
-                halves_over(("hm", BLOCKS[1]), hf_sb[1, 0])
+                half(("hm", BLOCKS[1]), 0, "mix")
+                staged["hm", BLOCKS[1]][1] = hf_sb[1, 0][:, part(1024, 0)]
                 hm_mix(BLOCKS[1], 1, "G")
-            if i > 2:
-                where[i] = where[i - 2][2:] + where[i - 2][:2]
-            ups(i, where[i], (0, 0, 4, 2, 2, 2, 2, 2)[i])
+            step_up(i, where[i], 0 if i < 2 else 4 if i == 2 else 2)
             if i >= 2:
                 turn(BLOCKS[i - 2], *where[i - 1][:2])
             if i == 1:
                 half(("hm", BLOCKS[0]), 0, "mix")
                 hm_mix(BLOCKS[0], 0, "S")
             if i < 5:
-                w_half((i + 3) // 2, 0, (i + 1) % 2, "S")
+                w_half(*first, "S", "half")
             if i >= 4:
                 la_widen(i - 4)
             if i == 5:
-                halves(("hm", BLOCKS[2]), False)
+                halves(("hm", BLOCKS[2]))
             if i in (5, 6):
                 hm_mix(BLOCKS[2], i - 5, "S")
             if i == 7:
                 hm_mix(BLOCKS[1], 0, "S")
-            hs(i)
+            step_h(i)
             if i < 6:
-                w_quant((i + 2) // 2, 1, i % 2)
+                w_quant(*second)
             if i < 5:
-                w_quant((i + 3) // 2, 0, (i + 1) % 2)
+                w_quant(*first)
             if i == 5:
                 hf_quant((0, 0), 0, 1)
             if i == 6:
                 hf_quant((1, 0), 0, 1)
                 hf_quant((2, 0), 0, 1)
-        last = BLOCKS[7]
-        tiles = [("y", g, s, half) for g in range(2) for s in range(4) for half in range(2)]
+
+        tiles = [("y", g, s, half_n) for g in range(2) for s in range(4) for half_n in range(2)]
         y_banks = where[6][2:] + where[6][:2]
         for G in range(2):
             for i in range(2):
-                y_mul(*tiles[i][1:], y_banks[i], range(G, G + 1))
+                y_mul(*tiles[i][1:], [G], y_banks[i])
         for i in range(2, 4):
-            y_mul(*tiles[i][1:], y_banks[i], range(2))
-        for i in range(1):
-            y_mul(*tiles[i][1:], None, range(2, 3))
+            y_mul(*tiles[i][1:], range(2), y_banks[i])
+        y_mul(*tiles[0][1:], [2])
         for G in range(3):
             hf_quant((G, 0), 1, 2)
-        ring8 = list(where[7] + y_banks)
-        turn(BLOCKS[6], ring8[0], ring8[1])
-        turn(last, ring8[2], ring8[3])
+        turn(BLOCKS[6], *where[7][:2])
+        turn(BLOCKS[7], *where[7][2:])
         hf_quant((0, 1))
         hf_quant((3, 0), 0, 1)
         hf_quant((3, 0), 1, 2)
         for i in range(1, 4):
-            y_mul(*tiles[i][1:], None, range(2, 3))
-        y_mul(*tiles[4][1:], ring8[0], range(3))
-        taken8 = [0]
-
-        def nx():
-            taken8[0] = (taken8[0] + 1) % 8
-            return ring8[taken8[0]]
+            y_mul(*tiles[i][1:], [2])
+        turns = list(where[7] + y_banks) * 3
+        y_mul(*tiles[4][1:], range(3), turns.pop(0))
 
         for i in range(16):
-            y_mul(*tiles[i][1:], None if i < 5 else nx(), range(3, 4) if i < 5 else range(4))
-            put(tiles[i], "V" if i in () else "S")
+            if i < 5:
+                y_mul(*tiles[i][1:], [3])
+            else:
+                y_mul(*tiles[i][1:], range(4), turns.pop(0))
+            put(tiles[i], "S")
             if i == 0:
                 for G in range(1, 4):
                     hf_quant((G, 1))
-                dz_mix("V")
+                dz_mix()
             if i == 3:
-                for j in range(3):
-                    hm_quant(BLOCKS[j])
+                for b in BLOCKS[:3]:
+                    hm_quant(b)
                 dz_quant()
-            j = i
-            if 3 <= j < 8:
-                halves(("hm", BLOCKS[j]), False)
-                hm_mix(BLOCKS[j], 0, "S" if j in S0 else "V")
-                hm_mix(BLOCKS[j], 1, "S" if j in S1 else "V")
-            if 4 <= j < 9:
-                hm_quant(BLOCKS[j - 1])
+            if 3 <= i < 8:
+                halves(("hm", BLOCKS[i]))
+                hm_mix(BLOCKS[i], 0, "V")
+                hm_mix(BLOCKS[i], 1, "S" if i % 2 else "V")
+            if 4 <= i < 9:
+                hm_quant(BLOCKS[i - 1])
             if i == 5:
-                la_mix("V")
+                la_mix()
             if i == 6:
                 la_quant()
-            if i in DA:
-                da_mul(DA.index(i), 0, 4, nx())
-                put(("da", DA.index(i), 0, 4), "S")
-        ends = [("z", 0, 0, 2), ("z", 0, 2, 4), ("z", 1, 0, 2), ("da", 3, 0, 2), ("da", 3, 2, 4), ("z", 1, 2, 3), ("z", 1, 3, 4)]
-        for j, key in enumerate(ends):
-            (z_mul if key[0] == "z" else da_mul)(*key[1:], nx())
-            put(key, "SSSVSVS"[j])
+            if i in DA_AFTER:
+                da_mul(DA_AFTER.index(i), 0, 4, turns.pop(0))
+                put(("da", DA_AFTER.index(i), 0, 4), "S")
+
+        for key, engine in (
+            (("z", 0, 0, 2), "S"),
+            (("z", 0, 2, 4), "S"),
+            (("z", 1, 0, 2), "S"),
+            (("da", 3, 0, 2), "V"),
+            (("da", 3, 2, 4), "S"),
+            (("z", 1, 2, 3), "V"),
+            (("z", 1, 3, 4), "S"),
+        ):
+            (z_mul if key[0] == "z" else da_mul)(*key[1:], turns.pop(0))
+            put(key, engine)

@@ -421,14 +421,12 @@ def tile_qlora_down_projection_s8_kernel(
                 hm_mix(BLOCKS[0], 0, "S")
             if i < 5:
                 w_half(*first, "S", "half")
-            if i >= 4:
-                la_widen(i - 4)
-            if i == 5:
+            if i in (5, 7):
+                for G in (i - 5, i - 4):
+                    la_widen(G)
+            if i == 6:
                 halves(("hm", BLOCKS[2]))
-            if i in (5, 6):
-                hm_mix(BLOCKS[2], i - 5, "S")
-            if i == 7:
-                hm_mix(BLOCKS[1], 0, "S")
+                hm_mix(BLOCKS[2], 1, "S")
             step_h(i)
             if i < 6:
                 w_quant(*second)
@@ -453,6 +451,7 @@ def tile_qlora_down_projection_s8_kernel(
         turn(BLOCKS[6], *where[7][:2])
         turn(BLOCKS[7], *where[7][2:])
         hf_quant((0, 1))
+        hm_mix(BLOCKS[1], 0, "V")
         hf_quant((3, 0), 0, 1)
         hf_quant((3, 0), 1, 2)
         for i in range(1, 4):
@@ -470,6 +469,8 @@ def tile_qlora_down_projection_s8_kernel(
                 for G in range(1, 4):
                     hf_quant((G, 1))
                 dz_mix()
+            if i == 1:
+                hm_mix(BLOCKS[2], 0, "V")
             if i == 3:
                 for b in BLOCKS[:3]:
                     hm_quant(b)

@@ -342,10 +342,9 @@ def tile_qlora_down_projection_s8_kernel(
         for i in range(1, 8):
             if i < 6:
                 load_w((i + 2) // 2, i % 2)
-            if i == 6:
-                load_lora()
             load_gate(BLOCKS[i])
         load_down()
+        load_lora()
         load_dz()
 
         for s in range(4):
@@ -421,12 +420,13 @@ def tile_qlora_down_projection_s8_kernel(
                 hm_mix(BLOCKS[0], 0, "S")
             if i < 5:
                 w_half(*first, "S", "half")
-            if i in (5, 7):
-                for G in (i - 5, i - 4):
-                    la_widen(G)
-            if i == 6:
+            if i == 5:
                 halves(("hm", BLOCKS[2]))
-                hm_mix(BLOCKS[2], 1, "S")
+            if i in (5, 6):
+                hm_mix(BLOCKS[2], i - 5, "S")
+            if i == 7:
+                halves(("hm", BLOCKS[3]))
+                hm_mix(BLOCKS[3], 1, "S")
             step_h(i)
             if i < 6:
                 w_quant(*second)
@@ -469,16 +469,18 @@ def tile_qlora_down_projection_s8_kernel(
                 for G in range(1, 4):
                     hf_quant((G, 1))
                 dz_mix()
-            if i == 1:
-                hm_mix(BLOCKS[2], 0, "V")
+            if i < 4:
+                la_widen(i)
             if i == 3:
                 for b in BLOCKS[:3]:
                     hm_quant(b)
                 dz_quant()
-            if 3 <= i < 8:
+            if i == 3:
+                hm_mix(BLOCKS[3], 0, "V")
+            if 4 <= i < 8:
                 halves(("hm", BLOCKS[i]))
                 hm_mix(BLOCKS[i], 0, "V")
-                hm_mix(BLOCKS[i], 1, "S" if i % 2 else "V")
+                hm_mix(BLOCKS[i], 1, "S" if i == 7 else "V")
             if 4 <= i < 9:
                 hm_quant(BLOCKS[i - 1])
             if i == 5:

@@ -20,9 +20,7 @@ COPY = mybir.ActivationFunctionType.Copy
 P = 128
 PASS = 512
 BLOCKS = [(G, g) for G in range(4) for g in range(2)]
-RINGS = {"xt": 2, "mix": 7, "early": 1, "pool": 1, "half": 2, "out": 10}
-DA_AFTER = (11, 13, 15)
-WARM_UPS = 3
+RINGS = {"xt": 2, "mix": 3, "early": 1, "half": 2, "out": 10}
 
 
 def tile_qlora_down_projection_s8_kernel(
@@ -68,10 +66,14 @@ def tile_qlora_down_projection_s8_kernel(
         down_sc = kept("down_sc", [P, 4, N], U8)
         nc.gpsimd.memset(down_sc[:].rearrange("p g n -> p (g n)").bitcast(I32), 0)
 
-        x_raw = [kept("x_raw%d" % g, [P, 4 * K], BF16) for g in range(2)]
-        x_tile = {(g, s): x_raw[g][:, part(K, s)] for g in range(2) for s in range(4)}
-        w_raw = {(G, c): kept("w_raw%d%d" % (G, c), [P, 4, PASS], BF16) for G in range(4) for c in range(2)}
-        gate_sb = {b: kept("gate%d%d" % b, [P, 4 * PASS], BF16)[:].rearrange("p (s f) -> p s f", s=4) for b in BLOCKS}
+        x_raw = kept("x_raw", [P, 8 * K], BF16)
+        x_tile = {(g, s): x_raw[:, part(K, 4 * g + s)] for g in range(2) for s in range(4)}
+        w_both = [kept("w_raw%d" % G, [P, 8 * PASS], BF16) for G in range(4)]
+        w_raw = {
+            (G, c): w_both[G][:, part(4 * PASS, c)].rearrange("p (j f) -> p j f", j=4) for G in range(4) for c in range(2)
+        }
+        gate_row = [kept("gate%d" % q, [P, 8 * PASS], BF16) for q in range(4)]
+        gate_sb = {(G, q): gate_row[q][:, part(2 * PASS, G)] for G in range(4) for q in range(4)}
         words = [kept("words%d" % G, [P, 2 * N], U8) for G in range(4)]
         lbytes = kept("lbytes", [P, 4, 4 * R], U8)
         lscale = kept("lscale", [P, 16], F32)
@@ -81,16 +83,19 @@ def tile_qlora_down_projection_s8_kernel(
         wv = w_up.rearrange("(c p j) f -> c p j f", p=P, j=4)
         gv = gate.rearrange("(g p s) f -> g p s f", p=P, s=4)
 
-        def load_x(g):
-            for s in range(4):
+        def load_x(g, pair):
+            for s in range(2 * pair, 2 * pair + 2):
                 nc.sync.dma_start(out=x_tile[g, s], in_=xv[g, :, s, :])
 
         def load_w(G, c):
-            nc.sync.dma_start(out=w_raw[G, c][:], in_=wv[c, :, :, part(PASS, G)])
+            nc.sync.dma_start(out=w_raw[G, c], in_=wv[c, :, :, part(PASS, G)])
 
         def load_gate(b):
-            for rows in (slice(0, 2), slice(2, 4)) if b == (1, 1) else (slice(0, 4),):
-                nc.sync.dma_start(out=gate_sb[b][:, rows, :], in_=gv[b[1], :, rows, part(PASS, b[0])])
+            for pair in range(2):
+                nc.sync.dma_start(
+                    out=gate_sb[b[0], 2 * b[1] + pair].rearrange("p (s f) -> p s f", s=2),
+                    in_=gv[b[1], :, part(2, pair), part(PASS, b[0])],
+                )
 
         def load_dz():
             nc.sync.dma_start(out=dz_raw[:], in_=dz.rearrange("(g p t) r -> p g t r", p=P, t=4))
@@ -113,25 +118,27 @@ def tile_qlora_down_projection_s8_kernel(
 
         x_q = {(g, pair): operand("x%d%d" % (g, pair), 4 * P) for g in range(2) for pair in range(2)}
         w_q = {(G, c): operand("w%d%d" % (G, c), PASS) for G in range(4) for c in range(2)}
-        hf_q = {b: operand("hf%d%d" % b, PASS) for b in BLOCKS}
-        hm_q = {b: operand("hm%d%d" % b, PASS) for b in BLOCKS}
+        hf_q = [operand("hf%d" % q, 2 * PASS) for q in range(4)]
+        hm_q = [operand("hm%d" % G, 2 * PASS) for G in range(4)]
         dz_q = operand("dz", 2 * R)
         la_q = operand("la", 4 * R)
         banks = {}
         staged = {}
+        number = {}
 
         def bank(key, n, shape):
             banks[key] = psum.tile(shape, F32, name="bank%d" % n, bufs=1)
+            number[key] = n
             return banks[key]
 
         def stage(key, ring, shape, dtype):
             staged[key] = work.tile(shape, dtype, name=ring, bufs=RINGS[ring], align_bytes=64)
             return staged[key]
 
-        def warm_up(n):
+        def warm_up(n, count, src):
             out = bank("warm", n, [P, PASS])
-            for i in range(WARM_UPS):
-                nc.tensor.matmul(out[:], lhsT=w_raw[0, 0][:, 0, :P], rhs=w_raw[0, 0][:, 0, :], start=True, stop=True)
+            for i in range(count):
+                nc.tensor.matmul(out[:], lhsT=src[:, :P], rhs=src[:, :PASS], start=True, stop=True)
 
         def x_turn(g, s, n):
             out = bank(("x", g, s), n, [P, 2, 2, P])
@@ -152,12 +159,13 @@ def tile_qlora_down_projection_s8_kernel(
         def x_quant(g, pair, first=0, last=2):
             quantize(x_q[g, pair], slice(2 * P * first, 2 * P * last), staged["x", g, pair][:, K * first : K * last])
 
-        def halves(key):
-            whole = stage((key, 2), "mix", [P, 4 * PASS], BF16)
-            staged[key] = [whole[:, part(1024, 0)], whole[:, part(1024, 1)]]
+        def quarters(key):
+            whole = stage(key, "mix", [P, 8 * PASS], BF16)
+            return [whole[:, part(1024, m)] for m in range(4)]
 
         def half(key, u, ring):
-            staged.setdefault(key, [None, None])[u] = stage((key, u), ring, [P, 2 * PASS], BF16)[:]
+            where = staged["pool"] if ring == "pool" else stage((key, u), ring, [P, 2 * PASS], BF16)[:]
+            staged.setdefault(key, [None, None])[u] = where
 
         def pool_copy(out, in_):
             nc.gpsimd.tensor_scalar(out=out, in0=in_, scalar1=1.0, scalar2=0.0, op0=ALU.mult, op1=ALU.add)
@@ -167,13 +175,13 @@ def tile_qlora_down_projection_s8_kernel(
             if engine == "G":
                 pool_copy(
                     out.rearrange("p (n e j) -> p n e j", e=2, j=4),
-                    w_raw[G, c][:].rearrange("p j (n u e) -> p u n e j", u=2, e=2)[:, u],
+                    w_raw[G, c].rearrange("p j (n u e) -> p u n e j", u=2, e=2)[:, u],
                 )
             else:
                 copy_on(
                     engine,
                     out.rearrange("p (m i e j) -> p m j i e", i=2, e=2, j=4),
-                    w_raw[G, c][:].rearrange("p j (m i u e) -> p u m j i e", i=2, u=2, e=2)[:, u],
+                    w_raw[G, c].rearrange("p j (m i u e) -> p u m j i e", i=2, u=2, e=2)[:, u],
                 )
 
         def w_half(G, c, u, engine, ring):
@@ -183,17 +191,8 @@ def tile_qlora_down_projection_s8_kernel(
         def w_quant(G, c, u):
             quantize(w_q[G, c], part(256, u), staged["w", G, c][u])
 
-        h_sb = {(G, g): w_raw[G - 1, g][:].rearrange("p (u j) f -> p u (j f)", u=2) for G, g in BLOCKS[2:]}
-        for g in range(2):
-            h_sb[0, g] = x_raw[g][:, : 2 * K].rearrange("p (u m) -> p u m", u=2)
-        hf_sb = {b: gate_sb[b].rearrange("p s f -> p (s f)") for b in BLOCKS}
-
-        def up(b, pair, u, n):
-            G, g = b
-            out = bank(("up", b, pair, u), n, [P, 2, 256])
-            for i in range(2):
-                for c in range(2):
-                    multiply(out[:, i, :], x_q[g, pair], part(P, 2 * i + c), w_q[G, c], part(256, u), c == 0, c == 1)
+        h_all = [x_raw[:, : 4 * K]] + [w_both[G][:] for G in range(3)]
+        h_sb = {(G, g): h_all[G][:, part(4 * PASS, g)].rearrange("p (u m) -> p u m", u=2) for G, g in BLOCKS}
 
         def up_pass(b, pair, u, c, n):
             G, g = b
@@ -208,7 +207,7 @@ def tile_qlora_down_projection_s8_kernel(
         def h_mul(b, pair, u):
             nc.vector.scalar_tensor_tensor(
                 out=h_sb[b][:, u, part(PASS, pair)].rearrange("p (m e) -> p m e", e=2),
-                in0=gate_sb[b].rearrange("p s (n u e) -> p u (s n) e", u=2, e=2)[:, u, part(256, pair), :],
+                in0=gate_sb[b[0], 2 * b[1] + pair].rearrange("p (m u e) -> p u m e", u=2, e=2)[:, u],
                 scalar=0.0,
                 in1=banks["up", b, pair, u][:].rearrange("p i (n e) -> p (i n) e", e=2),
                 op0=ALU.max,
@@ -222,41 +221,38 @@ def tile_qlora_down_projection_s8_kernel(
                 for u in range(2):
                     nc.tensor.transpose(out[:, i, u, :], hw[:, u, part(P, 2 * pair + i)], ident[:])
 
-        def h_copy(b, pair):
+        def h_copy(b, pair, engine="S"):
             copy_on(
-                "S",
-                hf_sb[b][:, part(1024, pair)].bitcast(F32).rearrange("p (i q u) -> p i q u", i=2, u=2),
+                engine,
+                gate_sb[b[0], 2 * b[1] + pair].bitcast(F32).rearrange("p (i q u) -> p i q u", i=2, u=2),
                 banks["h", b, pair][:].rearrange("p i u q -> p i q u"),
             )
 
-        def turn(b, n0, n1):
-            for pair in range(2):
-                h_turn(b, pair, (n0, n1)[pair])
-                h_copy(b, pair)
+        def hf_quant(q, first, last):
+            quantize(hf_q[q], slice(256 * first, 256 * last), gate_row[q][:, 1024 * first : 1024 * last])
 
-        def hf_quant(b, first=0, last=2):
-            quantize(hf_q[b], slice(256 * first, 256 * last), hf_sb[b][:, 1024 * first : 1024 * last])
-
-        def hm_mix(b, u, engine):
-            out = staged["hm", b][u]
+        def hm_mix(G, first, last, engine):
+            out = staged["hm", G][:, 1024 * first : 1024 * last]
+            in_ = h_all[G][:, 1024 * first : 1024 * last]
             if engine == "G":
                 pool_copy(
-                    out.rearrange("p (e n s) -> p e n s", e=2, s=4),
-                    h_sb[b][:, u, :].rearrange("p (s n e) -> p e n s", s=4, e=2),
+                    out.rearrange("p (e n s) -> p e n s", e=2, s=4), in_.rearrange("p (s n e) -> p e n s", s=4, e=2)
+                )
+            elif last - first == 1:
+                copy_on(
+                    engine,
+                    out.rearrange("p (e n i s) -> p n s i e", e=2, i=2, s=4),
+                    in_.rearrange("p (s n i e) -> p n s i e", s=4, i=2, e=2),
                 )
             else:
                 copy_on(
                     engine,
-                    out.rearrange("p (e n i s) -> p n s i e", e=2, i=2, s=4),
-                    h_sb[b][:, u, :].rearrange("p (s n i e) -> p n s i e", s=4, i=2, e=2),
+                    out.rearrange("p (m e n s) -> p m e n s", e=2, n=P, s=4),
+                    in_.rearrange("p (m s n e) -> p m e n s", s=4, n=P, e=2),
                 )
 
-        def hm_quant(b):
-            if (("hm", b), 2) in staged:
-                quantize(hm_q[b], slice(0, PASS), staged[("hm", b), 2][:])
-            else:
-                for u in range(2):
-                    quantize(hm_q[b], part(256, u), staged["hm", b][u])
+        def hm_quant(G, first=0, last=4):
+            quantize(hm_q[G], slice(256 * first, 256 * last), staged["hm", G][:, 1024 * first : 1024 * last])
 
         def dz_mix():
             t = stage("dz", "xt", [P, 2 * R * 4], BF16)
@@ -271,7 +267,8 @@ def tile_qlora_down_projection_s8_kernel(
 
         def la_widen(G):
             if G == 0:
-                stage("la_wide", "mix", [P, 4, 4, R], BF16)
+                staged["la"] = stage("lora", "mix", [P, 8 * PASS], BF16)[:, : 4 * PASS]
+                staged["la_wide"] = staged["lora"][:, 4 * PASS :].rearrange("p (g t r) -> p g t r", g=4, t=4)
             for t in range(4):
                 nc.scalar.activation(
                     out=staged["la_wide"][:, G, t, :],
@@ -281,15 +278,14 @@ def tile_qlora_down_projection_s8_kernel(
                 )
 
         def la_mix():
-            t = stage("la", "mix", [P, 4 * R * 4], BF16)
             copy_on(
                 "V",
-                t[:].rearrange("p (g r i t) -> p g r t i", g=4, i=4, t=4),
-                staged["la_wide"][:].rearrange("p g t (r i) -> p g r t i", i=4),
+                staged["la"].rearrange("p (g r i t) -> p g r t i", g=4, i=4, t=4),
+                staged["la_wide"].rearrange("p g t (r i) -> p g r t i", i=4),
             )
 
         def la_quant():
-            quantize(la_q, slice(0, 4 * R), staged["la"][:])
+            quantize(la_q, slice(0, 4 * R), staged["la"])
 
         yv = y.rearrange("(g q s) n -> g s q n", q=P, s=4)
         zv = z.rearrange("(g q s) r -> g q (s r)", q=P, s=4)
@@ -302,8 +298,8 @@ def tile_qlora_down_projection_s8_kernel(
             for G in groups:
                 nc.tensor.matmul_mx(
                     out=out[:],
-                    lhsT=hf_q[G, g][0][:, part(P, s)].bitcast(FP8X4),
-                    lhsT_scale=hf_q[G, g][1][:, part(P, s)],
+                    lhsT=hf_q[2 * g + s // 2][0][:, part(P, 2 * G + s % 2)].bitcast(FP8X4),
+                    lhsT_scale=hf_q[2 * g + s // 2][1][:, part(P, 2 * G + s % 2)],
                     rhs=words[G][:, part(1024, half)].bitcast(FP4X4),
                     rhs_scale=down_sc[:, G, part(512, half)],
                     start=(G == 0),
@@ -314,17 +310,18 @@ def tile_qlora_down_projection_s8_kernel(
             out = bank(("z", g, first, last), n, [P, (last - first) * R])
             for s in range(first, last):
                 for G in range(4):
-                    multiply(out[:, part(R, s - first)], hf_q[G, g], part(P, s), la_q, part(R, G), G == 0, G == 3)
+                    multiply(out[:, part(R, s - first)], hf_q[2 * g + s // 2], part(P, 2 * G + s % 2), la_q, part(R, G), G == 0, G == 3)
 
         def da_mul(G, first, last, n):
             out = bank(("da", G, first, last), n, [P, (last - first) * R])
             for a in range(first, last):
                 for g in range(2):
-                    multiply(out[:, part(R, a - first)], hm_q[G, g], part(P, a), dz_q, part(R, g), g == 0, g == 1)
+                    multiply(out[:, part(R, a - first)], hm_q[G], part(P, 4 * g + a), dz_q, part(R, g), g == 0, g == 1)
 
         def put(key, engine):
             t = stage(key, "out", list(banks[key].shape), F32)
             copy_on(engine, t[:], banks[key][:])
+            free.append(number[key])
             if key[0] == "y":
                 dst = yv[key[1], key[2], :, part(512, key[3])]
             else:
@@ -332,11 +329,72 @@ def tile_qlora_down_projection_s8_kernel(
             nc.sync.dma_start(out=dst, in_=t[:])
 
         ctx.enter_context(tc.manual_schedule())
+        free = list(range(8))
 
-        load_x(0)
-        for c in range(2):
-            load_w(0, c)
-        load_x(1)
+        def take():
+            return free.pop(0)
+
+        held = {}
+
+        def x_in(g, s, engine, ring="xt"):
+            n = take()
+            x_turn(g, s, n)
+            x_copy(g, s, engine, ring)
+            free.append(n)
+
+        def first(G, q, u):
+            held[G, q, u] = take()
+            up_pass((G, q // 2), q % 2, u, 0, held[G, q, u])
+
+        def second(G, q, u):
+            if (G, q, u) not in held:
+                first(G, q, u)
+            up_pass((G, q // 2), q % 2, u, 1, held[G, q, u])
+
+        def gated(G, q, u):
+            h_mul((G, q // 2), q % 2, u)
+            free.append(held[G, q, u])
+
+        def turn_pair(b, pair):
+            held[b, pair] = take()
+            h_turn(b, pair, held[b, pair])
+
+        def copy_pair(b, pair, engine="S"):
+            h_copy(b, pair, engine)
+            free.append(held[b, pair])
+
+        def cells(g):
+            return [(2 * g + k % 2, k // 2) for k in range(4)]
+
+
+        def ahead(G, g, u):
+            for pair in range(2):
+                first(G, 2 * g + pair, u)
+
+        def both(G, g, u):
+            for pair in range(2):
+                second(G, 2 * g + pair, u)
+
+        def gate_pair(G, g, u):
+            for pair in range(2):
+                gated(G, 2 * g + pair, u)
+
+        def turn_block(b):
+            for pair in range(2):
+                turn_pair(b, pair)
+                copy_pair(b, pair)
+
+        WIDEN = (1, 2, 4)
+        SMIX = (5, 8)
+        S3 = "S"
+        SMALL = {9: [("da", 0, 0, 4)], 12: [("da", 1, 0, 4)], 14: [("da", 2, 0, 4)]}
+        LAST = ((("da", 3, 0, 4), "V"),(("z", 0, 0, 2), "S"), (("z", 0, 2, 4), "V"), (("z", 1, 0, 2), "S"), (("z", 1, 2, 3), "V"), (("z", 1, 3, 4), "S"))
+        load_x(0, 0)
+        load_x(0, 1)
+        load_w(0, 0)
+        load_w(0, 1)
+        load_x(1, 0)
+        load_x(1, 1)
         load_gate(BLOCKS[0])
         load_w(1, 0)
         for i in range(1, 8):
@@ -348,12 +406,13 @@ def tile_qlora_down_projection_s8_kernel(
         load_dz()
 
         for s in range(4):
-            x_turn(0, s, s)
-            x_copy(0, s, "V" if s == 1 else "S")
+            x_in(0, s, "V" if s == 1 else "S")
             if s == 1:
                 x_quant(0, 0)
+        first_group = quarters("w0")
+        staged["pool"] = quarters(("hm", 1))[3]
         for c in range(2):
-            halves(("w", 0, c))
+            staged["w", 0, c] = first_group[2 * c : 2 * c + 2]
         w_mix(0, 0, 0, "V")
         w_mix(0, 0, 1, "S")
         x_quant(0, 1)
@@ -363,142 +422,122 @@ def tile_qlora_down_projection_s8_kernel(
         w_quant(0, 0, 1)
         for u in range(2):
             w_quant(0, 1, u)
-        warm_up(6)
+        warm_up(6, 3, w_raw[0, 0][:, 0, :])
         for s in range(4):
-            x_turn(1, s, (4, 5, 7, 6)[s])
-            x_copy(1, s, "V" if s == 1 else "S", "xt" if s < 2 else "early")
+            x_in(1, s, "V" if s == 1 else "S", "xt" if s < 2 else "early")
             if s == 1:
                 x_quant(1, 0)
         for i in range(2):
             x_quant(1, 1, i, i + 1)
-
-        def step(i):
-            if i < 2:
-                return [((0, i), k // 2, k % 2) for k in range(4)]
-            return [((i // 2, k // 2), k % 2, i % 2) for k in range(4)]
-
-        def step_up(i, where, ahead):
-            for c in range(2):
-                for k in range(ahead):
-                    up_pass(*step(i)[k], c, where[k])
-            for k in range(ahead, 4):
-                up(*step(i)[k], where[k])
-
-        def step_h(i):
-            for item in step(i):
-                h_mul(*item)
-
-        where = {0: (0, 1, 2, 3), 1: (4, 5, 0, 1), 2: (2, 3, 7, 6)}
-        for i in range(3, 8):
-            where[i] = where[i - 2][2:] + where[i - 2][:2]
-
         w_half(1, 0, 1, "G", "early")
         w_half(1, 0, 0, "S", "half")
         w_half(1, 1, 0, "S", "pool")
-        step_up(0, where[0], 0)
+
+        def step(i):
+            if i < 2:
+                return [(0, 2 * i + k // 2, k % 2) for k in range(4)]
+            return [(i // 2, k, i % 2) for k in range(4)]
+
+        def step_up(i, ahead):
+            for item in step(i)[:ahead]:
+                first(*item)
+            for item in step(i):
+                second(*item)
+
+        def step_h(i):
+            for item in step(i):
+                gated(*item)
+
+        step_up(0, 0)
         step_h(0)
         w_quant(1, 0, 0)
         w_quant(1, 0, 1)
         w_quant(1, 1, 0)
-        for i in range(1, 8):
-            second = ((i + 2) // 2, 1, i % 2)
-            first = ((i + 3) // 2, 0, (i + 1) % 2)
-            if i < 6:
-                w_half(*second, "G", "pool")
-            elif i == 6:
-                half(("hm", BLOCKS[0]), 1, "pool")
-                hm_mix(BLOCKS[0], 1, "G")
-            else:
-                half(("hm", BLOCKS[1]), 0, "mix")
-                staged["hm", BLOCKS[1]][1] = hf_sb[1, 0][:, part(1024, 0)]
-                hm_mix(BLOCKS[1], 1, "G")
-            step_up(i, where[i], 0 if i < 2 else 4 if i == 2 else 2)
+        quarters(("hm", 0))
+        for i in range(1, 6):
+            second_half = ((i + 2) // 2, 1, i % 2)
+            first_half = ((i + 3) // 2, 0, (i + 1) % 2)
+            w_half(*second_half, "G", "pool")
+            step_up(i, 0 if i < 2 else 4 if i == 2 else 2)
             if i >= 2:
-                turn(BLOCKS[i - 2], *where[i - 1][:2])
+                turn_block(BLOCKS[i - 2])
             if i == 1:
-                half(("hm", BLOCKS[0]), 0, "mix")
-                hm_mix(BLOCKS[0], 0, "S")
+                hm_mix(0, 0, 1, "S")
             if i < 5:
-                w_half(*first, "S", "half")
-            if i == 5:
-                halves(("hm", BLOCKS[2]))
-            if i in (5, 6):
-                hm_mix(BLOCKS[2], i - 5, "S")
-            if i == 7:
-                halves(("hm", BLOCKS[3]))
-                hm_mix(BLOCKS[3], 1, "S")
+                w_half(*first_half, "S", "half")
+            else:
+                hm_mix(0, 1, 2, "S")
             step_h(i)
-            if i < 6:
-                w_quant(*second)
+            w_quant(*second_half)
             if i < 5:
-                w_quant(*first)
-            if i == 5:
-                hf_quant((0, 0), 0, 1)
-            if i == 6:
-                hf_quant((1, 0), 0, 1)
-                hf_quant((2, 0), 0, 1)
-
+                w_quant(*first_half)
+            else:
+                hf_quant(0, 0, 2)
         tiles = [("y", g, s, half_n) for g in range(2) for s in range(4) for half_n in range(2)]
-        y_banks = where[6][2:] + where[6][:2]
-        for G in range(2):
-            for i in range(2):
-                y_mul(*tiles[i][1:], [G], y_banks[i])
-        for i in range(2, 4):
-            y_mul(*tiles[i][1:], range(2), y_banks[i])
-        y_mul(*tiles[0][1:], [2])
-        for G in range(3):
-            hf_quant((G, 0), 1, 2)
-        turn(BLOCKS[6], *where[7][:2])
-        turn(BLOCKS[7], *where[7][2:])
-        hf_quant((0, 1))
-        hm_mix(BLOCKS[1], 0, "V")
-        hf_quant((3, 0), 0, 1)
-        hf_quant((3, 0), 1, 2)
-        for i in range(1, 4):
-            y_mul(*tiles[i][1:], [2])
-        turns = list(where[7] + y_banks) * 3
-        y_mul(*tiles[4][1:], range(3), turns.pop(0))
+        hm_mix(1, 3, 4, "G")
+        step_up(6, 2)
+        turn_block(BLOCKS[4])
+        hm_mix(0, 2, 3, "S")
+        gate_pair(3, 0, 0)
+        ahead(3, 0, 1)
+        both(3, 0, 1)
+        for i in range(2):
+            y_mul(*tiles[i][1:], (0, 1), take())
+        gate_pair(3, 0, 1)
+        turn_block(BLOCKS[5])
+        hf_quant(0, 2, 3)
+        for pair in range(2):
+            turn_pair(BLOCKS[6], pair)
+        copy_pair(BLOCKS[6], 0, "V")
+        copy_pair(BLOCKS[6], 1)
+        hf_quant(1, 0, 2)
+        hf_quant(0, 3, 4)
+        staged["hm", 2] = gate_row[0][:]
+        hm_mix(2, 3, 4, "G")
+        la_widen(0)
+        for i in range(2):
+            y_mul(*tiles[i][1:], (2,))
+        both(3, 1, 1)
+        gate_pair(3, 1, 0)
+        gate_pair(3, 1, 1)
+        hf_quant(1, 2, 4)
+
+        def small(key, engine):
+            (z_mul if key[0] == "z" else da_mul)(*key[1:], take())
+            put(key, engine)
 
         for i in range(16):
-            if i < 5:
+            if i < 2:
                 y_mul(*tiles[i][1:], [3])
             else:
-                y_mul(*tiles[i][1:], range(4), turns.pop(0))
+                y_mul(*tiles[i][1:], range(4), take())
             put(tiles[i], "S")
-            if i == 0:
-                for G in range(1, 4):
-                    hf_quant((G, 1))
+            if i == 3:
+                turn_block(BLOCKS[7])
+                hm_mix(0, 3, 4, "V")
                 dz_mix()
-            if i < 4:
-                la_widen(i)
-            if i == 3:
-                for b in BLOCKS[:3]:
-                    hm_quant(b)
+                hm_quant(0)
                 dz_quant()
-            if i == 3:
-                hm_mix(BLOCKS[3], 0, "V")
-            if 4 <= i < 8:
-                halves(("hm", BLOCKS[i]))
-                hm_mix(BLOCKS[i], 0, "V")
-                hm_mix(BLOCKS[i], 1, "S" if i == 7 else "V")
-            if 4 <= i < 9:
-                hm_quant(BLOCKS[i - 1])
-            if i == 5:
+                hf_quant(2, 0, 4)
+                hm_mix(1, 0, 2, "V")
+                hf_quant(3, 0, 4)
+                hm_mix(1, 2, 3, "V")
+                hm_mix(2, 0, 2, "V")
+                hm_quant(1)
+                staged["hm", 3] = gate_row[1][:]
+            if i in WIDEN:
+                la_widen(1 + WIDEN.index(i))
+            if i == SMIX[0]:
+                hm_mix(2, 2, 3, "S")
+                hm_mix(3, 0, 2, "V")
+                hm_quant(2)
+            if i == SMIX[1]:
+                hm_mix(3, 3, 4, "S")
+                hm_mix(3, 2, 3, S3)
                 la_mix()
-            if i == 6:
+                hm_quant(3)
                 la_quant()
-            if i in DA_AFTER:
-                da_mul(DA_AFTER.index(i), 0, 4, turns.pop(0))
-                put(("da", DA_AFTER.index(i), 0, 4), "S")
-
-        for key, engine in (
-            (("z", 0, 0, 2), "S"),
-            (("z", 0, 2, 4), "S"),
-            (("z", 1, 0, 2), "S"),
-            (("da", 3, 0, 2), "V"),
-            (("da", 3, 2, 4), "S"),
-            (("z", 1, 2, 3), "V"),
-            (("z", 1, 3, 4), "S"),
-        ):
-            (z_mul if key[0] == "z" else da_mul)(*key[1:], turns.pop(0))
-            put(key, engine)
+            for key in SMALL.get(i, ()):
+                small(key, "S")
+        for key, engine in LAST:
+            small(key, engine)

@@ -238,18 +238,13 @@ def tile_qlora_down_projection_s8_kernel(
                 pool_copy(
                     out.rearrange("p (e n s) -> p e n s", e=2, s=4), in_.rearrange("p (s n e) -> p e n s", s=4, e=2)
                 )
-            elif last - first == 1:
-                copy_on(
-                    engine,
-                    out.rearrange("p (e n i s) -> p n s i e", e=2, i=2, s=4),
-                    in_.rearrange("p (s n i e) -> p n s i e", s=4, i=2, e=2),
-                )
             else:
-                copy_on(
-                    engine,
-                    out.rearrange("p (m e n s) -> p m e n s", e=2, n=P, s=4),
-                    in_.rearrange("p (m s n e) -> p m e n s", s=4, n=P, e=2),
-                )
+                for m in range(last - first):
+                    copy_on(
+                        engine,
+                        out[:, part(1024, m)].rearrange("p (e n i s) -> p n s i e", e=2, i=2, s=4),
+                        in_[:, part(1024, m)].rearrange("p (s n i e) -> p n s i e", s=4, i=2, e=2),
+                    )
 
         def hm_quant(G, first=0, last=4):
             quantize(hm_q[G], slice(256 * first, 256 * last), staged["hm", G][:, 1024 * first : 1024 * last])
@@ -384,11 +379,12 @@ def tile_qlora_down_projection_s8_kernel(
                 turn_pair(b, pair)
                 copy_pair(b, pair)
 
-        WIDEN = (1, 2, 4)
-        SMIX = (5, 8)
-        S3 = "S"
-        SMALL = {9: [("da", 0, 0, 4)], 12: [("da", 1, 0, 4)], 14: [("da", 2, 0, 4)]}
-        LAST = ((("da", 3, 0, 4), "V"),(("z", 0, 0, 2), "S"), (("z", 0, 2, 4), "V"), (("z", 1, 0, 2), "S"), (("z", 1, 2, 3), "V"), (("z", 1, 3, 4), "S"))
+        CP = "S"
+        WIDEN = (6, 7)
+        SMIX = (8, 10)
+        S3 = "V"
+        SMALL = {7: [("da", 0, 0, 4)], 11: [("da", 1, 0, 4)], 13: [("da", 2, 0, 4)], 15: [("da", 3, 0, 4)]}
+        LAST = ((("z", 0, 0, 2), "V"), (("z", 0, 2, 4), "S"), (("z", 1, 0, 2), "V"), (("z", 1, 2, 3), "S"), (("z", 1, 3, 4), "V"))
         load_x(0, 0)
         load_x(0, 1)
         load_w(0, 0)
@@ -422,9 +418,11 @@ def tile_qlora_down_projection_s8_kernel(
         w_quant(0, 0, 1)
         for u in range(2):
             w_quant(0, 1, u)
-        warm_up(6, 3, w_raw[0, 0][:, 0, :])
+        warm_up(free[0], 3, w_raw[0, 0][:, 0, :])
         for s in range(4):
             x_in(1, s, "V" if s == 1 else "S", "xt" if s < 2 else "early")
+            if s == 0:
+                ahead(0, 0, 0)
             if s == 1:
                 x_quant(1, 0)
         for i in range(2):
@@ -448,85 +446,106 @@ def tile_qlora_down_projection_s8_kernel(
             for item in step(i):
                 gated(*item)
 
+        tiles = [("y", g, s, half_n) for g in range(2) for s in range(4) for half_n in range(2)]
         step_up(0, 0)
+        step_up(1, 0)
         step_h(0)
         w_quant(1, 0, 0)
         w_quant(1, 0, 1)
         w_quant(1, 1, 0)
         quarters(("hm", 0))
-        for i in range(1, 6):
-            second_half = ((i + 2) // 2, 1, i % 2)
-            first_half = ((i + 3) // 2, 0, (i + 1) % 2)
-            w_half(*second_half, "G", "pool")
-            step_up(i, 0 if i < 2 else 4 if i == 2 else 2)
-            if i >= 2:
-                turn_block(BLOCKS[i - 2])
-            if i == 1:
+        w_half(1, 1, 1, "G", "pool")
+        turn_block((0, 0))
+        w_half(2, 0, 0, "S", "half")
+        step_h(1)
+        w_quant(1, 1, 1)
+        w_quant(2, 0, 0)
+        for G in range(1, 4):
+            if G < 3:
+                w_half(G + 1, 1, 0, "G", "pool")
+            else:
+                hm_mix(1, 3, 4, "G")
+                hm_mix(0, 3, 4, "G")
+            ahead(G, 0, 0)
+            both(G, 0, 0)
+            both(G, 1, 0)
+            turn_block((G - 1, 1))
+            if G < 3:
+                w_half(G + 1, 0, 1, "S", "half")
+            else:
+                hm_mix(0, 2, 3, "S")
                 hm_mix(0, 0, 1, "S")
-            if i < 5:
-                w_half(*first_half, "S", "half")
+                for k in range(2):
+                    la_widen(k)
+            gate_pair(G, 0, 0)
+            ahead(G, 0, 1)
+            both(G, 0, 1)
+            both(G, 1, 1)
+            if G == 3:
+                break
+            gate_pair(G, 0, 1)
+            w_quant(G + 1, 1, 0)
+            w_half(G + 1, 1, 1, "G", "pool")
+            w_quant(G + 1, 0, 1)
+            for pair in range(2):
+                turn_pair((G, 0), pair)
+            gate_pair(G, 1, 0)
+            for pair in range(2):
+                copy_pair((G, 0), pair)
+            if G < 2:
+                w_half(G + 2, 0, 0, "S", "half")
             else:
                 hm_mix(0, 1, 2, "S")
-            step_h(i)
-            w_quant(*second_half)
-            if i < 5:
-                w_quant(*first_half)
+            gate_pair(G, 1, 1)
+            if G == 2:
+                hf_quant(0, 2, 3)
+            w_quant(G + 1, 1, 1)
+            if G < 2:
+                w_quant(G + 2, 0, 0)
             else:
                 hf_quant(0, 0, 2)
-        tiles = [("y", g, s, half_n) for g in range(2) for s in range(4) for half_n in range(2)]
-        hm_mix(1, 3, 4, "G")
-        step_up(6, 2)
-        turn_block(BLOCKS[4])
-        hm_mix(0, 2, 3, "S")
-        gate_pair(3, 0, 0)
-        ahead(3, 0, 1)
-        both(3, 0, 1)
         for i in range(2):
-            y_mul(*tiles[i][1:], (0, 1), take())
+            y_mul(*tiles[i][1:], range(3), take())
         gate_pair(3, 0, 1)
-        turn_block(BLOCKS[5])
-        hf_quant(0, 2, 3)
-        for pair in range(2):
-            turn_pair(BLOCKS[6], pair)
-        copy_pair(BLOCKS[6], 0, "V")
-        copy_pair(BLOCKS[6], 1)
-        hf_quant(1, 0, 2)
-        hf_quant(0, 3, 4)
-        staged["hm", 2] = gate_row[0][:]
-        hm_mix(2, 3, 4, "G")
-        la_widen(0)
-        for i in range(2):
-            y_mul(*tiles[i][1:], (2,))
-        both(3, 1, 1)
+        for i in range(2, 4):
+            y_mul(*tiles[i][1:], range(2), take())
         gate_pair(3, 1, 0)
         gate_pair(3, 1, 1)
-        hf_quant(1, 2, 4)
+        turn_block((3, 0))
+        turn_block((3, 1))
+        hf_quant(1, 0, 2)
+        hf_quant(1, 2, 3)
+        for i in range(2, 4):
+            y_mul(*tiles[i][1:], range(2, 3))
+        y_mul(*tiles[4][1:], range(3), take())
+        hm_quant(0)
+        hf_quant(0, 3, 4)
+        dz_mix()
+        hf_quant(1, 3, 4)
 
         def small(key, engine):
             (z_mul if key[0] == "z" else da_mul)(*key[1:], take())
             put(key, engine)
 
         for i in range(16):
-            if i < 2:
+            if i < 5:
                 y_mul(*tiles[i][1:], [3])
             else:
                 y_mul(*tiles[i][1:], range(4), take())
             put(tiles[i], "S")
-            if i == 3:
-                turn_block(BLOCKS[7])
-                hm_mix(0, 3, 4, "V")
-                dz_mix()
-                hm_quant(0)
+            if i == 0:
                 dz_quant()
-                hf_quant(2, 0, 4)
                 hm_mix(1, 0, 2, "V")
-                hf_quant(3, 0, 4)
+                hf_quant(2, 0, 4)
                 hm_mix(1, 2, 3, "V")
+                hf_quant(3, 0, 4)
+                staged["hm", 2] = gate_row[0][:]
                 hm_mix(2, 0, 2, "V")
                 hm_quant(1)
+                hm_mix(2, 3, 4, "V")
                 staged["hm", 3] = gate_row[1][:]
             if i in WIDEN:
-                la_widen(1 + WIDEN.index(i))
+                la_widen(2 + WIDEN.index(i))
             if i == SMIX[0]:
                 hm_mix(2, 2, 3, "S")
                 hm_mix(3, 0, 2, "V")

@@ -20,7 +20,7 @@ COPY = mybir.ActivationFunctionType.Copy
 P = 128
 PASS = 512
 BLOCKS = [(G, g) for G in range(4) for g in range(2)]
-RINGS = {"xt": 2, "mix": 3, "early": 1, "half": 2, "out": 10}
+RINGS = {"xt": 2, "mix": 3, "early": 1, "out": 10}
 
 
 def tile_qlora_down_projection_s8_kernel(
@@ -90,8 +90,8 @@ def tile_qlora_down_projection_s8_kernel(
         def load_w(G, c):
             nc.sync.dma_start(out=w_raw[G, c], in_=wv[c, :, :, part(PASS, G)])
 
-        def load_gate(b):
-            for pair in range(2):
+        def load_gate(b, pairs=(0, 1)):
+            for pair in pairs:
                 nc.sync.dma_start(
                     out=gate_sb[b[0], 2 * b[1] + pair].rearrange("p (s f) -> p s f", s=2),
                     in_=gv[b[1], :, part(2, pair), part(PASS, b[0])],
@@ -163,9 +163,10 @@ def tile_qlora_down_projection_s8_kernel(
             whole = stage(key, "mix", [P, 8 * PASS], BF16)
             return [whole[:, part(1024, m)] for m in range(4)]
 
-        def half(key, u, ring):
-            where = staged["pool"] if ring == "pool" else stage((key, u), ring, [P, 2 * PASS], BF16)[:]
-            staged.setdefault(key, [None, None])[u] = where
+        def half(key, u, place):
+            staged.setdefault(key, [None, None])[u] = (
+                stage((key, u), place, [P, 2 * PASS], BF16)[:] if place == "early" else staged[place]
+            )
 
         def pool_copy(out, in_):
             nc.gpsimd.tensor_scalar(out=out, in0=in_, scalar1=1.0, scalar2=0.0, op0=ALU.mult, op1=ALU.add)
@@ -245,6 +246,13 @@ def tile_qlora_down_projection_s8_kernel(
                         out[:, part(1024, m)].rearrange("p (e n i s) -> p n s i e", e=2, i=2, s=4),
                         in_[:, part(1024, m)].rearrange("p (s n i e) -> p n s i e", s=4, i=2, e=2),
                     )
+
+        def hm_piece(G, m, k):
+            copy_on(
+                "S",
+                staged["hm", G][:, part(1024, m)].rearrange("p (e n i s) -> p n s i e", e=2, i=2, s=4)[:, part(32, k)],
+                h_all[G][:, part(1024, m)].rearrange("p (s n i e) -> p n s i e", s=4, i=2, e=2)[:, part(32, k)],
+            )
 
         def hm_quant(G, first=0, last=4):
             quantize(hm_q[G], slice(256 * first, 256 * last), staged["hm", G][:, 1024 * first : 1024 * last])
@@ -383,7 +391,7 @@ def tile_qlora_down_projection_s8_kernel(
         WIDEN = (6, 7)
         SMIX = (8, 10)
         S3 = "V"
-        SMALL = {7: [("da", 0, 0, 4)], 11: [("da", 1, 0, 4)], 13: [("da", 2, 0, 4)], 15: [("da", 3, 0, 4)]}
+        SMALL = {7: [("da", 0, 0, 4)], 10: [("da", 1, 0, 4)], 13: [("da", 2, 0, 4)], 15: [("da", 3, 0, 4)]}
         LAST = ((("z", 0, 0, 2), "V"), (("z", 0, 2, 4), "S"), (("z", 1, 0, 2), "V"), (("z", 1, 2, 3), "S"), (("z", 1, 3, 4), "V"))
         load_x(0, 0)
         load_x(0, 1)
@@ -391,12 +399,22 @@ def tile_qlora_down_projection_s8_kernel(
         load_w(0, 1)
         load_x(1, 0)
         load_x(1, 1)
-        load_gate(BLOCKS[0])
+        load_gate((0, 0))
         load_w(1, 0)
-        for i in range(1, 8):
-            if i < 6:
-                load_w((i + 2) // 2, i % 2)
-            load_gate(BLOCKS[i])
+        load_w(1, 1)
+        load_gate((0, 1))
+        load_w(2, 0)
+        load_gate((1, 0), (0,))
+        load_w(2, 1)
+        load_gate((1, 0), (1,))
+        load_gate((1, 1))
+        load_w(3, 0)
+        load_gate((2, 0), (0,))
+        load_w(3, 1)
+        load_gate((2, 0), (1,))
+        load_gate((2, 1))
+        load_gate((3, 0))
+        load_gate((3, 1))
         load_down()
         load_lora()
         load_dz()
@@ -406,7 +424,9 @@ def tile_qlora_down_projection_s8_kernel(
             if s == 1:
                 x_quant(0, 0)
         first_group = quarters("w0")
-        staged["pool"] = quarters(("hm", 1))[3]
+        staged["Y"] = quarters(("hm", 1))[3]
+        for name in "XZ":
+            staged[name] = kept(name, [P, 2 * PASS], BF16)[:]
         for c in range(2):
             staged["w", 0, c] = first_group[2 * c : 2 * c + 2]
         w_mix(0, 0, 0, "V")
@@ -428,8 +448,8 @@ def tile_qlora_down_projection_s8_kernel(
         for i in range(2):
             x_quant(1, 1, i, i + 1)
         w_half(1, 0, 1, "G", "early")
-        w_half(1, 0, 0, "S", "half")
-        w_half(1, 1, 0, "S", "pool")
+        w_half(1, 0, 0, "S", "Z")
+        w_half(1, 1, 0, "S", "X")
 
         def step(i):
             if i < 2:
@@ -454,27 +474,31 @@ def tile_qlora_down_projection_s8_kernel(
         w_quant(1, 0, 1)
         w_quant(1, 1, 0)
         quarters(("hm", 0))
-        w_half(1, 1, 1, "G", "pool")
+        w_half(1, 1, 1, "G", "X")
         turn_block((0, 0))
-        w_half(2, 0, 0, "S", "half")
+        w_half(2, 0, 0, "S", "Y")
+        hm_piece(0, 0, 0)
+        pass
         step_h(1)
         w_quant(1, 1, 1)
         w_quant(2, 0, 0)
         for G in range(1, 4):
+            place = "Y"
             if G < 3:
-                w_half(G + 1, 1, 0, "G", "pool")
+                w_half(G + 1, 1, 0, "G", place)
             else:
                 hm_mix(1, 3, 4, "G")
                 hm_mix(0, 3, 4, "G")
-            ahead(G, 0, 0)
+            if G == 1 or not False:
+                ahead(G, 0, 0)
             both(G, 0, 0)
             both(G, 1, 0)
             turn_block((G - 1, 1))
             if G < 3:
-                w_half(G + 1, 0, 1, "S", "half")
+                w_half(G + 1, 0, 1, "S", "Z")
+                hm_piece(0, G - 1, 1)
             else:
-                hm_mix(0, 2, 3, "S")
-                hm_mix(0, 0, 1, "S")
+                hm_mix(1, 0, 2, "S")
                 for k in range(2):
                     la_widen(k)
             gate_pair(G, 0, 0)
@@ -483,9 +507,11 @@ def tile_qlora_down_projection_s8_kernel(
             both(G, 1, 1)
             if G == 3:
                 break
+            if False:
+                ahead(G + 1, 0, 0)
             gate_pair(G, 0, 1)
             w_quant(G + 1, 1, 0)
-            w_half(G + 1, 1, 1, "G", "pool")
+            w_half(G + 1, 1, 1, "G", place)
             w_quant(G + 1, 0, 1)
             for pair in range(2):
                 turn_pair((G, 0), pair)
@@ -493,9 +519,11 @@ def tile_qlora_down_projection_s8_kernel(
             for pair in range(2):
                 copy_pair((G, 0), pair)
             if G < 2:
-                w_half(G + 2, 0, 0, "S", "half")
+                w_half(G + 2, 0, 0, "S", "X")
+                hm_piece(0, 1, 0)
+                pass
             else:
-                hm_mix(0, 1, 2, "S")
+                hm_mix(0, 2, 3, "S")
             gate_pair(G, 1, 1)
             if G == 2:
                 hf_quant(0, 2, 3)
@@ -518,10 +546,11 @@ def tile_qlora_down_projection_s8_kernel(
         for i in range(2, 4):
             y_mul(*tiles[i][1:], range(2, 3))
         y_mul(*tiles[4][1:], range(3), take())
-        hm_quant(0)
+        hm_quant(0, 0, 2)
         hf_quant(0, 3, 4)
-        dz_mix()
+        hm_quant(0, 2, 4)
         hf_quant(1, 3, 4)
+        dz_mix()
 
         def small(key, engine):
             (z_mul if key[0] == "z" else da_mul)(*key[1:], take())
@@ -534,14 +563,14 @@ def tile_qlora_down_projection_s8_kernel(
                 y_mul(*tiles[i][1:], range(4), take())
             put(tiles[i], "S")
             if i == 0:
-                dz_quant()
-                hm_mix(1, 0, 2, "V")
-                hf_quant(2, 0, 4)
                 hm_mix(1, 2, 3, "V")
-                hf_quant(3, 0, 4)
+                dz_quant()
                 staged["hm", 2] = gate_row[0][:]
-                hm_mix(2, 0, 2, "V")
+                hm_mix(2, 0, 1, "V")
+                hf_quant(2, 0, 4)
                 hm_quant(1)
+                hf_quant(3, 0, 4)
+                hm_mix(2, 1, 2, "V")
                 hm_mix(2, 3, 4, "V")
                 staged["hm", 3] = gate_row[1][:]
             if i in WIDEN:

@@ -396,22 +396,21 @@ def tile_qlora_down_projection_s8_kernel(
         load_x(0, 0)
         load_x(0, 1)
         load_w(0, 0)
-        load_w(0, 1)
         load_x(1, 0)
+        load_w(0, 1)
         load_x(1, 1)
         load_gate((0, 0))
         load_w(1, 0)
         load_w(1, 1)
-        load_gate((0, 1))
+        load_gate((0, 1), (0,))
         load_w(2, 0)
-        load_gate((1, 0), (0,))
+        load_gate((0, 1), (1,))
+        load_gate((1, 0))
         load_w(2, 1)
-        load_gate((1, 0), (1,))
         load_gate((1, 1))
         load_w(3, 0)
-        load_gate((2, 0), (0,))
+        load_gate((2, 0))
         load_w(3, 1)
-        load_gate((2, 0), (1,))
         load_gate((2, 1))
         load_gate((3, 0))
         load_gate((3, 1))
@@ -419,32 +418,34 @@ def tile_qlora_down_projection_s8_kernel(
         load_lora()
         load_dz()
 
-        for s in range(4):
-            x_in(0, s, "V" if s == 1 else "S")
-            if s == 1:
-                x_quant(0, 0)
         first_group = quarters("w0")
         staged["Y"] = quarters(("hm", 1))[3]
         for name in "XZ":
             staged[name] = kept(name, [P, 2 * PASS], BF16)[:]
         for c in range(2):
             staged["w", 0, c] = first_group[2 * c : 2 * c + 2]
+        for s in range(4):
+            x_in(0, s, "V" if s == 1 else "S")
+            if s == 1:
+                x_quant(0, 0)
         w_mix(0, 0, 0, "V")
         w_mix(0, 0, 1, "S")
         x_quant(0, 1)
         w_quant(0, 0, 0)
+        pass
+        x_in(1, 0, "V")
+        x_in(1, 1, "S")
+        warm_up(free[0], 2, w_raw[0, 0][:, 0, :])
+        w_quant(0, 0, 1)
         w_mix(0, 1, 0, "V")
         w_mix(0, 1, 1, "S")
-        w_quant(0, 0, 1)
-        for u in range(2):
-            w_quant(0, 1, u)
-        warm_up(free[0], 3, w_raw[0, 0][:, 0, :])
-        for s in range(4):
-            x_in(1, s, "V" if s == 1 else "S", "xt" if s < 2 else "early")
-            if s == 0:
-                ahead(0, 0, 0)
-            if s == 1:
-                x_quant(1, 0)
+        ahead(0, 0, 0)
+        x_quant(1, 0)
+        w_quant(0, 1, 0)
+        x_in(1, 2, "S", "early")
+        pass
+        x_in(1, 3, "S", "early")
+        w_quant(0, 1, 1)
         for i in range(2):
             x_quant(1, 1, i, i + 1)
         w_half(1, 0, 1, "G", "early")
@@ -474,45 +475,53 @@ def tile_qlora_down_projection_s8_kernel(
         w_quant(1, 0, 1)
         w_quant(1, 1, 0)
         quarters(("hm", 0))
-        w_half(1, 1, 1, "G", "X")
+        w_half(2, 0, 0, "G", "X")
         turn_block((0, 0))
-        w_half(2, 0, 0, "S", "Y")
+        w_half(1, 1, 1, "S", "Y")
         hm_piece(0, 0, 0)
-        pass
         step_h(1)
         w_quant(1, 1, 1)
-        w_quant(2, 0, 0)
         for G in range(1, 4):
-            place = "Y"
             if G < 3:
-                w_half(G + 1, 1, 0, "G", place)
+                w_half(G + 1, 0, 1, "G", "Y")
             else:
                 hm_mix(1, 3, 4, "G")
                 hm_mix(0, 3, 4, "G")
-            if G == 1 or not False:
-                ahead(G, 0, 0)
+            ahead(G, 0, 0)
             both(G, 0, 0)
             both(G, 1, 0)
-            turn_block((G - 1, 1))
+            if G == 1:
+                ahead(G, 0, 1)
+            for pair in range(2):
+                turn_pair((G - 1, 1), pair)
             if G < 3:
-                w_half(G + 1, 0, 1, "S", "Z")
-                hm_piece(0, G - 1, 1)
+                gated(G, 0, 0)
+            copy_pair((G - 1, 1), 0)
+            if G == 3:
+                copy_pair((G - 1, 1), 1)
+                gated(G, 0, 0)
+            if G < 3:
+                w_half(G + 1, 1, 0, "S", "Z")
             else:
-                hm_mix(1, 0, 2, "S")
+                hm_mix(0, 1, 2, "S")
+                hm_mix(1, 0, 1, "S")
                 for k in range(2):
                     la_widen(k)
-            gate_pair(G, 0, 0)
-            ahead(G, 0, 1)
+            gated(G, 1, 0)
+            if not (G == 1):
+                ahead(G, 0, 1)
             both(G, 0, 1)
             both(G, 1, 1)
             if G == 3:
                 break
-            if False:
-                ahead(G + 1, 0, 0)
             gate_pair(G, 0, 1)
+            if not False:
+                copy_pair((G - 1, 1), 1)
+            if G == 1:
+                w_quant(2, 0, 0)
             w_quant(G + 1, 1, 0)
-            w_half(G + 1, 1, 1, "G", place)
             w_quant(G + 1, 0, 1)
+            w_half(G + 1, 1, 1, "G", "Y")
             for pair in range(2):
                 turn_pair((G, 0), pair)
             gate_pair(G, 1, 0)
@@ -520,17 +529,16 @@ def tile_qlora_down_projection_s8_kernel(
                 copy_pair((G, 0), pair)
             if G < 2:
                 w_half(G + 2, 0, 0, "S", "X")
-                hm_piece(0, 1, 0)
-                pass
+                hm_piece(0, 0, 1)
             else:
                 hm_mix(0, 2, 3, "S")
             gate_pair(G, 1, 1)
             if G == 2:
                 hf_quant(0, 2, 3)
-            w_quant(G + 1, 1, 1)
-            if G < 2:
-                w_quant(G + 2, 0, 0)
             else:
+                w_quant(G + 2, 0, 0)
+            w_quant(G + 1, 1, 1)
+            if G == 2:
                 hf_quant(0, 0, 2)
         for i in range(2):
             y_mul(*tiles[i][1:], range(3), take())
@@ -563,7 +571,7 @@ def tile_qlora_down_projection_s8_kernel(
                 y_mul(*tiles[i][1:], range(4), take())
             put(tiles[i], "S")
             if i == 0:
-                hm_mix(1, 2, 3, "V")
+                hm_mix(1, 1, 3, "V")
                 dz_quant()
                 staged["hm", 2] = gate_row[0][:]
                 hm_mix(2, 0, 1, "V")

@@ -396,8 +396,8 @@ def tile_qlora_down_projection_s8_kernel(
         load_x(0, 0)
         load_x(0, 1)
         load_w(0, 0)
-        load_x(1, 0)
         load_w(0, 1)
+        load_x(1, 0)
         load_x(1, 1)
         load_gate((0, 0))
         load_w(1, 0)
@@ -418,34 +418,32 @@ def tile_qlora_down_projection_s8_kernel(
         load_lora()
         load_dz()
 
+        for s in range(4):
+            x_in(0, s, "V" if s == 1 else "S")
+            if s == 1:
+                x_quant(0, 0)
         first_group = quarters("w0")
         staged["Y"] = quarters(("hm", 1))[3]
         for name in "XZ":
             staged[name] = kept(name, [P, 2 * PASS], BF16)[:]
         for c in range(2):
             staged["w", 0, c] = first_group[2 * c : 2 * c + 2]
-        for s in range(4):
-            x_in(0, s, "V" if s == 1 else "S")
-            if s == 1:
-                x_quant(0, 0)
         w_mix(0, 0, 0, "V")
         w_mix(0, 0, 1, "S")
         x_quant(0, 1)
         w_quant(0, 0, 0)
-        pass
-        x_in(1, 0, "V")
-        x_in(1, 1, "S")
-        warm_up(free[0], 2, w_raw[0, 0][:, 0, :])
-        w_quant(0, 0, 1)
         w_mix(0, 1, 0, "V")
         w_mix(0, 1, 1, "S")
-        ahead(0, 0, 0)
-        x_quant(1, 0)
-        w_quant(0, 1, 0)
-        x_in(1, 2, "S", "early")
-        pass
-        x_in(1, 3, "S", "early")
-        w_quant(0, 1, 1)
+        w_quant(0, 0, 1)
+        for u in range(2):
+            w_quant(0, 1, u)
+        warm_up(free[0], 3, w_raw[0, 0][:, 0, :])
+        for s in range(4):
+            x_in(1, s, "V" if s == 1 else "S", "xt" if s < 2 else "early")
+            if s == 0:
+                ahead(0, 0, 0)
+            if s == 1:
+                x_quant(1, 0)
         for i in range(2):
             x_quant(1, 1, i, i + 1)
         w_half(1, 0, 1, "G", "early")

@@ -135,11 +135,6 @@ def tile_qlora_down_projection_s8_kernel(
             staged[key] = work.tile(shape, dtype, name=ring, bufs=RINGS[ring], align_bytes=64)
             return staged[key]
 
-        def warm_up(n, count, src):
-            out = bank("warm", n, [P, PASS])
-            for i in range(count):
-                nc.tensor.matmul(out[:], lhsT=src[:, :P], rhs=src[:, :PASS], start=True, stop=True)
-
         def x_turn(g, s, n):
             out = bank(("x", g, s), n, [P, 2, 2, P])
             xw = x_tile[g, s].bitcast(F32)
@@ -437,7 +432,6 @@ def tile_qlora_down_projection_s8_kernel(
         w_quant(0, 0, 1)
         for u in range(2):
             w_quant(0, 1, u)
-        warm_up(free[0], 3, w_raw[0, 0][:, 0, :])
         for s in range(4):
             x_in(1, s, "V" if s == 1 else "S", "xt" if s < 2 else "early")
             if s == 0:

from contextlib import ExitStack

import concourse.mybir as mybir
from concourse.masks import make_identity

M, K, F, N, R = 1024, 1024, 2048, 1024, 128
FLOPS = 2 * M * K * F + 2 * M * F * N + 4 * M * F * R

F32 = mybir.dt.float32
BF16 = mybir.dt.bfloat16
I32 = mybir.dt.int32
U32 = mybir.dt.uint32
U8 = mybir.dt.uint8
FP8 = mybir.dt.float8_e4m3fn
FP8X4 = mybir.dt.float8_e4m3fn_x4
FP4X4 = mybir.dt.float4_e2m1fn_x4
ALU = mybir.AluOpType
COPY = mybir.ActivationFunctionType.Copy

P = 128
PASS = 512
BLOCKS = [(G, g) for G in range(4) for g in range(2)]
RINGS = {"xt": 2, "mix": 3, "early": 1, "out": 10}


def tile_qlora_down_projection_s8_kernel(
    tc, x, w_up, gate, down_words, down_scales, lora_a_bytes, lora_a_scale, dz, y, z, da
):
    nc = tc.nc
    with ExitStack() as ctx:
        keep = ctx.enter_context(tc.tile_pool(name="keep", bufs=1))
        work = ctx.enter_context(tc.tile_pool(name="work", bufs=2))
        psum = ctx.enter_context(tc.psum_pool(name="psum", bufs=2))

        def kept(name, shape, dtype):
            return keep.tile(shape, dtype, name=name, align_bytes=64)

        def operand(name, columns):
            return kept(name + "c", [P, columns], U32), kept(name + "s", [P, columns], U8)

        def quantize(op, cols, src):
            nc.vector.quantize_mx(out=op[0][:, cols].bitcast(FP8X4), scales=op[1][:, cols], in_=src)

        def multiply(out, lhs, lhs_cols, rhs, rhs_cols, first, last):
            nc.tensor.matmul_mx(
                out=out,
                lhsT=lhs[0][:, lhs_cols].bitcast(FP8X4),
                lhsT_scale=lhs[1][:, lhs_cols],
                rhs=rhs[0][:, rhs_cols].bitcast(FP8X4),
                rhs_scale=rhs[1][:, rhs_cols],
                start=first,
                stop=last,
            )

        def copy_on(engine, out, in_):
            if engine == "V":
                nc.vector.tensor_copy(out=out, in_=in_)
            else:
                nc.scalar.copy(out=out, in_=in_)

        def part(width, index):
            return slice(width * index, width * (index + 1))

        ident = kept("ident", [P, P], F32)
        make_identity(nc, ident[:])
        down_sc = kept("down_sc", [P, 4, N], U8)
        nc.gpsimd.memset(down_sc[:].rearrange("p g n -> p (g n)").bitcast(I32), 0)

        x_raw = kept("x_raw", [P, 8 * K], BF16)
        x_tile = {(g, s): x_raw[:, part(K, 4 * g + s)] for g in range(2) for s in range(4)}
        w_both = [kept("w_raw%d" % G, [P, 8 * PASS], BF16) for G in range(4)]
        w_raw = {
            (G, c): w_both[G][:, part(4 * PASS, c)].rearrange("p (j f) -> p j f", j=4) for G in range(4) for c in range(2)
        }
        gate_row = [kept("gate%d" % q, [P, 8 * PASS], BF16) for q in range(4)]
        gate_sb = {(G, q): gate_row[q][:, part(2 * PASS, G)] for G in range(4) for q in range(4)}
        words = [kept("words%d" % G, [P, 2 * N], U8) for G in range(4)]
        lbytes = kept("lbytes", [P, 4, 4 * R], U8)
        lscale = kept("lscale", [P, 16], F32)
        dz_raw = kept("dz_raw", [P, 2, 4, R], BF16)

        xv = x.rearrange("(g p s) k -> g p s k", p=P, s=4)
        wv = w_up.rearrange("(c p j) f -> c p j f", p=P, j=4)
        gv = gate.rearrange("(g p s) f -> g p s f", p=P, s=4)

        def load_x(g, pair):
            for s in range(2 * pair, 2 * pair + 2):
                nc.sync.dma_start(out=x_tile[g, s], in_=xv[g, :, s, :])

        def load_w(G, c):
            nc.sync.dma_start(out=w_raw[G, c], in_=wv[c, :, :, part(PASS, G)])

        def load_gate(b, pairs=(0, 1)):
            for pair in pairs:
                nc.sync.dma_start(
                    out=gate_sb[b[0], 2 * b[1] + pair].rearrange("p (s f) -> p s f", s=2),
                    in_=gv[b[1], :, part(2, pair), part(PASS, b[0])],
                )

        def load_dz():
            nc.sync.dma_start(out=dz_raw[:], in_=dz.rearrange("(g p t) r -> p g t r", p=P, t=4))

        def load_down():
            for r in range(4):
                nc.sync.dma_start(
                    out=down_sc[r:P:32].bitcast(I32),
                    in_=down_scales[:, r:16:4, :].bitcast(I32).rearrange("g q w -> q g w"),
                )
            for G in range(4):
                nc.sync.dma_start(out=words[G][:], in_=down_words[G])

        def load_lora():
            nc.sync.dma_start(out=lbytes[:], in_=lora_a_bytes.rearrange("(g p t) r -> p g (t r)", p=P, t=4))
            nc.sync.dma_start(
                out=lscale[:].rearrange("p (g t) -> p g t", t=4),
                in_=lora_a_scale.rearrange("(g p t) o -> p g (t o)", p=P, t=4),
            )

        x_q = {(g, pair): operand("x%d%d" % (g, pair), 4 * P) for g in range(2) for pair in range(2)}
        w_q = {(G, c): operand("w%d%d" % (G, c), PASS) for G in range(4) for c in range(2)}
        hf_q = [operand("hf%d" % q, 2 * PASS) for q in range(4)]
        hm_q = [operand("hm%d" % G, 2 * PASS) for G in range(4)]
        dz_q = operand("dz", 2 * R)
        la_q = operand("la", 4 * R)
        banks = {}
        staged = {}
        number = {}

        def bank(key, n, shape):
            banks[key] = psum.tile(shape, F32, name="bank%d" % n, bufs=1)
            number[key] = n
            return banks[key]

        def stage(key, ring, shape, dtype):
            staged[key] = work.tile(shape, dtype, name=ring, bufs=RINGS[ring], align_bytes=64)
            return staged[key]

        def x_turn(g, s, n):
            out = bank(("x", g, s), n, [P, 2, 2, P])
            xw = x_tile[g, s].bitcast(F32)
            for c in range(2):
                for u in range(2):
                    nc.tensor.transpose(out[:, c, u, :], xw[:, 256 * c + u : 256 * (c + 1) : 2], ident[:])

        def x_copy(g, s, engine, ring="xt"):
            if s % 2 == 0:
                stage(("x", g, s // 2), ring, [P, 2 * K], BF16)
            copy_on(
                engine,
                staged["x", g, s // 2][:, part(K, s % 2)].bitcast(F32).rearrange("p (c q u) -> p c q u", c=2, u=2),
                banks["x", g, s][:].rearrange("p c u q -> p c q u"),
            )

        def x_quant(g, pair, first=0, last=2):
            quantize(x_q[g, pair], slice(2 * P * first, 2 * P * last), staged["x", g, pair][:, K * first : K * last])

        def quarters(key):
            whole = stage(key, "mix", [P, 8 * PASS], BF16)
            return [whole[:, part(1024, m)] for m in range(4)]

        def half(key, u, place):
            staged.setdefault(key, [None, None])[u] = (
                stage((key, u), place, [P, 2 * PASS], BF16)[:] if place == "early" else staged[place]
            )

        def pool_copy(out, in_):
            nc.gpsimd.tensor_scalar(out=out, in0=in_, scalar1=1.0, scalar2=0.0, op0=ALU.mult, op1=ALU.add)

        def w_mix(G, c, u, engine):
            out = staged["w", G, c][u]
            if engine == "G":
                pool_copy(
                    out.rearrange("p (n e j) -> p n e j", e=2, j=4),
                    w_raw[G, c].rearrange("p j (n u e) -> p u n e j", u=2, e=2)[:, u],
                )
            else:
                copy_on(
                    engine,
                    out.rearrange("p (m i e j) -> p m j i e", i=2, e=2, j=4),
                    w_raw[G, c].rearrange("p j (m i u e) -> p u m j i e", i=2, u=2, e=2)[:, u],
                )

        def w_half(G, c, u, engine, ring):
            half(("w", G, c), u, ring)
            w_mix(G, c, u, engine)

        def w_quant(G, c, u):
            quantize(w_q[G, c], part(256, u), staged["w", G, c][u])

        h_all = [x_raw[:, : 4 * K]] + [w_both[G][:] for G in range(3)]
        h_sb = {(G, g): h_all[G][:, part(4 * PASS, g)].rearrange("p (u m) -> p u m", u=2) for G, g in BLOCKS}

        def up_pass(b, pair, u, c, n):
            G, g = b
            if c == 0:
                bank(("up", b, pair, u), n, [P, 2, 256])
            out = banks["up", b, pair, u]
            for i in range(2):
                multiply(
                    out[:, i, :], x_q[g, pair], part(P, 2 * i + c), w_q[G, c], part(256, u), c == 0 and i == 0, c == 1 and i == 1
                )

        def h_mul(b, pair, u):
            nc.vector.scalar_tensor_tensor(
                out=h_sb[b][:, u, part(PASS, pair)].rearrange("p (m e) -> p m e", e=2),
                in0=gate_sb[b[0], 2 * b[1] + pair].rearrange("p (m u e) -> p u m e", u=2, e=2)[:, u],
                scalar=0.0,
                in1=banks["up", b, pair, u][:].rearrange("p i (n e) -> p (i n) e", e=2),
                op0=ALU.max,
                op1=ALU.mult,
            )

        def h_turn(b, pair, n):
            out = bank(("h", b, pair), n, [P, 2, 2, P])
            hw = h_sb[b].bitcast(F32)
            for i in range(2):
                for u in range(2):
                    nc.tensor.transpose(out[:, i, u, :], hw[:, u, part(P, 2 * pair + i)], ident[:])

        def h_copy(b, pair, engine="S"):
            copy_on(
                engine,
                gate_sb[b[0], 2 * b[1] + pair].bitcast(F32).rearrange("p (i q u) -> p i q u", i=2, u=2),
                banks["h", b, pair][:].rearrange("p i u q -> p i q u"),
            )

        def hf_quant(q, first, last):
            quantize(hf_q[q], slice(256 * first, 256 * last), gate_row[q][:, 1024 * first : 1024 * last])

        def hm_mix(G, first, last, engine):
            out = staged["hm", G][:, 1024 * first : 1024 * last]
            in_ = h_all[G][:, 1024 * first : 1024 * last]
            if engine == "G":
                pool_copy(
                    out.rearrange("p (e n s) -> p e n s", e=2, s=4), in_.rearrange("p (s n e) -> p e n s", s=4, e=2)
                )
            else:
                for m in range(last - first):
                    copy_on(
                        engine,
                        out[:, part(1024, m)].rearrange("p (e n i s) -> p n s i e", e=2, i=2, s=4),
                        in_[:, part(1024, m)].rearrange("p (s n i e) -> p n s i e", s=4, i=2, e=2),
                    )

        def hm_piece(G, m, k):
            copy_on(
                "S",
                staged["hm", G][:, part(1024, m)].rearrange("p (e n i s) -> p n s i e", e=2, i=2, s=4)[:, part(32, k)],
                h_all[G][:, part(1024, m)].rearrange("p (s n i e) -> p n s i e", s=4, i=2, e=2)[:, part(32, k)],
            )

        def hm_quant(G, first=0, last=4):
            quantize(hm_q[G], slice(256 * first, 256 * last), staged["hm", G][:, 1024 * first : 1024 * last])

        def dz_mix():
            t = stage("dz", "xt", [P, 2 * R * 4], BF16)
            copy_on(
                "V",
                t[:].rearrange("p (g r i t) -> p g r t i", g=2, i=4, t=4),
                dz_raw[:].rearrange("p g t (r i) -> p g r t i", i=4),
            )

        def dz_quant():
            quantize(dz_q, slice(0, 2 * R), staged["dz"][:])

        def la_widen(G):
            if G == 0:
                staged["la"] = stage("lora", "mix", [P, 8 * PASS], BF16)[:, : 4 * PASS]
                staged["la_wide"] = staged["lora"][:, 4 * PASS :].rearrange("p (g t r) -> p g t r", g=4, t=4)
            for t in range(4):
                nc.scalar.activation(
                    out=staged["la_wide"][:, G, t, :],
                    in_=lbytes[:, G, part(R, t)].bitcast(FP8),
                    func=COPY,
                    scale=lscale[:, 4 * G + t : 4 * G + t + 1],
                )

        def la_mix():
            copy_on(
                "V",
                staged["la"].rearrange("p (g r i t) -> p g r t i", g=4, i=4, t=4),
                staged["la_wide"].rearrange("p g t (r i) -> p g r t i", i=4),
            )

        def la_quant():
            quantize(la_q, slice(0, 4 * R), staged["la"])

        yv = y.rearrange("(g q s) n -> g s q n", q=P, s=4)
        zv = z.rearrange("(g q s) r -> g q (s r)", q=P, s=4)
        dav = da.rearrange("(g n a) r -> g n (a r)", n=P, a=4)

        def y_mul(g, s, half, groups, n=None):
            if 0 in groups:
                bank(("y", g, s, half), n, [P, 512])
            out = banks["y", g, s, half]
            for G in groups:
                nc.tensor.matmul_mx(
                    out=out[:],
                    lhsT=hf_q[2 * g + s // 2][0][:, part(P, 2 * G + s % 2)].bitcast(FP8X4),
                    lhsT_scale=hf_q[2 * g + s // 2][1][:, part(P, 2 * G + s % 2)],
                    rhs=words[G][:, part(1024, half)].bitcast(FP4X4),
                    rhs_scale=down_sc[:, G, part(512, half)],
                    start=(G == 0),
                    stop=(G == 3),
                )

        def z_mul(g, first, last, n):
            out = bank(("z", g, first, last), n, [P, (last - first) * R])
            for s in range(first, last):
                for G in range(4):
                    multiply(out[:, part(R, s - first)], hf_q[2 * g + s // 2], part(P, 2 * G + s % 2), la_q, part(R, G), G == 0, G == 3)

        def da_mul(G, first, last, n):
            out = bank(("da", G, first, last), n, [P, (last - first) * R])
            for a in range(first, last):
                for g in range(2):
                    multiply(out[:, part(R, a - first)], hm_q[G], part(P, 4 * g + a), dz_q, part(R, g), g == 0, g == 1)

        def put(key, engine):
            t = stage(key, "out", list(banks[key].shape), F32)
            copy_on(engine, t[:], banks[key][:])
            free.append(number[key])
            if key[0] == "y":
                dst = yv[key[1], key[2], :, part(512, key[3])]
            else:
                dst = (zv if key[0] == "z" else dav)[key[1], :, R * key[2] : R * key[3]]
            nc.sync.dma_start(out=dst, in_=t[:])

        ctx.enter_context(tc.manual_schedule())
        free = list(range(8))

        def take():
            return free.pop(0)

        held = {}

        def x_in(g, s, engine, ring="xt"):
            n = take()
            x_turn(g, s, n)
            x_copy(g, s, engine, ring)
            free.append(n)

        def first(G, q, u):
            held[G, q, u] = take()
            up_pass((G, q // 2), q % 2, u, 0, held[G, q, u])

        def second(G, q, u):
            if (G, q, u) not in held:
                first(G, q, u)
            up_pass((G, q // 2), q % 2, u, 1, held[G, q, u])

        def gated(G, q, u):
            h_mul((G, q // 2), q % 2, u)
            free.append(held[G, q, u])

        def turn_pair(b, pair):
            held[b, pair] = take()
            h_turn(b, pair, held[b, pair])

        def copy_pair(b, pair, engine="S"):
            h_copy(b, pair, engine)
            free.append(held[b, pair])

        def cells(g):
            return [(2 * g + k % 2, k // 2) for k in range(4)]


        def ahead(G, g, u):
            for pair in range(2):
                first(G, 2 * g + pair, u)

        def both(G, g, u):
            for pair in range(2):
                second(G, 2 * g + pair, u)

        def gate_pair(G, g, u):
            for pair in range(2):
                gated(G, 2 * g + pair, u)

        def turn_block(b):
            for pair in range(2):
                turn_pair(b, pair)
                copy_pair(b, pair)

        CP = "S"
        WIDEN = (6, 7)
        SMIX = (8, 10)
        S3 = "V"
        SMALL = {7: [("da", 0, 0, 4)], 10: [("da", 1, 0, 4)], 13: [("da", 2, 0, 4)], 15: [("da", 3, 0, 4)]}
        LAST = ((("z", 0, 0, 2), "V"), (("z", 0, 2, 4), "S"), (("z", 1, 0, 2), "V"), (("z", 1, 2, 3), "S"), (("z", 1, 3, 4), "V"))
        load_x(0, 0)
        load_x(0, 1)
        load_w(0, 0)
        load_w(0, 1)
        load_x(1, 0)
        load_x(1, 1)
        load_gate((0, 0))
        load_w(1, 0)
        load_w(1, 1)
        load_gate((0, 1), (0,))
        load_w(2, 0)
        load_gate((0, 1), (1,))
        load_gate((1, 0))
        load_w(2, 1)
        load_gate((1, 1))
        load_w(3, 0)
        load_gate((2, 0))
        load_w(3, 1)
        load_gate((2, 1))
        load_gate((3, 0))
        load_gate((3, 1))
        load_down()
        load_lora()
        load_dz()

        for s in range(4):
            x_in(0, s, "V" if s == 1 else "S")
            if s == 1:
                x_quant(0, 0)
        first_group = quarters("w0")
        staged["Y"] = quarters(("hm", 1))[3]
        for name in "XZ":
            staged[name] = kept(name, [P, 2 * PASS], BF16)[:]
        for c in range(2):
            staged["w", 0, c] = first_group[2 * c : 2 * c + 2]
        w_mix(0, 0, 0, "V")
        w_mix(0, 0, 1, "S")
        x_quant(0, 1)
        w_quant(0, 0, 0)
        w_mix(0, 1, 0, "V")
        w_mix(0, 1, 1, "S")
        w_quant(0, 0, 1)
        for u in range(2):
            w_quant(0, 1, u)
        for s in range(4):
            x_in(1, s, "V" if s == 1 else "S", "xt" if s < 2 else "early")
            if s == 0:
                ahead(0, 0, 0)
            if s == 1:
                x_quant(1, 0)
        for i in range(2):
            x_quant(1, 1, i, i + 1)
        w_half(1, 0, 1, "G", "early")
        w_half(1, 0, 0, "S", "Z")
        w_half(1, 1, 0, "S", "X")

        def step(i):
            if i < 2:
                return [(0, 2 * i + k // 2, k % 2) for k in range(4)]
            return [(i // 2, k, i % 2) for k in range(4)]

        def step_up(i, ahead):
            for item in step(i)[:ahead]:
                first(*item)
            for item in step(i):
                second(*item)

        def step_h(i):
            for item in step(i):
                gated(*item)

        tiles = [("y", g, s, half_n) for g in range(2) for s in range(4) for half_n in range(2)]
        step_up(0, 0)
        step_up(1, 0)
        step_h(0)
        w_quant(1, 0, 0)
        w_quant(1, 0, 1)
        w_quant(1, 1, 0)
        quarters(("hm", 0))
        w_half(2, 0, 0, "G", "X")
        turn_block((0, 0))
        w_half(1, 1, 1, "S", "Y")
        hm_piece(0, 0, 0)
        step_h(1)
        w_quant(1, 1, 1)
        for G in range(1, 4):
            if G < 3:
                w_half(G + 1, 0, 1, "G", "Y")
            else:
                hm_mix(1, 3, 4, "G")
                hm_mix(0, 3, 4, "G")
            ahead(G, 0, 0)
            both(G, 0, 0)
            both(G, 1, 0)
            if G == 1:
                ahead(G, 0, 1)
            for pair in range(2):
                turn_pair((G - 1, 1), pair)
            if G < 3:
                gated(G, 0, 0)
            copy_pair((G - 1, 1), 0)
            if G == 3:
                copy_pair((G - 1, 1), 1)
                gated(G, 0, 0)
            if G < 3:
                w_half(G + 1, 1, 0, "S", "Z")
            else:
                hm_mix(0, 1, 2, "S")
                hm_mix(1, 0, 1, "S")
                for k in range(2):
                    la_widen(k)
            gated(G, 1, 0)
            if not (G == 1):
                ahead(G, 0, 1)
            both(G, 0, 1)
            both(G, 1, 1)
            if G == 3:
                break
            gate_pair(G, 0, 1)
            if not False:
                copy_pair((G - 1, 1), 1)
            if G == 1:
                w_quant(2, 0, 0)
            w_quant(G + 1, 1, 0)
            w_quant(G + 1, 0, 1)
            w_half(G + 1, 1, 1, "G", "Y")
            for pair in range(2):
                turn_pair((G, 0), pair)
            gate_pair(G, 1, 0)
            for pair in range(2):
                copy_pair((G, 0), pair)
            if G < 2:
                w_half(G + 2, 0, 0, "S", "X")
                hm_piece(0, 0, 1)
            else:
                hm_mix(0, 2, 3, "S")
            gate_pair(G, 1, 1)
            if G == 2:
                hf_quant(0, 2, 3)
            else:
                w_quant(G + 2, 0, 0)
            w_quant(G + 1, 1, 1)
            if G == 2:
                hf_quant(0, 0, 2)
        for i in range(2):
            y_mul(*tiles[i][1:], range(3), take())
        gate_pair(3, 0, 1)
        for i in range(2, 4):
            y_mul(*tiles[i][1:], range(2), take())
        gate_pair(3, 1, 0)
        gate_pair(3, 1, 1)
        turn_block((3, 0))
        turn_block((3, 1))
        hf_quant(1, 0, 2)
        hf_quant(1, 2, 3)
        for i in range(2, 4):
            y_mul(*tiles[i][1:], range(2, 3))
        y_mul(*tiles[4][1:], range(3), take())
        hm_quant(0, 0, 2)
        hf_quant(0, 3, 4)
        hm_quant(0, 2, 4)
        hf_quant(1, 3, 4)
        dz_mix()

        def small(key, engine):
            (z_mul if key[0] == "z" else da_mul)(*key[1:], take())
            put(key, engine)

        for i in range(16):
            if i < 5:
                y_mul(*tiles[i][1:], [3])
            else:
                y_mul(*tiles[i][1:], range(4), take())
            put(tiles[i], "S")
            if i == 0:
                hm_mix(1, 1, 3, "V")
                dz_quant()
                staged["hm", 2] = gate_row[0][:]
                hm_mix(2, 0, 1, "V")
                hf_quant(2, 0, 4)
                hm_quant(1)
                hf_quant(3, 0, 4)
                hm_mix(2, 1, 2, "V")
                hm_mix(2, 3, 4, "V")
                staged["hm", 3] = gate_row[1][:]
            if i in WIDEN:
                la_widen(2 + WIDEN.index(i))
            if i == SMIX[0]:
                hm_mix(2, 2, 3, "S")
                hm_mix(3, 0, 2, "V")
                hm_quant(2)
            if i == SMIX[1]:
                hm_mix(3, 3, 4, "S")
                hm_mix(3, 2, 3, S3)
                la_mix()
                hm_quant(3)
                la_quant()
            for key in SMALL.get(i, ()):
                small(key, "S")
        for key, engine in LAST:
            small(key, engine)
